import numpy as np
import ml_dtypes


def mxq(x, axis, fmt="e4m3"):
    dtype, down = {"e4m3": (ml_dtypes.float8_e4m3fn, 7), "e5m2": (ml_dtypes.float8_e5m2, 14)}[fmt]
    v = np.moveaxis(np.asarray(x, np.float32).astype(ml_dtypes.bfloat16).astype(np.float64), axis, -1)
    blocks = v.reshape(v.shape[:-1] + (-1, 32))
    amax = np.abs(blocks).max(-1, keepdims=True)
    byte = np.maximum(np.where(amax > 0, np.frexp(amax)[1] - 1 + 127, 0) - down, 1)
    scale = np.exp2(byte - 127.0)
    codes = (blocks / scale).astype(np.float32).astype(dtype).astype(np.float64)
    return np.moveaxis((codes * scale).reshape(v.shape), -1, axis)


WIDE = False


def mx_kscale(k):
    if not WIDE:
        return np.ones(k)
    levels = np.array([10, -10, 5, -5, 0])
    if k % 512:
        return np.exp2(np.random.permutation(np.resize(levels, k // 32))).repeat(32)
    a = np.empty((k // 512, 16))
    for p in range(k // 512):
        a[p, :8] = np.random.permutation(np.resize(levels, 8))
        for g in range(8):
            far = levels[np.abs(levels - a[p, g]) >= 10]
            a[p, g + 8] = far[np.random.randint(len(far))]
    return np.exp2(a.ravel()).repeat(32)


def f64(x):
    return np.asarray(x).astype(np.float64)


def striped(idx):
    return np.tile(idx.reshape(-1, 16).T, (8, 1)).astype(np.uint16)


def unstriped(offs):
    return offs[:16].T.reshape(-1).astype(np.int64)


E2M1 = np.array([0.0, 0.5, 1.0, 1.5, 2.0, 3.0, 4.0, 6.0, -0.0, -0.5, -1.0, -1.5, -2.0, -3.0, -4.0, -6.0])


def pack_weight(w, fmt):
    k, n = w.shape
    w = f64(np.asarray(w, np.float32).astype(ml_dtypes.bfloat16)).reshape(k // 32, 32, n)
    amax = np.abs(w).max(1)
    if fmt == "e4m3":
        byte = np.frexp(amax)[1] - 1 + 127 - 7
    else:
        mant, ex = np.frexp(amax / 6.0)
        byte = np.where(mant > 0.5, ex, ex - 1) + 127
    byte = np.clip(np.where(amax > 0, byte, 1), 1, 254)
    scaled = (w * np.exp2(127.0 - byte)[:, None, :]).reshape(k, n).astype(np.float32)
    by_word = np.ascontiguousarray(scaled.reshape(k // 512, 128, 4, n).transpose(0, 1, 3, 2))
    if fmt == "e4m3":
        words = by_word.astype(ml_dtypes.float8_e4m3fn).view(np.uint8)
    else:
        c = by_word.astype(ml_dtypes.float4_e2m1fn).view(np.uint8) & 0xF
        words = (c[..., 0::2] | (c[..., 1::2] << 4)).reshape(k // 512, 128, 2 * n)
    return np.ascontiguousarray(words), np.ascontiguousarray(byte.astype(np.uint8).reshape(k // 512, 16, n))


def unpack_weight(words, scales, fmt):
    g, _, n = scales.shape
    words = np.ascontiguousarray(words).reshape(g, 128, n, -1)
    if fmt == "e4m3":
        vals = words.view(ml_dtypes.float8_e4m3fn).astype(np.float64)
    else:
        nib = np.empty((g, 128, n, 4), np.uint8)
        nib[..., 0::2] = words & 0xF
        nib[..., 1::2] = words >> 4
        vals = E2M1[nib]
    vals = vals * np.repeat(np.exp2(scales.astype(np.float64) - 127.0), 8, axis=1)[..., None]
    return vals.transpose(0, 1, 3, 2).reshape(g * 512, n)


def gelu(v):
    return 0.5 * v * (1.0 + np.tanh(np.sqrt(2.0 / np.pi) * (v + 0.044715 * v**3)))


def bf(x):
    return np.asarray(x, np.float32).astype(ml_dtypes.bfloat16)


def planes(Y):
    n, m = Y.shape
    b = f64(bf(Y)).reshape(n // 32, 32, m)
    amax = np.abs(b).max(1)
    byte = np.clip(np.where(amax > 0, np.frexp(amax)[1] - 1 + 127 - 7, 1), 1, 254)
    codes = (b * np.exp2(127.0 - byte)[:, None, :]).reshape(n, m).astype(np.float32).astype(ml_dtypes.float8_e4m3fn).view(np.uint8)
    words = codes.reshape(n // 512, 128, 4, m).transpose(0, 1, 3, 2)
    return np.ascontiguousarray(words), np.ascontiguousarray(byte.astype(np.uint8).reshape(n // 512, 16, m))


K, N, T, S = 1024, 512, 2048, 1024

def setup_inputs():
    n = np.random.standard_normal
    s = mx_kscale(K)[:, None]
    u = mx_kscale(K)[:, None]
    tab_words, tab_scales = pack_weight(n((K, T)) * s, "e4m3")
    flow = n((K, K)) / np.sqrt(K)
    flow_words, flow_scales = pack_weight(flow / s, "e2m1")
    size = np.exp(0.8 * n(N))
    return {
        "tab_words": tab_words, "tab_scales": tab_scales,
        "offs": striped(np.random.permutation(T)[:S]),
        "flow_words": flow_words, "flow_scales": flow_scales,
        "flowT": (flow.T / s).astype(np.float32),
        "gain": (np.random.uniform(0.5, 1.5, K) * u[:, 0]).astype(np.float32),
        "wm": (n((K, N)) / np.sqrt(K) / u * size).astype(np.float32),
        "gT": (n((N, T)) * size[:, None]).astype(np.float32),
        "docks": np.random.uniform(1.0, 3.0, S).astype(np.float32),
    }

def reference(tab_words, tab_scales, offs, flow_words, flow_scales, flowT,
              gain, wm, gT, docks):
    v = unpack_weight(tab_words, tab_scales, "e4m3")[:, unstriped(offs)]
    inflow = unpack_weight(flow_words, flow_scales, "e2m1").T @ v
    outflow = mxq(f64(flowT), 0, "e4m3").T @ v
    h = np.tanh(inflow - outflow) * f64(gain)[:, None]
    move = mxq(f64(wm), 0, "e4m3").T @ mxq(h, 0, "e4m3")
    g = f64(gT)[:, unstriped(offs)]
    new = np.minimum(g + move, f64(docks)[None, :])
    y = f64(gT).copy()
    y[:, unstriped(offs)] = new
    words, scales = planes(y)
    return y, words, scales

@@ -1,0 +1,331 @@
+from contextlib import ExitStack
+
+import concourse.mybir as mybir
+from concourse.masks import make_identity
+
+K, N, T, S = 1024, 512, 2048, 1024
+FLOPS = 2 * K * K * S * 2 + 2 * K * N * S
+
+F32 = mybir.dt.float32
+BF16 = mybir.dt.bfloat16
+I32 = mybir.dt.int32
+U32 = mybir.dt.uint32
+U16 = mybir.dt.uint16
+U8 = mybir.dt.uint8
+FP8X4 = mybir.dt.float8_e4m3fn_x4
+FP4X4 = mybir.dt.float4_e2m1fn_x4
+ACT = mybir.ActivationFunctionType
+ALU = mybir.AluOpType
+
+P = 128
+PACK = 4
+GROUP = P * PACK
+PASSES = K // GROUP
+QUADS = 4
+BANK = 512
+CHUNK = 256
+CHUNKS = S // CHUNK
+PIECE = 512
+RUN = 4
+HALF = PACK // 2
+LOAD_ORDER = ("flow", "gain", "ts", "f00", "t0", "fs", "docks", "t1", "f10", "f01", "f11", "w0", "w1", "g0", "g1", "g2", "g3")
+HELD = {("f11", 1): ("f10", 1), ("w0", 1): ("f11", 0), ("w1", 1): ("h", 0, 0)}
+DEFER_FROM = 2
+ON_VECTOR = {("f01", 1), ("f11", 1), ("w0", 1), ("w1", 1)}
+
+
+def tile_list_bike_route_rebalance_kernel(
+    tc, tab_words, tab_scales, offs, flow_words, flow_scales, flowT, gain, wm, gT, docks, out_0, out_1, out_2
+):
+    nc = tc.nc
+    with ExitStack() as ctx:
+        keep = ctx.enter_context(tc.tile_pool(name="keep", bufs=1))
+        ring = ctx.enter_context(tc.tile_pool(name="ring", bufs=1))
+        psum = ctx.enter_context(tc.psum_pool(name="psum", bufs=1))
+
+        offsets = keep.tile([P, S // 16], U16, name="offsets")
+        nc.sync.dma_start(offsets[:], offs)
+
+        tab_planes = keep.tile([P, PASSES, T], U8, name="tab_planes", align_bytes=64)
+        nc.vector.memset(tab_planes[:].bitcast(I32), 0)
+        flow_plane_raw = keep.tile([P, PASSES, K], U8, name="flow_plane_raw", align_bytes=64)
+        nc.gpsimd.memset(flow_plane_raw[:].bitcast(I32), 0)
+        warm = keep.tile([P, 8], F32, name="warm")
+        nc.gpsimd.memset(warm[:], 0.0)
+        nc.scalar.activation(warm[:, 0:1], warm[:, 1:2], ACT.Tanh)
+        docks_rows = keep.tile([P, S // P], F32, name="docks_rows")
+
+        table = [keep.tile([P, T], I32, name=f"table{a}", align_bytes=64) for a in range(PASSES)]
+        flow_raw = keep.tile([P, PASSES, K // 2], I32, name="flow_raw", align_bytes=64)
+        pages = [ring.tile([P, T], F32, name=f"page{t}", tag="raw", bufs=6, align_bytes=64) for t in range(PACK)]
+        gain_sb = keep.tile([P, PASSES, PACK], F32, name="gain_sb")
+
+        def load_planes(tile, scales):
+            for q in range(QUADS):
+                nc.sync.dma_start(
+                    tile[32 * q : 32 * q + 4, :, :].bitcast(I32),
+                    scales[:, 4 * q : 4 * q + 4, :].rearrange("a r c -> r a c").bitcast(I32),
+                )
+
+        def load_weight(w, a, b):
+            raw = ring.tile([P, PACK, GROUP], F32, name="raw", tag="raw", bufs=6, align_bytes=64)
+            rows = w[a * GROUP : (a + 1) * GROUP, b * GROUP : (b + 1) * GROUP]
+            nc.sync.dma_start(raw[:], rows.rearrange("(p i) c -> p i c", i=PACK))
+            return raw
+
+        raws = {}
+        gT_rows = gT.rearrange("(p t) m -> p t m", t=PACK)
+        for item in LOAD_ORDER:
+            if item == "flow":
+                nc.sync.dma_start(flow_raw[:], flow_words.rearrange("a p c -> p a c").bitcast(I32))
+            elif item == "ts":
+                load_planes(tab_planes, tab_scales)
+            elif item == "fs":
+                load_planes(flow_plane_raw, flow_scales)
+            elif item == "gain":
+                nc.sync.dma_start(gain_sb[:], gain.rearrange("(b p t) -> p b t", p=P, t=PACK))
+            elif item == "docks":
+                nc.sync.dma_start(docks_rows[:], docks.rearrange("(p c) -> p c", p=P))
+            elif item[0] == "t":
+                a = int(item[1])
+                nc.sync.dma_start(table[a][:], tab_words[a].rearrange("p t i -> p (t i)").bitcast(I32))
+            elif item[0] == "f":
+                raws[item] = load_weight(flowT, int(item[1]), int(item[2]))
+            elif item[0] == "w":
+                raws[item] = load_weight(wm, int(item[1]), 0)
+            else:
+                t = int(item[1])
+                nc.sync.dma_start(pages[t][:], gT_rows[:, t, :])
+
+        ident = keep.tile([P, P], F32, name="ident", align_bytes=64)
+        make_identity(nc, ident[:])
+        limit = keep.tile([P, S], F32, name="limit", align_bytes=64)
+        per_row = S // P
+        for half in range(per_row // PACK):
+            spread = psum.tile([P, PACK, P], F32, name="spread", tag="move_bank", bufs=2)
+            for c in range(PACK):
+                col = half * PACK + c
+                nc.tensor.transpose(spread[:, c, :], docks_rows[:, col : col + 1].to_broadcast([P, P]), ident[:])
+            nc.scalar.copy(
+                limit[:].rearrange("p (r c) -> p r c", c=per_row)[:, :, half * PACK : (half + 1) * PACK],
+                spread[:].rearrange("p c r -> p r c"),
+            )
+
+        quantised = {}
+        woven_of = {}
+        spent_bytes = {}
+
+        def quantise_weight(name, sign):
+            src = raws[name][:].rearrange("p i (m t) -> p m i t", t=PACK)
+            for half in range(PACK // HALF):
+                if (name, half) in HELD:
+                    dealt = spent_bytes[HELD[name, half]]
+                else:
+                    dealt = ring.tile([P, HALF, P, PACK], BF16, name="dealt", tag="dealt", bufs=6, align_bytes=64)[:]
+                spent_bytes[name, half] = dealt
+                dst = dealt.rearrange("p t m i -> p m i t")
+                part = src[:, :, :, half * HALF : (half + 1) * HALF]
+                if (name, half) in ON_VECTOR:
+                    nc.vector.tensor_scalar(dst, part, sign, None, ALU.mult)
+                else:
+                    nc.scalar.activation(dst, part, ACT.Copy, scale=sign)
+                codes = keep.tile([P, HALF * P], U32, name=f"{name}_codes{half}", align_bytes=64)
+                plane = keep.tile([P, HALF * P], U8, name=f"{name}_plane{half}", align_bytes=64)
+                nc.vector.quantize_mx(
+                    out=codes[:].bitcast(FP8X4), scales=plane[:], in_=dealt.rearrange("p t m i -> p (t m i)")
+                )
+                for t in range(HALF):
+                    cols = slice(t * P, (t + 1) * P)
+                    quantised[name, half * HALF + t] = (codes[:, cols].bitcast(FP8X4), plane[:, cols])
+
+        v_words = [keep.tile([P, S], U32, name=f"v_words{a}", align_bytes=64) for a in range(PASSES)]
+        v_planes = [keep.tile([P, S], U8, name=f"v_plane{a}", align_bytes=64) for a in range(PASSES)]
+        flow_codes = keep.tile([P, PASSES * PASSES, PACK, 2 * P], U8, name="flow_codes", align_bytes=64)
+        flow_plane = keep.tile([P, PASSES * PASSES, PACK, P], U8, name="flow_plane", align_bytes=64)
+        nc.vector.tensor_copy(
+            flow_codes[:].bitcast(U16),
+            flow_raw[:].bitcast(U16).rearrange("p a (b m t) -> p (a b) t m", m=P, t=PACK),
+        )
+        nc.vector.tensor_copy(v_planes[0][:], tab_planes[:, 0, :].indirect(offsets[:]))
+        nc.vector.tensor_copy(v_planes[1][:], tab_planes[:, 1, :].indirect(offsets[:]))
+        nc.vector.tensor_copy(v_words[0][:], table[0][:].bitcast(U32).indirect(offsets[:]))
+        nc.vector.tensor_copy(v_words[1][:], table[1][:].bitcast(U32).indirect(offsets[:]))
+        nc.vector.tensor_copy(
+            flow_plane[:], flow_plane_raw[:].rearrange("p a (b m t) -> p (a b) t m", m=P, t=PACK)
+        )
+        quantise_weight("f00", -1.0)
+        quantise_weight("f10", -1.0)
+        quantise_weight("f01", -1.0)
+        quantise_weight("f11", -1.0)
+
+        def imbalance_bank(b, ranges):
+            bank = psum.tile([P, BANK], F32, name="score_bank", tag=f"score_bank{b}", bufs=2)
+            steps = [(kind, a, r) for a in range(PASSES) for kind in range(2) for r in range(len(ranges))]
+            for n, (kind, a, r) in enumerate(steps):
+                t, j0 = ranges[r]
+                if kind == 0:
+                    lhs = flow_codes[:, a * PASSES + b, t, :].bitcast(FP4X4)
+                    lhs_plane = flow_plane[:, a * PASSES + b, t, :]
+                else:
+                    lhs, lhs_plane = quantised[f"f{a}{b}", t]
+                nc.tensor.matmul_mx(
+                    out=bank[:, r * P : (r + 1) * P],
+                    lhsT=lhs,
+                    lhsT_scale=lhs_plane,
+                    rhs=v_words[a][:, j0 : j0 + P].bitcast(FP8X4),
+                    rhs_scale=v_planes[a][:, j0 : j0 + P],
+                    start=(n == 0),
+                    stop=(n == len(steps) - 1),
+                )
+            return bank
+
+        h_q = {}
+
+        def quantise_h(woven, c, b):
+            codes = keep.tile([P, CHUNK], U32, name=f"h_codes{c}{b}", align_bytes=64)
+            plane = keep.tile([P, CHUNK], U8, name=f"h_plane{c}{b}", align_bytes=64)
+            nc.vector.quantize_mx(
+                out=codes[:].bitcast(FP8X4), scales=plane[:], in_=woven[:].rearrange("p j t -> p (j t)")
+            )
+            h_q[c, b] = (codes, plane)
+            woven_of[c, b] = woven
+            spent_bytes["h", c, b] = woven[:].rearrange("p (t m) i -> p t m i", t=HALF)
+
+        def h_by_vector(c, b):
+            j0 = c * CHUNK
+            woven = ring.tile([P, CHUNK, PACK], BF16, name="woven", tag="woven", bufs=4, align_bytes=64)
+            for s in range(CHUNK // P):
+                bank = imbalance_bank(b, [(t, j0 + s * P) for t in range(PACK)])
+                bounded = ring.tile([P, P, PACK], F32, name="bounded", tag="bounded", bufs=4, align_bytes=64)
+                nc.scalar.activation(bounded[:], bank[:].rearrange("p (t j) -> p j t", t=PACK), ACT.Tanh)
+                nc.vector.tensor_tensor(
+                    woven[:, s * P : (s + 1) * P, :],
+                    bounded[:],
+                    gain_sb[:, b : b + 1, :].to_broadcast([P, P, PACK]),
+                    ALU.mult,
+                )
+            quantise_h(woven, c, b)
+
+        def h_by_scalar(c, b):
+            j0 = c * CHUNK
+            rounded = ring.tile([P, PACK, CHUNK], BF16, name="rounded", tag="rounded", bufs=2, align_bytes=64)
+            per_bank = BANK // CHUNK
+            for t0 in range(0, PACK, per_bank):
+                ts = range(t0, t0 + per_bank)
+                bank = imbalance_bank(b, [(t, j) for t in ts for j in range(j0, j0 + CHUNK, P)])
+                bounded = ring.tile([P, BANK], F32, name="bounded", tag="bounded", bufs=4, align_bytes=64)
+                nc.scalar.activation(bounded[:], bank[:], ACT.Tanh)
+                for t in ts:
+                    nc.scalar.activation(
+                        rounded[:, t, :],
+                        bounded[:, (t - t0) * CHUNK : (t - t0 + 1) * CHUNK],
+                        ACT.Copy,
+                        scale=gain_sb[:, b, t : t + 1],
+                    )
+            woven = ring.tile([P, CHUNK, PACK], BF16, name="woven", tag="woven", bufs=4, align_bytes=64)
+            nc.scalar.copy(
+                woven[:].rearrange("p (c i) t -> p c t i", i=RUN),
+                rounded[:].rearrange("p t (c i) -> p c t i", i=RUN),
+            )
+            quantise_h(woven, c, b)
+
+        def move_chunk(c):
+            per_bank = BANK // CHUNK
+            for t0 in range(0, PACK, per_bank):
+                bank = psum.tile([P, per_bank, CHUNK], F32, name="move_bank", tag="move_bank", bufs=2)
+                for t in range(t0, t0 + per_bank):
+                    for b in reversed(range(PASSES)):
+                        nc.tensor.matmul_mx(
+                            out=bank[:, t - t0, :],
+                            lhsT=quantised[f"w{b}", t][0],
+                            lhsT_scale=quantised[f"w{b}", t][1],
+                            rhs=h_q[c, b][0][:].bitcast(FP8X4),
+                            rhs_scale=h_q[c, b][1][:],
+                            start=(b == PASSES - 1),
+                            stop=(b == 0),
+                        )
+                nc.scalar.copy(move[:, t0 : t0 + per_bank, c * CHUNK : (c + 1) * CHUNK], bank[:])
+
+        move = keep.tile([P, PACK, S], F32, name="move", align_bytes=64)
+
+        def update_pages(steps, spent):
+            new = {}
+
+            def add_state(n):
+                t, j0, j1 = steps[n]
+                summed = ring.tile([P, j1 - j0], F32, name="summed", tag="summed", bufs=4, align_bytes=64)
+                nc.vector.tensor_tensor(
+                    summed[:], pages[t][:].indirect(offsets[:, j0 // 16 : j1 // 16]), move[:, t, j0:j1], ALU.add
+                )
+                new[n] = summed[:]
+
+            add_state(0)
+            for n, (t, j0, j1) in enumerate(steps):
+                if n + 1 < len(steps):
+                    add_state(n + 1)
+                clipped = new[n]
+                k = n - (len(steps) - 2)
+                if spent is not None and k >= 0:
+                    clipped = spent[:].rearrange("p j t -> p (j t)").bitcast(F32)[:, k * CHUNK : (k + 1) * CHUNK]
+                nc.vector.tensor_tensor(clipped, new[n], limit[:, j0:j1], ALU.min)
+                nc.vector.tensor_copy(pages[t][:].indirect(offsets[:, j0 // 16 : j1 // 16]), clipped)
+
+        h_by_vector(0, 0)
+        h_by_vector(0, 1)
+        quantise_weight("w0", 1.0)
+        quantise_weight("w1", 1.0)
+        for c in range(CHUNKS):
+            move_chunk(c)
+            if c + 1 < CHUNKS:
+                for b in range(PASSES):
+                    h_by_scalar(c + 1, b)
+            steps = [(t, c * CHUNK, (c + 1) * CHUNK) for t in range(PACK if c < DEFER_FROM else PACK - 1)]
+            if c + 1 == CHUNKS:
+                steps.append((PACK - 1, DEFER_FROM * CHUNK, S))
+            update_pages(steps, woven_of.get((c + 1, PASSES - 1)))
+
+        out_rows = out_0.rearrange("(p t) m -> p t m", t=PACK)
+        pieces = T // PIECE
+        y_rounded = [
+            ring.tile([P, PACK, PIECE], BF16, name="y_rounded", tag="y_rounded", bufs=4, align_bytes=64) for q in range(pieces)
+        ]
+        y_woven = [
+            ring.tile([P, PIECE, PACK], BF16, name="y_woven", tag="y_woven", bufs=4, align_bytes=64) for q in range(pieces)
+        ]
+        by_vector = range(pieces // 2)
+
+        def weave(copy, q, t0, t1):
+            copy(
+                y_woven[q][:].rearrange("p (c i) t -> p c t i", i=RUN)[:, :, t0:t1, :],
+                y_rounded[q][:].rearrange("p t (c i) -> p c t i", i=RUN)[:, :, t0:t1, :],
+            )
+
+        for t in range(PACK):
+            nc.sync.dma_start(out_rows[:, t, :], pages[t][:])
+            if t + 1 < PACK:
+                for q in reversed(range(pieces)):
+                    nc.scalar.copy(y_rounded[q][:, t, :], pages[t][:, q * PIECE : (q + 1) * PIECE])
+            if t == PACK - 2:
+                for q in range(pieces // 2, pieces):
+                    weave(nc.scalar.copy, q, 0, PACK - 1)
+        for q in range(pieces):
+            cols = slice(q * PIECE, (q + 1) * PIECE)
+            if q in by_vector:
+                nc.vector.tensor_copy(y_rounded[q][:, PACK - 1, :], pages[PACK - 1][:, cols])
+            else:
+                nc.scalar.copy(y_woven[q][:, :, PACK - 1], pages[PACK - 1][:, cols])
+        for q in by_vector:
+            weave(nc.vector.tensor_copy, q, 0, PACK)
+        y_plane = keep.tile([P, T], U8, name="y_plane", align_bytes=64)
+        words_out = out_1[0].rearrange("p m t -> p (m t)").bitcast(I32)
+        for q in (0, 2, 1, 3):
+            cols = slice(q * PIECE, (q + 1) * PIECE)
+            y_codes = keep.tile([P, PIECE], I32, name=f"y_codes{q}", align_bytes=64)
+            nc.vector.quantize_mx(
+                out=y_codes[:].bitcast(FP8X4), scales=y_plane[:, cols], in_=y_woven[q][:].rearrange("p m t -> p (m t)")
+            )
+            nc.sync.dma_start(words_out[:, cols], y_codes[:])
+        for q in range(QUADS):
+            nc.sync.dma_start(
+                out_2[0, 4 * q : 4 * q + 4, :].bitcast(I32), y_plane[32 * q : 32 * q + 4, :].bitcast(I32)
+            )

@@ -28,10 +28,11 @@ CHUNKS = S // CHUNK
 PIECE = 512
 RUN = 4
 HALF = PACK // 2
-LOAD_ORDER = ("flow", "gain", "ts", "f00", "t0", "fs", "docks", "t1", "f10", "f01", "f11", "w0", "w1", "g0", "g1", "g2", "g3")
-HELD = {("f11", 1): ("f10", 1), ("w0", 1): ("f11", 0), ("w1", 1): ("h", 0, 0)}
+LOAD_ORDER = ("flow", "ts", "t0", "f00", "fs", "gain", "f01", "t1", "f10", "f11", "w0", "w1", "g0", "g1", "g2", "g3")
+HELD = {("f11", 0): ("f10", 1), ("w0", 0): ("f11", 1), ("w1", 0): ("h", 0, 0)}
 DEFER_FROM = 2
-ON_VECTOR = {("f01", 1), ("f11", 1), ("w0", 1), ("w1", 1)}
+JOINT = {1: 2, 2: 4}
+ON_VECTOR = {("f11", 0), ("w0", 0), ("w1", 0)}
 
 
 def tile_list_bike_route_rebalance_kernel(
@@ -47,7 +48,8 @@ def tile_list_bike_route_rebalance_kernel(
         nc.sync.dma_start(offsets[:], offs)
 
         tab_planes = keep.tile([P, PASSES, T], U8, name="tab_planes", align_bytes=64)
-        nc.vector.memset(tab_planes[:].bitcast(I32), 0)
+        nc.vector.memset(tab_planes[:, 0, :].bitcast(I32), 0)
+        nc.gpsimd.memset(tab_planes[:, 1, :].bitcast(I32), 0)
         flow_plane_raw = keep.tile([P, PASSES, K], U8, name="flow_plane_raw", align_bytes=64)
         nc.gpsimd.memset(flow_plane_raw[:].bitcast(I32), 0)
         warm = keep.tile([P, 8], F32, name="warm")
@@ -55,9 +57,10 @@ def tile_list_bike_route_rebalance_kernel(
         nc.scalar.activation(warm[:, 0:1], warm[:, 1:2], ACT.Tanh)
         docks_rows = keep.tile([P, S // P], F32, name="docks_rows")
 
+        nc.scalar.dma_start(docks_rows[:], docks.rearrange("(p c) -> p c", p=P))
         table = [keep.tile([P, T], I32, name=f"table{a}", align_bytes=64) for a in range(PASSES)]
         flow_raw = keep.tile([P, PASSES, K // 2], I32, name="flow_raw", align_bytes=64)
-        pages = [ring.tile([P, T], F32, name=f"page{t}", tag="raw", bufs=6, align_bytes=64) for t in range(PACK)]
+        pages = [ring.tile([P, T], F32, name=f"page{t}", tag="raw", bufs=5, align_bytes=64) for t in range(PACK)]
         gain_sb = keep.tile([P, PASSES, PACK], F32, name="gain_sb")
 
         def load_planes(tile, scales):
@@ -68,7 +71,7 @@ def tile_list_bike_route_rebalance_kernel(
                 )
 
         def load_weight(w, a, b):
-            raw = ring.tile([P, PACK, GROUP], F32, name="raw", tag="raw", bufs=6, align_bytes=64)
+            raw = ring.tile([P, PACK, GROUP], F32, name="raw", tag="raw", bufs=5, align_bytes=64)
             rows = w[a * GROUP : (a + 1) * GROUP, b * GROUP : (b + 1) * GROUP]
             nc.sync.dma_start(raw[:], rows.rearrange("(p i) c -> p i c", i=PACK))
             return raw
@@ -97,27 +100,28 @@ def tile_list_bike_route_rebalance_kernel(
                 t = int(item[1])
                 nc.sync.dma_start(pages[t][:], gT_rows[:, t, :])
 
+        banks = [[psum.tile([P, BANK], F32, name=f"bank{x}{y}") for y in range(2)] for x in range(3)]
         ident = keep.tile([P, P], F32, name="ident", align_bytes=64)
         make_identity(nc, ident[:])
         limit = keep.tile([P, S], F32, name="limit", align_bytes=64)
         per_row = S // P
         for half in range(per_row // PACK):
-            spread = psum.tile([P, PACK, P], F32, name="spread", tag="move_bank", bufs=2)
+            spread = banks[2][half][:].rearrange("p (c r) -> p c r", c=PACK)
             for c in range(PACK):
                 col = half * PACK + c
                 nc.tensor.transpose(spread[:, c, :], docks_rows[:, col : col + 1].to_broadcast([P, P]), ident[:])
             nc.scalar.copy(
                 limit[:].rearrange("p (r c) -> p r c", c=per_row)[:, :, half * PACK : (half + 1) * PACK],
-                spread[:].rearrange("p c r -> p r c"),
+                spread.rearrange("p c r -> p r c"),
             )
 
         quantised = {}
         woven_of = {}
         spent_bytes = {}
 
-        def quantise_weight(name, sign):
+        def quantise_weight(name, sign, halves=(0, 1)):
             src = raws[name][:].rearrange("p i (m t) -> p m i t", t=PACK)
-            for half in range(PACK // HALF):
+            for half in halves:
                 if (name, half) in HELD:
                     dealt = spent_bytes[HELD[name, half]]
                 else:
@@ -147,37 +151,41 @@ def tile_list_bike_route_rebalance_kernel(
             flow_raw[:].bitcast(U16).rearrange("p a (b m t) -> p (a b) t m", m=P, t=PACK),
         )
         nc.vector.tensor_copy(v_planes[0][:], tab_planes[:, 0, :].indirect(offsets[:]))
-        nc.vector.tensor_copy(v_planes[1][:], tab_planes[:, 1, :].indirect(offsets[:]))
         nc.vector.tensor_copy(v_words[0][:], table[0][:].bitcast(U32).indirect(offsets[:]))
-        nc.vector.tensor_copy(v_words[1][:], table[1][:].bitcast(U32).indirect(offsets[:]))
+        nc.vector.tensor_copy(v_planes[1][:], tab_planes[:, 1, :].indirect(offsets[:]))
         nc.vector.tensor_copy(
             flow_plane[:], flow_plane_raw[:].rearrange("p a (b m t) -> p (a b) t m", m=P, t=PACK)
         )
         quantise_weight("f00", -1.0)
-        quantise_weight("f10", -1.0)
         quantise_weight("f01", -1.0)
+        nc.vector.tensor_copy(v_words[1][:], table[1][:].bitcast(U32).indirect(offsets[:]))
+        quantise_weight("f10", -1.0)
         quantise_weight("f11", -1.0)
 
-        def imbalance_bank(b, ranges):
-            bank = psum.tile([P, BANK], F32, name="score_bank", tag=f"score_bank{b}", bufs=2)
-            steps = [(kind, a, r) for a in range(PASSES) for kind in range(2) for r in range(len(ranges))]
-            for n, (kind, a, r) in enumerate(steps):
-                t, j0 = ranges[r]
-                if kind == 0:
+        def imbalance(bank, b, ranges):
+            steps = []
+            for a in range(PASSES):
+                for packed in (True, False):
+                    col = 0
+                    for t, j0, width in ranges:
+                        step = P if packed and width < BANK else width
+                        steps.extend((a, packed, t, j0 + d, col + d, step) for d in range(0, width, step))
+                        col += width
+            for n, (a, packed, t, j0, col, width) in enumerate(steps):
+                if packed:
                     lhs = flow_codes[:, a * PASSES + b, t, :].bitcast(FP4X4)
                     lhs_plane = flow_plane[:, a * PASSES + b, t, :]
                 else:
                     lhs, lhs_plane = quantised[f"f{a}{b}", t]
                 nc.tensor.matmul_mx(
-                    out=bank[:, r * P : (r + 1) * P],
+                    out=bank[:, col : col + width],
                     lhsT=lhs,
                     lhsT_scale=lhs_plane,
-                    rhs=v_words[a][:, j0 : j0 + P].bitcast(FP8X4),
-                    rhs_scale=v_planes[a][:, j0 : j0 + P],
+                    rhs=v_words[a][:, j0 : j0 + width].bitcast(FP8X4),
+                    rhs_scale=v_planes[a][:, j0 : j0 + width],
                     start=(n == 0),
                     stop=(n == len(steps) - 1),
                 )
-            return bank
 
         h_q = {}
 
@@ -195,8 +203,9 @@ def tile_list_bike_route_rebalance_kernel(
             j0 = c * CHUNK
             woven = ring.tile([P, CHUNK, PACK], BF16, name="woven", tag="woven", bufs=4, align_bytes=64)
             for s in range(CHUNK // P):
-                bank = imbalance_bank(b, [(t, j0 + s * P) for t in range(PACK)])
-                bounded = ring.tile([P, P, PACK], F32, name="bounded", tag="bounded", bufs=4, align_bytes=64)
+                bank = banks[b][s]
+                imbalance(bank, b, [(t, j0 + s * P, P) for t in range(PACK)])
+                bounded = ring.tile([P, P, PACK], F32, name="bounded", tag="bounded", bufs=10, align_bytes=64)
                 nc.scalar.activation(bounded[:], bank[:].rearrange("p (t j) -> p j t", t=PACK), ACT.Tanh)
                 nc.vector.tensor_tensor(
                     woven[:, s * P : (s + 1) * P, :],
@@ -206,33 +215,47 @@ def tile_list_bike_route_rebalance_kernel(
                 )
             quantise_h(woven, c, b)
 
-        def h_by_scalar(c, b):
-            j0 = c * CHUNK
-            rounded = ring.tile([P, PACK, CHUNK], BF16, name="rounded", tag="rounded", bufs=2, align_bytes=64)
-            per_bank = BANK // CHUNK
+        bounded_of = {}
+
+        def bound_scores(c0, c1, b):
+            width = (c1 - c0) * CHUNK
+            per_bank = BANK // width
             for t0 in range(0, PACK, per_bank):
-                ts = range(t0, t0 + per_bank)
-                bank = imbalance_bank(b, [(t, j) for t in ts for j in range(j0, j0 + CHUNK, P)])
-                bounded = ring.tile([P, BANK], F32, name="bounded", tag="bounded", bufs=4, align_bytes=64)
+                bank = banks[b if c0 == 1 else 1 - b][t0 // per_bank % 2]
+                imbalance(bank, b, [(t, c0 * CHUNK, width) for t in range(t0, t0 + per_bank)])
+                bounded = ring.tile([P, BANK], F32, name="bounded", tag="bounded", bufs=10, align_bytes=64)
                 nc.scalar.activation(bounded[:], bank[:], ACT.Tanh)
-                for t in ts:
-                    nc.scalar.activation(
-                        rounded[:, t, :],
-                        bounded[:, (t - t0) * CHUNK : (t - t0 + 1) * CHUNK],
-                        ACT.Copy,
-                        scale=gain_sb[:, b, t : t + 1],
-                    )
-            woven = ring.tile([P, CHUNK, PACK], BF16, name="woven", tag="woven", bufs=4, align_bytes=64)
-            nc.scalar.copy(
-                woven[:].rearrange("p (c i) t -> p c t i", i=RUN),
-                rounded[:].rearrange("p t (c i) -> p c t i", i=RUN),
-            )
-            quantise_h(woven, c, b)
+                for t in range(t0, t0 + per_bank):
+                    for c in range(c0, c1):
+                        col = (t - t0) * width + (c - c0) * CHUNK
+                        bounded_of[c, b, t] = bounded[:, col : col + CHUNK]
+                    weigh(c0, b, t)
+
+        rounded_of = {}
+
+        def weigh(c, b, t):
+            if t == 0:
+                rounded_of[c, b] = ring.tile([P, PACK, CHUNK], BF16, name="rounded", tag="rounded", bufs=2, align_bytes=64)
+            nc.scalar.activation(rounded_of[c, b][:, t, :], bounded_of[c, b, t], ACT.Copy, scale=gain_sb[:, b, t : t + 1])
+            if t == PACK - 1:
+                woven = ring.tile([P, CHUNK, PACK], BF16, name="woven", tag="woven", bufs=4, align_bytes=64)
+                nc.scalar.copy(
+                    woven[:].rearrange("p (c i) t -> p c t i", i=RUN),
+                    rounded_of[c, b][:].rearrange("p t (c i) -> p c t i", i=RUN),
+                )
+                quantise_h(woven, c, b)
+
+        def h_by_scalar(c, b):
+            if c in JOINT:
+                bound_scores(c, JOINT[c], b)
+            else:
+                for t in range(PACK):
+                    weigh(c, b, t)
 
         def move_chunk(c):
             per_bank = BANK // CHUNK
             for t0 in range(0, PACK, per_bank):
-                bank = psum.tile([P, per_bank, CHUNK], F32, name="move_bank", tag="move_bank", bufs=2)
+                bank = banks[(1, 0, 2, 2)[c]][t0 // per_bank][:].rearrange("p (t j) -> p t j", t=per_bank)
                 for t in range(t0, t0 + per_bank):
                     for b in reversed(range(PASSES)):
                         nc.tensor.matmul_mx(
@@ -244,16 +267,16 @@ def tile_list_bike_route_rebalance_kernel(
                             start=(b == PASSES - 1),
                             stop=(b == 0),
                         )
-                nc.scalar.copy(move[:, t0 : t0 + per_bank, c * CHUNK : (c + 1) * CHUNK], bank[:])
+                nc.scalar.copy(move[:, t0 : t0 + per_bank, c * CHUNK : (c + 1) * CHUNK], bank)
 
         move = keep.tile([P, PACK, S], F32, name="move", align_bytes=64)
 
-        def update_pages(steps, spent):
+        def update_pages(steps, spent, held):
             new = {}
 
             def add_state(n):
                 t, j0, j1 = steps[n]
-                summed = ring.tile([P, j1 - j0], F32, name="summed", tag="summed", bufs=4, align_bytes=64)
+                summed = ring.tile([P, j1 - j0], F32, name="summed", tag="summed", bufs=2, align_bytes=64)
                 nc.vector.tensor_tensor(
                     summed[:], pages[t][:].indirect(offsets[:, j0 // 16 : j1 // 16]), move[:, t, j0:j1], ALU.add
                 )
@@ -264,25 +287,30 @@ def tile_list_bike_route_rebalance_kernel(
                 if n + 1 < len(steps):
                     add_state(n + 1)
                 clipped = new[n]
-                k = n - (len(steps) - 2)
+                k = n - (len(steps) - held)
                 if spent is not None and k >= 0:
                     clipped = spent[:].rearrange("p j t -> p (j t)").bitcast(F32)[:, k * CHUNK : (k + 1) * CHUNK]
                 nc.vector.tensor_tensor(clipped, new[n], limit[:, j0:j1], ALU.min)
                 nc.vector.tensor_copy(pages[t][:].indirect(offsets[:, j0 // 16 : j1 // 16]), clipped)
 
         h_by_vector(0, 0)
+        quantise_weight("w0", 1.0, (0,))
         h_by_vector(0, 1)
-        quantise_weight("w0", 1.0)
-        quantise_weight("w1", 1.0)
+        quantise_weight("w1", 1.0, (0,))
+        quantise_weight("w0", 1.0, (1,))
+        quantise_weight("w1", 1.0, (1,))
         for c in range(CHUNKS):
             move_chunk(c)
             if c + 1 < CHUNKS:
                 for b in range(PASSES):
                     h_by_scalar(c + 1, b)
-            steps = [(t, c * CHUNK, (c + 1) * CHUNK) for t in range(PACK if c < DEFER_FROM else PACK - 1)]
+            if c < CHUNKS - 2:
+                steps = [(t, c * CHUNK, (c + 1) * CHUNK) for t in range(PACK)]
+            else:
+                steps = [(t, c * CHUNK, (c + 1) * CHUNK) for t in range(HALF)]
             if c + 1 == CHUNKS:
-                steps.append((PACK - 1, DEFER_FROM * CHUNK, S))
-            update_pages(steps, woven_of.get((c + 1, PASSES - 1)))
+                steps.extend((t, (CHUNKS - 2) * CHUNK, S) for t in range(HALF, PACK))
+            update_pages(steps, woven_of.get((c + 1, PASSES - 1)), HALF)
 
         out_rows = out_0.rearrange("(p t) m -> p t m", t=PACK)
         pieces = T // PIECE
@@ -300,32 +328,30 @@ def tile_list_bike_route_rebalance_kernel(
                 y_rounded[q][:].rearrange("p t (c i) -> p c t i", i=RUN)[:, :, t0:t1, :],
             )
 
+        by_scalar = range(pieces // 2, pieces)
+
+        def page_cols(t, q):
+            return pages[t][:, q * PIECE : (q + 1) * PIECE]
+
         for t in range(PACK):
             nc.sync.dma_start(out_rows[:, t, :], pages[t][:])
-            if t + 1 < PACK:
-                for q in reversed(range(pieces)):
-                    nc.scalar.copy(y_rounded[q][:, t, :], pages[t][:, q * PIECE : (q + 1) * PIECE])
-            if t == PACK - 2:
-                for q in range(pieces // 2, pieces):
-                    weave(nc.scalar.copy, q, 0, PACK - 1)
-        for q in range(pieces):
-            cols = slice(q * PIECE, (q + 1) * PIECE)
-            if q in by_vector:
-                nc.vector.tensor_copy(y_rounded[q][:, PACK - 1, :], pages[PACK - 1][:, cols])
-            else:
-                nc.scalar.copy(y_woven[q][:, :, PACK - 1], pages[PACK - 1][:, cols])
+            for q in range(pieces):
+                copy = nc.vector.tensor_copy if t == PACK - 1 and q in by_vector else nc.scalar.copy
+                copy(y_rounded[q][:, t, :], page_cols(t, q))
+                if q in by_scalar and t % HALF == HALF - 1:
+                    weave(nc.scalar.copy, q, t + 1 - HALF, t + 1)
         for q in by_vector:
             weave(nc.vector.tensor_copy, q, 0, PACK)
         y_plane = keep.tile([P, T], U8, name="y_plane", align_bytes=64)
         words_out = out_1[0].rearrange("p m t -> p (m t)").bitcast(I32)
-        for q in (0, 2, 1, 3):
+        for q in range(pieces):
             cols = slice(q * PIECE, (q + 1) * PIECE)
             y_codes = keep.tile([P, PIECE], I32, name=f"y_codes{q}", align_bytes=64)
             nc.vector.quantize_mx(
                 out=y_codes[:].bitcast(FP8X4), scales=y_plane[:, cols], in_=y_woven[q][:].rearrange("p m t -> p (m t)")
             )
             nc.sync.dma_start(words_out[:, cols], y_codes[:])
-        for q in range(QUADS):
+        for quad in range(QUADS):
             nc.sync.dma_start(
-                out_2[0, 4 * q : 4 * q + 4, :].bitcast(I32), y_plane[32 * q : 32 * q + 4, :].bitcast(I32)
+                out_2[0, 4 * quad : 4 * quad + 4, :].bitcast(I32), y_plane[32 * quad : 32 * quad + 4, :].bitcast(I32)
             )

@@ -28,7 +28,7 @@ CHUNKS = S // CHUNK
 PIECE = 512
 RUN = 4
 HALF = PACK // 2
-LOAD_ORDER = ("flow", "ts", "t0", "f00", "fs", "gain", "f01", "t1", "f10", "f11", "w0", "w1", "g0", "g1", "g2", "g3")
+LOAD_ORDER = ("flow", "offs", "ts", "t0", "f00", "fs", "gain", "f01", "t1", "f10", "f11", "w0", "w1", "g0", "g1", "g2", "g3")
 HELD = {("f11", 0): ("f10", 1), ("w0", 0): ("f11", 1), ("w1", 0): ("h", 0, 0)}
 DEFER_FROM = 2
 JOINT = {1: 2, 2: 4}
@@ -45,7 +45,6 @@ def tile_list_bike_route_rebalance_kernel(
         psum = ctx.enter_context(tc.psum_pool(name="psum", bufs=1))
 
         offsets = keep.tile([P, S // 16], U16, name="offsets")
-        nc.sync.dma_start(offsets[:], offs)
 
         tab_planes = keep.tile([P, PASSES, T], U8, name="tab_planes", align_bytes=64)
         nc.vector.memset(tab_planes[:, 0, :].bitcast(I32), 0)
@@ -64,11 +63,9 @@ def tile_list_bike_route_rebalance_kernel(
         gain_sb = keep.tile([P, PASSES, PACK], F32, name="gain_sb")
 
         def load_planes(tile, scales):
-            for q in range(QUADS):
-                nc.sync.dma_start(
-                    tile[32 * q : 32 * q + 4, :, :].bitcast(I32),
-                    scales[:, 4 * q : 4 * q + 4, :].rearrange("a r c -> r a c").bitcast(I32),
-                )
+            rows = scales.rearrange("a (q r) c -> r q a c", q=QUADS)
+            for r in range(4):
+                nc.sync.dma_start(tile[r:P:32, :, :].bitcast(I32), rows[r].bitcast(I32))
 
         def load_weight(w, a, b):
             raw = ring.tile([P, PACK, GROUP], F32, name="raw", tag="raw", bufs=5, align_bytes=64)
@@ -79,7 +76,9 @@ def tile_list_bike_route_rebalance_kernel(
         raws = {}
         gT_rows = gT.rearrange("(p t) m -> p t m", t=PACK)
         for item in LOAD_ORDER:
-            if item == "flow":
+            if item == "offs":
+                nc.sync.dma_start(offsets[:], offs)
+            elif item == "flow":
                 nc.sync.dma_start(flow_raw[:], flow_words.rearrange("a p c -> p a c").bitcast(I32))
             elif item == "ts":
                 load_planes(tab_planes, tab_scales)
@@ -100,7 +99,7 @@ def tile_list_bike_route_rebalance_kernel(
                 t = int(item[1])
                 nc.sync.dma_start(pages[t][:], gT_rows[:, t, :])
 
-        banks = [[psum.tile([P, BANK], F32, name=f"bank{x}{y}") for y in range(2)] for x in range(3)]
+        banks = [[psum.tile([P, BANK], F32, name=f"bank{x}{y}") for y in range(2)] for x in range(4)]
         ident = keep.tile([P, P], F32, name="ident", align_bytes=64)
         make_identity(nc, ident[:])
         limit = keep.tile([P, S], F32, name="limit", align_bytes=64)
@@ -253,21 +252,24 @@ def tile_list_bike_route_rebalance_kernel(
                     weigh(c, b, t)
 
         def move_chunk(c):
-            per_bank = BANK // CHUNK
-            for t0 in range(0, PACK, per_bank):
-                bank = banks[(1, 0, 2, 2)[c]][t0 // per_bank][:].rearrange("p (t j) -> p t j", t=per_bank)
-                for t in range(t0, t0 + per_bank):
-                    for b in reversed(range(PASSES)):
+            groups = ((0,), (1,), (2, 3)) if c == 0 else ((0, 1), (2, 3))
+            free = (banks[2] + banks[3], banks[0], banks[2], banks[2])[c]
+            order = range(PASSES) if c == 0 else range(PASSES - 1, -1, -1)
+            for ts, tile in zip(groups, free):
+                bank = tile[:, 0 : len(ts) * CHUNK].rearrange("p (t j) -> p t j", j=CHUNK)
+                for t in ts:
+                    for b in order:
                         nc.tensor.matmul_mx(
-                            out=bank[:, t - t0, :],
+                            out=bank[:, t - ts[0], :],
                             lhsT=quantised[f"w{b}", t][0],
                             lhsT_scale=quantised[f"w{b}", t][1],
                             rhs=h_q[c, b][0][:].bitcast(FP8X4),
                             rhs_scale=h_q[c, b][1][:],
-                            start=(b == PASSES - 1),
-                            stop=(b == 0),
+                            start=(b == order[0]),
+                            stop=(b == order[-1]),
                         )
-                nc.scalar.copy(move[:, t0 : t0 + per_bank, c * CHUNK : (c + 1) * CHUNK], bank)
+                copy = nc.vector.tensor_copy if c == 0 and ts[0] < HALF else nc.scalar.copy
+                copy(move[:, ts[0] : ts[-1] + 1, c * CHUNK : (c + 1) * CHUNK], bank)
 
         move = keep.tile([P, PACK, S], F32, name="move", align_bytes=64)
 
@@ -295,9 +297,9 @@ def tile_list_bike_route_rebalance_kernel(
 
         h_by_vector(0, 0)
         quantise_weight("w0", 1.0, (0,))
+        quantise_weight("w0", 1.0, (1,))
         h_by_vector(0, 1)
         quantise_weight("w1", 1.0, (0,))
-        quantise_weight("w0", 1.0, (1,))
         quantise_weight("w1", 1.0, (1,))
         for c in range(CHUNKS):
             move_chunk(c)
@@ -351,7 +353,6 @@ def tile_list_bike_route_rebalance_kernel(
                 out=y_codes[:].bitcast(FP8X4), scales=y_plane[:, cols], in_=y_woven[q][:].rearrange("p m t -> p (m t)")
             )
             nc.sync.dma_start(words_out[:, cols], y_codes[:])
-        for quad in range(QUADS):
-            nc.sync.dma_start(
-                out_2[0, 4 * quad : 4 * quad + 4, :].bitcast(I32), y_plane[32 * quad : 32 * quad + 4, :].bitcast(I32)
-            )
+        scale_rows = out_2[0].rearrange("(q r) m -> r q m", q=QUADS)
+        for r in range(4):
+            nc.sync.dma_start(scale_rows[r].bitcast(I32), y_plane[r:P:32, :].bitcast(I32))

@@ -50,10 +50,12 @@ def tile_list_bike_route_rebalance_kernel(
         nc.vector.memset(tab_planes[:, 0, :].bitcast(I32), 0)
         nc.gpsimd.memset(tab_planes[:, 1, :].bitcast(I32), 0)
         flow_plane_raw = keep.tile([P, PASSES, K], U8, name="flow_plane_raw", align_bytes=64)
-        nc.gpsimd.memset(flow_plane_raw[:].bitcast(I32), 0)
+        nc.vector.memset(flow_plane_raw[:].bitcast(I32), 0)
         warm = keep.tile([P, 8], F32, name="warm")
-        nc.gpsimd.memset(warm[:], 0.0)
+        nc.vector.memset(warm[:], 0.0)
         nc.scalar.activation(warm[:, 0:1], warm[:, 1:2], ACT.Tanh)
+        ident = keep.tile([P, P], F32, name="ident", align_bytes=64)
+        make_identity(nc, ident[:])
         docks_rows = keep.tile([P, S // P], F32, name="docks_rows")
 
         nc.scalar.dma_start(docks_rows[:], docks.rearrange("(p c) -> p c", p=P))
@@ -62,10 +64,10 @@ def tile_list_bike_route_rebalance_kernel(
         pages = [ring.tile([P, T], F32, name=f"page{t}", tag="raw", bufs=5, align_bytes=64) for t in range(PACK)]
         gain_sb = keep.tile([P, PASSES, PACK], F32, name="gain_sb")
 
-        def load_planes(tile, scales):
+        def load_planes(queue, tile, scales):
             rows = scales.rearrange("a (q r) c -> r q a c", q=QUADS)
             for r in range(4):
-                nc.sync.dma_start(tile[r:P:32, :, :].bitcast(I32), rows[r].bitcast(I32))
+                queue.dma_start(tile[r:P:32, :, :].bitcast(I32), rows[r].bitcast(I32))
 
         def load_weight(w, a, b):
             raw = ring.tile([P, PACK, GROUP], F32, name="raw", tag="raw", bufs=5, align_bytes=64)
@@ -81,11 +83,11 @@ def tile_list_bike_route_rebalance_kernel(
             elif item == "flow":
                 nc.sync.dma_start(flow_raw[:], flow_words.rearrange("a p c -> p a c").bitcast(I32))
             elif item == "ts":
-                load_planes(tab_planes, tab_scales)
+                load_planes(nc.sync, tab_planes, tab_scales)
             elif item == "fs":
-                load_planes(flow_plane_raw, flow_scales)
+                load_planes(nc.gpsimd, flow_plane_raw, flow_scales)
             elif item == "gain":
-                nc.sync.dma_start(gain_sb[:], gain.rearrange("(b p t) -> p b t", p=P, t=PACK))
+                nc.gpsimd.dma_start(gain_sb[:], gain.rearrange("(b p t) -> p b t", p=P, t=PACK))
             elif item == "docks":
                 nc.sync.dma_start(docks_rows[:], docks.rearrange("(p c) -> p c", p=P))
             elif item[0] == "t":
@@ -100,8 +102,6 @@ def tile_list_bike_route_rebalance_kernel(
                 nc.sync.dma_start(pages[t][:], gT_rows[:, t, :])
 
         banks = [[psum.tile([P, BANK], F32, name=f"bank{x}{y}") for y in range(2)] for x in range(4)]
-        ident = keep.tile([P, P], F32, name="ident", align_bytes=64)
-        make_identity(nc, ident[:])
         limit = keep.tile([P, S], F32, name="limit", align_bytes=64)
         per_row = S // P
         for half in range(per_row // PACK):
@@ -324,6 +324,15 @@ def tile_list_bike_route_rebalance_kernel(
         ]
         by_vector = range(pieces // 2)
 
+        def weave_pair(cols, t0):
+            q, m0 = divmod(cols.start, PIECE)
+            ms = slice(m0, m0 + cols.stop - cols.start)
+            nc.scalar.copy(
+                y_woven[q][:, ms, t0 : t0 + HALF], y_rounded[q][:, t0 : t0 + HALF, ms].rearrange("p t m -> p m t")
+            )
+
+        parts = [slice(0, 512), slice(512, 1024), slice(1024, 1536), slice(1536, 1792), slice(1792, 2048)]
+
         def weave(copy, q, t0, t1):
             copy(
                 y_woven[q][:].rearrange("p (c i) t -> p c t i", i=RUN)[:, :, t0:t1, :],
@@ -341,18 +350,25 @@ def tile_list_bike_route_rebalance_kernel(
                 copy = nc.vector.tensor_copy if t == PACK - 1 and q in by_vector else nc.scalar.copy
                 copy(y_rounded[q][:, t, :], page_cols(t, q))
                 if q in by_scalar and t % HALF == HALF - 1:
-                    weave(nc.scalar.copy, q, t + 1 - HALF, t + 1)
+                    for cols in parts:
+                        if cols.start // PIECE == q:
+                            weave_pair(cols, t + 1 - HALF)
         for q in by_vector:
             weave(nc.vector.tensor_copy, q, 0, PACK)
         y_plane = keep.tile([P, T], U8, name="y_plane", align_bytes=64)
         words_out = out_1[0].rearrange("p m t -> p (m t)").bitcast(I32)
-        for q in range(pieces):
-            cols = slice(q * PIECE, (q + 1) * PIECE)
-            y_codes = keep.tile([P, PIECE], I32, name=f"y_codes{q}", align_bytes=64)
+        y_codes = keep.tile([P, T], I32, name="y_codes", align_bytes=64)
+        stored = 0
+        for cols in parts:
+            q, m0 = divmod(cols.start, PIECE)
             nc.vector.quantize_mx(
-                out=y_codes[:].bitcast(FP8X4), scales=y_plane[:, cols], in_=y_woven[q][:].rearrange("p m t -> p (m t)")
+                out=y_codes[:, cols].bitcast(FP8X4),
+                scales=y_plane[:, cols],
+                in_=y_woven[q][:, m0 : m0 + cols.stop - cols.start, :].rearrange("p m t -> p (m t)"),
             )
-            nc.sync.dma_start(words_out[:, cols], y_codes[:])
+            if cols.stop > stored:
+                nc.sync.dma_start(words_out[:, stored : cols.stop], y_codes[:, stored : cols.stop])
+                stored = cols.stop
         scale_rows = out_2[0].rearrange("(q r) m -> r q m", q=QUADS)
         for r in range(4):
             nc.sync.dma_start(scale_rows[r].bitcast(I32), y_plane[r:P:32, :].bitcast(I32))

@@ -19,20 +19,20 @@ ALU = mybir.AluOpType
 
 P = 128
 PACK = 4
+HALF = PACK // 2
 GROUP = P * PACK
 PASSES = K // GROUP
 QUADS = 4
 BANK = 512
 CHUNK = 256
 CHUNKS = S // CHUNK
-PIECE = 512
+STRIPE = 16
 RUN = 4
-HALF = PACK // 2
-LOAD_ORDER = ("flow", "offs", "ts", "t0", "f00", "fs", "gain", "f01", "t1", "f10", "f11", "w0", "w1", "g0", "g1", "g2", "g3")
-HELD = {("f11", 0): ("f10", 1), ("w0", 0): ("f11", 1), ("w1", 0): ("h", 0, 0)}
-DEFER_FROM = 2
-JOINT = {1: 2, 2: 4}
-ON_VECTOR = {("f11", 0), ("w0", 0), ("w1", 0)}
+PIECES = (256, 256, 512, 512, 256, 256)
+SCALAR_PIECES = 2
+DEFER = 2
+SLOT = {1: 1, 4: 2, 7: 3}
+ORDER = (((0, True), (0, False), (1, True), (1, False)), ((0, True), (1, True), (0, False), (1, False)))
 
 
 def tile_list_bike_route_rebalance_kernel(
@@ -43,69 +43,75 @@ def tile_list_bike_route_rebalance_kernel(
         keep = ctx.enter_context(tc.tile_pool(name="keep", bufs=1))
         ring = ctx.enter_context(tc.tile_pool(name="ring", bufs=1))
         psum = ctx.enter_context(tc.psum_pool(name="psum", bufs=1))
+        stage = ctx.enter_context(tc.tile_pool(name="stage", bufs=1))
 
-        offsets = keep.tile([P, S // 16], U16, name="offsets")
+        def held(shape, dtype, name):
+            return keep.tile(shape, dtype, name=name, align_bytes=64)
 
-        tab_planes = keep.tile([P, PASSES, T], U8, name="tab_planes", align_bytes=64)
-        nc.vector.memset(tab_planes[:, 0, :].bitcast(I32), 0)
-        nc.gpsimd.memset(tab_planes[:, 1, :].bitcast(I32), 0)
-        flow_plane_raw = keep.tile([P, PASSES, K], U8, name="flow_plane_raw", align_bytes=64)
+        offsets = keep.tile([P, S // STRIPE], U16, name="offsets")
+        tab_planes = held([P, T], U8, "tab_planes")
+        v_plane_low = held([P, S], U8, "v_plane_low")
+        flow_plane_raw = held([P, PASSES, K], U8, "flow_plane_raw")
+        nc.vector.memset(tab_planes[:].bitcast(I32), 0)
         nc.vector.memset(flow_plane_raw[:].bitcast(I32), 0)
-        warm = keep.tile([P, 8], F32, name="warm")
-        nc.vector.memset(warm[:], 0.0)
-        nc.scalar.activation(warm[:, 0:1], warm[:, 1:2], ACT.Tanh)
-        ident = keep.tile([P, P], F32, name="ident", align_bytes=64)
+        nc.vector.memset(v_plane_low[:].bitcast(I32), 0)
+        ident = held([P, P], F32, "ident")
         make_identity(nc, ident[:])
-        docks_rows = keep.tile([P, S // P], F32, name="docks_rows")
-
-        nc.scalar.dma_start(docks_rows[:], docks.rearrange("(p c) -> p c", p=P))
-        table = [keep.tile([P, T], I32, name=f"table{a}", align_bytes=64) for a in range(PASSES)]
-        flow_raw = keep.tile([P, PASSES, K // 2], I32, name="flow_raw", align_bytes=64)
-        pages = [ring.tile([P, T], F32, name=f"page{t}", tag="raw", bufs=5, align_bytes=64) for t in range(PACK)]
-        gain_sb = keep.tile([P, PASSES, PACK], F32, name="gain_sb")
+        docks_rows = held([P, S // P], F32, "docks_rows")
+        gain_sb = held([P, PASSES, PACK], F32, "gain_sb")
+        table = [held([P, T], I32, f"table{a}") for a in range(PASSES)]
+        flow_raw = held([P, PASSES, K // 2], I32, "flow_raw")
+        pages = [held([P, T], F32, f"page{t}") for t in range(PACK)]
+        raws = {}
 
         def load_planes(queue, tile, scales):
             rows = scales.rearrange("a (q r) c -> r q a c", q=QUADS)
             for r in range(4):
                 queue.dma_start(tile[r:P:32, :, :].bitcast(I32), rows[r].bitcast(I32))
 
-        def load_weight(w, a, b):
-            raw = ring.tile([P, PACK, GROUP], F32, name="raw", tag="raw", bufs=5, align_bytes=64)
+        def load_weight(name, w, a, b):
+            raw = stage.tile([P, PACK, GROUP], F32, name=f"raw_{name}", tag=f"raw_{name}", align_bytes=64)
             rows = w[a * GROUP : (a + 1) * GROUP, b * GROUP : (b + 1) * GROUP]
             nc.sync.dma_start(raw[:], rows.rearrange("(p i) c -> p i c", i=PACK))
-            return raw
+            raws[name] = raw
 
-        raws = {}
+        def load_table(a):
+            nc.sync.dma_start(table[a][:], tab_words[a].rearrange("p t i -> p (t i)").bitcast(I32))
+
+        v_plane = held([P, S], U8, "v_plane")
+        nc.scalar.dma_start(docks_rows[:], docks.rearrange("(p c) -> p c", p=P))
+        nc.sync.dma_start(flow_raw[:], flow_words.rearrange("a p c -> p a c").bitcast(I32))
+        nc.sync.dma_start(offsets[:], offs)
+        for q in range(QUADS):
+            nc.sync.dma_start(
+                tab_planes[32 * q : 32 * q + 4 * PASSES, :].bitcast(I32),
+                tab_scales[:, 4 * q : 4 * q + 4, :].bitcast(I32),
+            )
+        load_table(0)
+        load_planes(nc.sync, flow_plane_raw, flow_scales)
+        load_weight("f00", flowT, 0, 0)
+        load_weight("f10", flowT, 1, 0)
+        nc.sync.dma_start(gain_sb[:], gain.rearrange("(b p t) -> p b t", p=P, t=PACK))
+        nc.vector.tensor_copy(v_plane[:], tab_planes[:].indirect(offsets[:]))
+        for q in range(QUADS):
+            nc.sync.dma_start(
+                v_plane_low[32 * q : 32 * q + 4, :].bitcast(I32), v_plane[32 * q + 4 : 32 * q + 8, :].bitcast(I32)
+            )
+        load_table(1)
+        load_weight("f01", flowT, 0, 1)
+        load_weight("f11", flowT, 1, 1)
+        load_weight("w0", wm, 0, 0)
+        load_weight("w1", wm, 1, 0)
         gT_rows = gT.rearrange("(p t) m -> p t m", t=PACK)
-        for item in LOAD_ORDER:
-            if item == "offs":
-                nc.sync.dma_start(offsets[:], offs)
-            elif item == "flow":
-                nc.sync.dma_start(flow_raw[:], flow_words.rearrange("a p c -> p a c").bitcast(I32))
-            elif item == "ts":
-                load_planes(nc.sync, tab_planes, tab_scales)
-            elif item == "fs":
-                load_planes(nc.gpsimd, flow_plane_raw, flow_scales)
-            elif item == "gain":
-                nc.gpsimd.dma_start(gain_sb[:], gain.rearrange("(b p t) -> p b t", p=P, t=PACK))
-            elif item == "docks":
-                nc.sync.dma_start(docks_rows[:], docks.rearrange("(p c) -> p c", p=P))
-            elif item[0] == "t":
-                a = int(item[1])
-                nc.sync.dma_start(table[a][:], tab_words[a].rearrange("p t i -> p (t i)").bitcast(I32))
-            elif item[0] == "f":
-                raws[item] = load_weight(flowT, int(item[1]), int(item[2]))
-            elif item[0] == "w":
-                raws[item] = load_weight(wm, int(item[1]), 0)
-            else:
-                t = int(item[1])
-                nc.sync.dma_start(pages[t][:], gT_rows[:, t, :])
+        for t in range(PACK):
+            nc.sync.dma_start(pages[t][:], gT_rows[:, t, :])
 
-        banks = [[psum.tile([P, BANK], F32, name=f"bank{x}{y}") for y in range(2)] for x in range(4)]
-        limit = keep.tile([P, S], F32, name="limit", align_bytes=64)
+        banks = [psum.tile([P, BANK], F32, name=f"bank{x}") for x in range(8)]
+
+        limit = held([P, S], F32, "limit")
         per_row = S // P
         for half in range(per_row // PACK):
-            spread = banks[2][half][:].rearrange("p (c r) -> p c r", c=PACK)
+            spread = banks[6 + half][:].rearrange("p (c r) -> p c r", c=PACK)
             for c in range(PACK):
                 col = half * PACK + c
                 nc.tensor.transpose(spread[:, c, :], docks_rows[:, col : col + 1].to_broadcast([P, P]), ident[:])
@@ -115,260 +121,282 @@ def tile_list_bike_route_rebalance_kernel(
             )
 
         quantised = {}
-        woven_of = {}
-        spent_bytes = {}
+        dealt_of = {}
 
-        def quantise_weight(name, sign, halves=(0, 1)):
-            src = raws[name][:].rearrange("p i (m t) -> p m i t", t=PACK)
-            for half in halves:
-                if (name, half) in HELD:
-                    dealt = spent_bytes[HELD[name, half]]
-                else:
-                    dealt = ring.tile([P, HALF, P, PACK], BF16, name="dealt", tag="dealt", bufs=6, align_bytes=64)[:]
-                spent_bytes[name, half] = dealt
-                dst = dealt.rearrange("p t m i -> p m i t")
-                part = src[:, :, :, half * HALF : (half + 1) * HALF]
-                if (name, half) in ON_VECTOR:
-                    nc.vector.tensor_scalar(dst, part, sign, None, ALU.mult)
-                else:
-                    nc.scalar.activation(dst, part, ACT.Copy, scale=sign)
-                codes = keep.tile([P, HALF * P], U32, name=f"{name}_codes{half}", align_bytes=64)
-                plane = keep.tile([P, HALF * P], U8, name=f"{name}_plane{half}", align_bytes=64)
-                nc.vector.quantize_mx(
-                    out=codes[:].bitcast(FP8X4), scales=plane[:], in_=dealt.rearrange("p t m i -> p (t m i)")
-                )
-                for t in range(HALF):
-                    cols = slice(t * P, (t + 1) * P)
-                    quantised[name, half * HALF + t] = (codes[:, cols].bitcast(FP8X4), plane[:, cols])
+        def cast_weight(name, half, sign, on_vector):
+            src = raws[name][:].rearrange("p i (m t) -> p m i t", t=PACK)[:, :, :, half * HALF : (half + 1) * HALF]
+            dealt = stage.tile([P, HALF * P * PACK], BF16, name=f"dealt_{name}{half}", tag=f"dealt_{name}{half}", align_bytes=64)
+            dealt_of[name, half] = dealt
+            dst = dealt[:].rearrange("p (t m i) -> p m i t", t=HALF, i=PACK)
+            if on_vector:
+                nc.vector.tensor_scalar(dst, src, sign, None, ALU.mult)
+            else:
+                nc.scalar.activation(dst, src, ACT.Copy, scale=sign)
 
-        v_words = [keep.tile([P, S], U32, name=f"v_words{a}", align_bytes=64) for a in range(PASSES)]
-        v_planes = [keep.tile([P, S], U8, name=f"v_plane{a}", align_bytes=64) for a in range(PASSES)]
-        flow_codes = keep.tile([P, PASSES * PASSES, PACK, 2 * P], U8, name="flow_codes", align_bytes=64)
-        flow_plane = keep.tile([P, PASSES * PASSES, PACK, P], U8, name="flow_plane", align_bytes=64)
-        nc.vector.tensor_copy(
-            flow_codes[:].bitcast(U16),
-            flow_raw[:].bitcast(U16).rearrange("p a (b m t) -> p (a b) t m", m=P, t=PACK),
-        )
-        nc.vector.tensor_copy(v_planes[0][:], tab_planes[:, 0, :].indirect(offsets[:]))
-        nc.vector.tensor_copy(v_words[0][:], table[0][:].bitcast(U32).indirect(offsets[:]))
-        nc.vector.tensor_copy(v_planes[1][:], tab_planes[:, 1, :].indirect(offsets[:]))
-        nc.vector.tensor_copy(
-            flow_plane[:], flow_plane_raw[:].rearrange("p a (b m t) -> p (a b) t m", m=P, t=PACK)
-        )
-        quantise_weight("f00", -1.0)
-        quantise_weight("f01", -1.0)
-        nc.vector.tensor_copy(v_words[1][:], table[1][:].bitcast(U32).indirect(offsets[:]))
-        quantise_weight("f10", -1.0)
-        quantise_weight("f11", -1.0)
+        def quantise_weight(name, half):
+            codes = held([P, HALF * P], U32, f"{name}_codes{half}")
+            plane = held([P, HALF * P], U8, f"{name}_plane{half}")
+            nc.vector.quantize_mx(out=codes[:].bitcast(FP8X4), scales=plane[:], in_=dealt_of[name, half][:])
+            for t in range(HALF):
+                cols = slice(t * P, (t + 1) * P)
+                quantised[name, half * HALF + t] = (codes[:, cols].bitcast(FP8X4), plane[:, cols])
+
+        def prepare_weight(name, sign, vector_halves):
+            for half in range(2):
+                cast_weight(name, half, sign, half in vector_halves)
+            for half in range(2):
+                quantise_weight(name, half)
+
+        v_words = [held([P, S], U32, f"v_words{a}") for a in range(PASSES)]
+        flow_codes = held([P, PASSES * PASSES, PACK, 2 * P], U8, "flow_codes")
+        flow_plane = held([P, PASSES * PASSES, PACK, P], U8, "flow_plane")
+
+        def listed(j0, j1):
+            return offsets[:, j0 // STRIPE : j1 // STRIPE]
+
+        def gather_words(a, j0, j1):
+            nc.vector.tensor_copy(v_words[a][:, j0:j1], table[a][:].bitcast(U32).indirect(listed(j0, j1)))
 
         def imbalance(bank, b, ranges):
             steps = []
-            for a in range(PASSES):
-                for packed in (True, False):
+            for a, packed in ORDER[b]:
+                if True:
                     col = 0
                     for t, j0, width in ranges:
-                        step = P if packed and width < BANK else width
+                        step = P if packed else width
                         steps.extend((a, packed, t, j0 + d, col + d, step) for d in range(0, width, step))
                         col += width
             for n, (a, packed, t, j0, col, width) in enumerate(steps):
                 if packed:
                     lhs = flow_codes[:, a * PASSES + b, t, :].bitcast(FP4X4)
                     lhs_plane = flow_plane[:, a * PASSES + b, t, :]
+                    rhs_plane = (v_plane, v_plane_low)[a][:, j0 : j0 + width]
                 else:
                     lhs, lhs_plane = quantised[f"f{a}{b}", t]
+                    rhs_plane = v_plane[4 * a : P, j0 : j0 + width]
                 nc.tensor.matmul_mx(
                     out=bank[:, col : col + width],
                     lhsT=lhs,
                     lhsT_scale=lhs_plane,
                     rhs=v_words[a][:, j0 : j0 + width].bitcast(FP8X4),
-                    rhs_scale=v_planes[a][:, j0 : j0 + width],
+                    rhs_scale=rhs_plane,
                     start=(n == 0),
                     stop=(n == len(steps) - 1),
                 )
 
         h_q = {}
+        woven_of = {}
 
-        def quantise_h(woven, c, b):
-            codes = keep.tile([P, CHUNK], U32, name=f"h_codes{c}{b}", align_bytes=64)
-            plane = keep.tile([P, CHUNK], U8, name=f"h_plane{c}{b}", align_bytes=64)
-            nc.vector.quantize_mx(
-                out=codes[:].bitcast(FP8X4), scales=plane[:], in_=woven[:].rearrange("p j t -> p (j t)")
-            )
+        def quantise_h(woven, c, b, codes):
+            plane = held([P, CHUNK], U8, f"h_plane{c}{b}")
+            nc.vector.quantize_mx(out=codes.bitcast(FP8X4), scales=plane[:], in_=woven)
             h_q[c, b] = (codes, plane)
-            woven_of[c, b] = woven
-            spent_bytes["h", c, b] = woven[:].rearrange("p (t m) i -> p t m i", t=HALF)
 
-        def h_by_vector(c, b):
-            j0 = c * CHUNK
-            woven = ring.tile([P, CHUNK, PACK], BF16, name="woven", tag="woven", bufs=4, align_bytes=64)
+        def fresh_woven():
+            return ring.tile([P, CHUNK * PACK], BF16, name="woven", tag="woven", bufs=4, align_bytes=64)[:]
+
+        def fresh_bounded():
+            return ring.tile([P, BANK], F32, name="bounded", tag="bounded", bufs=4, align_bytes=64)[:]
+
+        def h_by_vector(c, b, pair, woven):
             for s in range(CHUNK // P):
-                bank = banks[b][s]
-                imbalance(bank, b, [(t, j0 + s * P, P) for t in range(PACK)])
-                bounded = ring.tile([P, P, PACK], F32, name="bounded", tag="bounded", bufs=10, align_bytes=64)
-                nc.scalar.activation(bounded[:], bank[:].rearrange("p (t j) -> p j t", t=PACK), ACT.Tanh)
+                imbalance(pair[s], b, [(t, c * CHUNK + s * P, P) for t in range(PACK)])
+                bounded = fresh_bounded().rearrange("p (j t) -> p j t", t=PACK)
+                nc.scalar.activation(bounded, pair[s][:].rearrange("p (t j) -> p j t", t=PACK), ACT.Tanh)
                 nc.vector.tensor_tensor(
-                    woven[:, s * P : (s + 1) * P, :],
-                    bounded[:],
+                    woven[:, s * BANK : (s + 1) * BANK].rearrange("p (j t) -> p j t", t=PACK),
+                    bounded,
                     gain_sb[:, b : b + 1, :].to_broadcast([P, P, PACK]),
                     ALU.mult,
                 )
-            quantise_h(woven, c, b)
+            quantise_h(woven, c, b, held([P, CHUNK], U32, f"h_codes{c}{b}")[:])
 
-        bounded_of = {}
+        squashed = [held([P, BANK], F32, f"squashed{s}") for s in range(2)]
+        rounded = [held([P, PACK, CHUNK], BF16, f"rounded{b}") for b in range(PASSES)]
 
-        def bound_scores(c0, c1, b):
-            width = (c1 - c0) * CHUNK
-            per_bank = BANK // width
-            for t0 in range(0, PACK, per_bank):
-                bank = banks[b if c0 == 1 else 1 - b][t0 // per_bank % 2]
-                imbalance(bank, b, [(t, c0 * CHUNK, width) for t in range(t0, t0 + per_bank)])
-                bounded = ring.tile([P, BANK], F32, name="bounded", tag="bounded", bufs=10, align_bytes=64)
-                nc.scalar.activation(bounded[:], bank[:], ACT.Tanh)
-                for t in range(t0, t0 + per_bank):
-                    for c in range(c0, c1):
-                        col = (t - t0) * width + (c - c0) * CHUNK
-                        bounded_of[c, b, t] = bounded[:, col : col + CHUNK]
-                    weigh(c0, b, t)
+        def squash(c, b, s):
+            imbalance(pairs[c, b][s], b, [(t, c * CHUNK, CHUNK) for t in range(s * HALF, (s + 1) * HALF)])
+            nc.scalar.activation(bounded_of(c, b, s), pairs[c, b][s][:], ACT.Tanh)
 
-        rounded_of = {}
+        def bounded_of(c, b, s):
+            return raws["f11"][:, s, :] if (c, b) == (1, 0) else squashed[s][:]
 
-        def weigh(c, b, t):
-            if t == 0:
-                rounded_of[c, b] = ring.tile([P, PACK, CHUNK], BF16, name="rounded", tag="rounded", bufs=2, align_bytes=64)
-            nc.scalar.activation(rounded_of[c, b][:, t, :], bounded_of[c, b, t], ACT.Copy, scale=gain_sb[:, b, t : t + 1])
-            if t == PACK - 1:
-                woven = ring.tile([P, CHUNK, PACK], BF16, name="woven", tag="woven", bufs=4, align_bytes=64)
-                nc.scalar.copy(
-                    woven[:].rearrange("p (c i) t -> p c t i", i=RUN),
-                    rounded_of[c, b][:].rearrange("p t (c i) -> p c t i", i=RUN),
+        def weigh(c, b, s):
+            for t in range(s * HALF, (s + 1) * HALF):
+                col = (t - s * HALF) * CHUNK
+                nc.scalar.activation(
+                    rounded[b][:, t, :], bounded_of(c, b, s)[:, col : col + CHUNK], ACT.Copy, scale=gain_sb[:, b, t : t + 1]
                 )
-                quantise_h(woven, c, b)
+
+        def weave(c, b):
+            woven_of[c, b] = fresh_woven()
+            nc.scalar.copy(
+                woven_of[c, b].rearrange("p (c i t) -> p c t i", i=RUN, t=PACK),
+                rounded[b][:].rearrange("p t (c i) -> p c t i", i=RUN),
+            )
 
         def h_by_scalar(c, b):
-            if c in JOINT:
-                bound_scores(c, JOINT[c], b)
-            else:
-                for t in range(PACK):
-                    weigh(c, b, t)
+            squash(c, b, 1)
+            weigh(c, b, 0)
+            weigh(c, b, 1)
+            if (c, b) != (CHUNKS - 1, PASSES - 1):
+                squash(c + b, 1 - b, 0)
+            weave(c, b)
 
-        def move_chunk(c):
-            groups = ((0,), (1,), (2, 3)) if c == 0 else ((0, 1), (2, 3))
-            free = (banks[2] + banks[3], banks[0], banks[2], banks[2])[c]
-            order = range(PASSES) if c == 0 else range(PASSES - 1, -1, -1)
-            for ts, tile in zip(groups, free):
-                bank = tile[:, 0 : len(ts) * CHUNK].rearrange("p (t j) -> p t j", j=CHUNK)
-                for t in ts:
-                    for b in order:
-                        nc.tensor.matmul_mx(
-                            out=bank[:, t - ts[0], :],
-                            lhsT=quantised[f"w{b}", t][0],
-                            lhsT_scale=quantised[f"w{b}", t][1],
-                            rhs=h_q[c, b][0][:].bitcast(FP8X4),
-                            rhs_scale=h_q[c, b][1][:],
-                            start=(b == order[0]),
-                            stop=(b == order[-1]),
-                        )
-                copy = nc.vector.tensor_copy if c == 0 and ts[0] < HALF else nc.scalar.copy
-                copy(move[:, ts[0] : ts[-1] + 1, c * CHUNK : (c + 1) * CHUNK], bank)
+        move = held([P, PACK, S], F32, "move")
 
-        move = keep.tile([P, PACK, S], F32, name="move", align_bytes=64)
-
-        def update_pages(steps, spent, held):
-            new = {}
-
-            def add_state(n):
-                t, j0, j1 = steps[n]
-                summed = ring.tile([P, j1 - j0], F32, name="summed", tag="summed", bufs=2, align_bytes=64)
-                nc.vector.tensor_tensor(
-                    summed[:], pages[t][:].indirect(offsets[:, j0 // 16 : j1 // 16]), move[:, t, j0:j1], ALU.add
-                )
-                new[n] = summed[:]
-
-            add_state(0)
-            for n, (t, j0, j1) in enumerate(steps):
-                if n + 1 < len(steps):
-                    add_state(n + 1)
-                clipped = new[n]
-                k = n - (len(steps) - held)
-                if spent is not None and k >= 0:
-                    clipped = spent[:].rearrange("p j t -> p (j t)").bitcast(F32)[:, k * CHUNK : (k + 1) * CHUNK]
-                nc.vector.tensor_tensor(clipped, new[n], limit[:, j0:j1], ALU.min)
-                nc.vector.tensor_copy(pages[t][:].indirect(offsets[:, j0 // 16 : j1 // 16]), clipped)
-
-        h_by_vector(0, 0)
-        quantise_weight("w0", 1.0, (0,))
-        quantise_weight("w0", 1.0, (1,))
-        h_by_vector(0, 1)
-        quantise_weight("w1", 1.0, (0,))
-        quantise_weight("w1", 1.0, (1,))
-        for c in range(CHUNKS):
-            move_chunk(c)
-            if c + 1 < CHUNKS:
+        def move_pages(c, ts, tile, copy):
+            bank = tile[:, 0 : len(ts) * CHUNK].rearrange("p (t j) -> p t j", j=CHUNK)
+            for t in ts:
                 for b in range(PASSES):
-                    h_by_scalar(c + 1, b)
-            if c < CHUNKS - 2:
-                steps = [(t, c * CHUNK, (c + 1) * CHUNK) for t in range(PACK)]
+                    nc.tensor.matmul_mx(
+                        out=bank[:, t - ts[0], :],
+                        lhsT=quantised[f"w{b}", t][0],
+                        lhsT_scale=quantised[f"w{b}", t][1],
+                        rhs=h_q[c, b][0].bitcast(FP8X4),
+                        rhs_scale=h_q[c, b][1][:],
+                        start=(b == 0),
+                        stop=(b == PASSES - 1),
+                    )
+            copy(move[:, ts[0] : ts[-1] + 1, c * CHUNK : (c + 1) * CHUNK], bank)
+
+        nc.vector.tensor_copy(
+            flow_codes[:].bitcast(U16).rearrange("p g t m -> p g m t"),
+            flow_raw[:].bitcast(U16).rearrange("p a (b m t) -> p (a b) m t", m=P, t=PACK),
+        )
+        gather_words(0, 0, S)
+        nc.vector.tensor_copy(
+            flow_plane[:].rearrange("p g t m -> p g m t"),
+            flow_plane_raw[:].rearrange("p a (b m t) -> p (a b) m t", m=P, t=PACK),
+        )
+        prepare_weight("f00", -1.0, (1,))
+        prepare_weight("f10", -1.0, (1,))
+        gather_words(1, 0, CHUNK)
+        gather_words(1, CHUNK, S)
+        prepare_weight("f01", -1.0, (1,))
+        prepare_weight("f11", -1.0, (1,))
+        h_by_vector(0, 0, banks[0:2], fresh_woven())
+        prepare_weight("w0", 1.0, (0, 1))
+        h_by_vector(0, 1, banks[2:4], dealt_of["w0", 0][:])
+        cast_weight("w1", 0, 1.0, True)
+        quantise_weight("w1", 0)
+        move_pages(0, (0,), banks[4], nc.vector.tensor_copy)
+        move_pages(0, (1,), banks[5], nc.vector.tensor_copy)
+        cast_weight("w1", 1, 1.0, True)
+        quantise_weight("w1", 1)
+        move_pages(0, (2,), banks[6], nc.scalar.copy)
+        move_pages(0, (3,), banks[7], nc.scalar.copy)
+
+        steps = []
+        for c in range(CHUNKS):
+            steps.extend((t, c * CHUNK, (c + 1) * CHUNK) for t in range(PACK if c < DEFER else HALF))
+        steps.extend((t, DEFER * CHUNK, S) for t in range(HALF, PACK))
+        wide = S - DEFER * CHUNK
+        sum_tiles = [held([P, wide], F32, f"summed{x}") for x in range(2)]
+        clip_tiles = [held([P, wide], F32, f"clipped{x}") for x in range(2)]
+        clipped = {}
+
+        def summed(n):
+            return sum_tiles[n % 2][:, 0 : steps[n][2] - steps[n][1]]
+
+        def add_state(n):
+            t, j0, j1 = steps[n]
+            nc.vector.tensor_tensor(summed(n), pages[t][:].indirect(listed(j0, j1)), move[:, t, j0:j1], ALU.add)
+
+        def clip(n):
+            t, j0, j1 = steps[n]
+            k = [k for k in range(HALF) if n - 1 - k in SLOT]
+            if k:
+                clipped[n] = woven_of[SLOT[n - 1 - k[0]], PASSES - 1].bitcast(F32)[:, k[0] * CHUNK : (k[0] + 1) * CHUNK]
+            elif n == 0:
+                clipped[n] = ring.tile([P, PASSES, CHUNK], F32, name="gate", tag="gate", align_bytes=64)[:, 0, :]
             else:
-                steps = [(t, c * CHUNK, (c + 1) * CHUNK) for t in range(HALF)]
-            if c + 1 == CHUNKS:
-                steps.extend((t, (CHUNKS - 2) * CHUNK, S) for t in range(HALF, PACK))
-            update_pages(steps, woven_of.get((c + 1, PASSES - 1)), HALF)
+                clipped[n] = clip_tiles[n % 2][:, 0 : j1 - j0]
+            nc.vector.tensor_tensor(clipped[n], summed(n), limit[:, j0:j1], ALU.min)
+
+        def put(n):
+            t, j0, j1 = steps[n]
+            nc.vector.tensor_copy(pages[t][:].indirect(listed(j0, j1)), clipped[n])
+
+        def update_pages(n0, n1):
+            for n in range(n0, n1):
+                early = n in SLOT or (0 <= n < len(steps) - 2 and steps[n][0] == steps[n + 2][0])
+                if n + 2 < len(steps) and not early:
+                    add_state(n + 2)
+                if early:
+                    put(n)
+                if n in SLOT:
+                    c = SLOT[n]
+                    tag = "gate" if c == 1 else f"h_codes{c}"
+                    codes = ring.tile([P, PASSES, CHUNK], U32, name="h_codes", tag=tag, align_bytes=64)
+                    for b in range(PASSES - 1, -1, -1):
+                        quantise_h(woven_of[c, b], c, b, codes[:, b, :])
+                if 0 <= n + 1 < len(steps):
+                    clip(n + 1)
+                if n + 2 < len(steps) and early:
+                    add_state(n + 2)
+                if n >= 0 and not early:
+                    put(n)
+
+        pairs = {(c, b): banks[4 * min(c - 1, 1) + 2 * b :][0:2] for c in range(1, CHUNKS) for b in range(PASSES)}
+        squash(1, 0, 0)
+        h_by_scalar(1, 0)
+        h_by_scalar(1, 1)
+        done = -2
+        for n, c in SLOT.items():
+            update_pages(done, n + 1)
+            done = n + 1
+            if c + 1 < CHUNKS:
+                h_by_scalar(c + 1, 0)
+            move_pages(c, (0, 1), banks[0], nc.scalar.copy)
+            move_pages(c, (2, 3), banks[1], nc.scalar.copy)
+            if c + 1 < CHUNKS:
+                h_by_scalar(c + 1, 1)
+        update_pages(done, len(steps))
+
+        small = [f"dealt_f{a}{b}{half}" for a in range(PASSES) for b in range(PASSES) for half in range(2)]
+        large = ["raw_f00", "raw_f10", "raw_f01", "raw_w0"]
+
+        def late_tile(shape, width, name):
+            tag = (small if width == CHUNK else large).pop(0)
+            return stage.tile(shape, BF16, name=name, tag=tag, align_bytes=64)
 
         out_rows = out_0.rearrange("(p t) m -> p t m", t=PACK)
-        pieces = T // PIECE
-        y_rounded = [
-            ring.tile([P, PACK, PIECE], BF16, name="y_rounded", tag="y_rounded", bufs=4, align_bytes=64) for q in range(pieces)
+        starts = [sum(PIECES[:q]) for q in range(len(PIECES))]
+        paired = [
+            late_tile([P, HALF, width, 2], width, f"paired{q}") for q, width in enumerate(PIECES)
         ]
         y_woven = [
-            ring.tile([P, PIECE, PACK], BF16, name="y_woven", tag="y_woven", bufs=4, align_bytes=64) for q in range(pieces)
+            late_tile([P, width * PACK], width, f"y_woven{q}") for q, width in enumerate(PIECES)
         ]
-        by_vector = range(pieces // 2)
-
-        def weave_pair(cols, t0):
-            q, m0 = divmod(cols.start, PIECE)
-            ms = slice(m0, m0 + cols.stop - cols.start)
-            nc.scalar.copy(
-                y_woven[q][:, ms, t0 : t0 + HALF], y_rounded[q][:, t0 : t0 + HALF, ms].rearrange("p t m -> p m t")
-            )
-
-        parts = [slice(0, 512), slice(512, 1024), slice(1024, 1536), slice(1536, 1792), slice(1792, 2048)]
-
-        def weave(copy, q, t0, t1):
-            copy(
-                y_woven[q][:].rearrange("p (c i) t -> p c t i", i=RUN)[:, :, t0:t1, :],
-                y_rounded[q][:].rearrange("p t (c i) -> p c t i", i=RUN)[:, :, t0:t1, :],
-            )
-
-        by_scalar = range(pieces // 2, pieces)
-
-        def page_cols(t, q):
-            return pages[t][:, q * PIECE : (q + 1) * PIECE]
-
         for t in range(PACK):
             nc.sync.dma_start(out_rows[:, t, :], pages[t][:])
-            for q in range(pieces):
-                copy = nc.vector.tensor_copy if t == PACK - 1 and q in by_vector else nc.scalar.copy
-                copy(y_rounded[q][:, t, :], page_cols(t, q))
-                if q in by_scalar and t % HALF == HALF - 1:
-                    for cols in parts:
-                        if cols.start // PIECE == q:
-                            weave_pair(cols, t + 1 - HALF)
-        for q in by_vector:
-            weave(nc.vector.tensor_copy, q, 0, PACK)
-        y_plane = keep.tile([P, T], U8, name="y_plane", align_bytes=64)
+            for q, width in enumerate(PIECES):
+                copy = nc.vector.tensor_copy if q == 0 and t >= HALF else nc.scalar.copy
+                copy(paired[q][:, t // 2, :, t % 2], pages[t][:, starts[q] : starts[q] + width])
+        y_plane = held([P, T], U8, "y_plane")
+        y_codes = held([P, T], I32, "y_codes")
         words_out = out_1[0].rearrange("p m t -> p (m t)").bitcast(I32)
-        y_codes = keep.tile([P, T], I32, name="y_codes", align_bytes=64)
-        stored = 0
-        for cols in parts:
-            q, m0 = divmod(cols.start, PIECE)
-            nc.vector.quantize_mx(
-                out=y_codes[:, cols].bitcast(FP8X4),
-                scales=y_plane[:, cols],
-                in_=y_woven[q][:, m0 : m0 + cols.stop - cols.start, :].rearrange("p m t -> p (m t)"),
-            )
-            if cols.stop > stored:
-                nc.sync.dma_start(words_out[:, stored : cols.stop], y_codes[:, stored : cols.stop])
-                stored = cols.stop
         scale_rows = out_2[0].rearrange("(q r) m -> r q m", q=QUADS)
-        for r in range(4):
-            nc.sync.dma_start(scale_rows[r].bitcast(I32), y_plane[r:P:32, :].bitcast(I32))
+
+        def weave_words(q):
+            copy = nc.scalar.copy if q >= len(PIECES) - SCALAR_PIECES else nc.vector.tensor_copy
+            copy(
+                y_woven[q][:].bitcast(U32).rearrange("p (m u) -> p m u", u=HALF),
+                paired[q][:].rearrange("p u m e -> p (u m e)").bitcast(U32).rearrange("p (u m) -> p m u", u=HALF),
+            )
+
+        def store_scales(m0, m1, queues):
+            for r in range(4):
+                queues[r % 2].dma_start(scale_rows[r][:, m0:m1].bitcast(I32), y_plane[r:P:32, m0:m1].bitcast(I32))
+
+        weave_words(0)
+        for q, width in enumerate(PIECES):
+            if q + 1 < len(PIECES):
+                weave_words(q + 1)
+            cols = slice(starts[q], starts[q] + width)
+            nc.vector.quantize_mx(out=y_codes[:, cols].bitcast(FP8X4), scales=y_plane[:, cols], in_=y_woven[q][:])
+            if cols.stop % BANK == 0:
+                done_cols = slice(cols.stop - BANK, cols.stop)
+                nc.sync.dma_start(words_out[:, done_cols], y_codes[:, done_cols])
+        store_scales(0, T, (nc.sync, nc.scalar))

@@ -30,8 +30,8 @@ STRIPE = 16
 RUN = 4
 PIECES = (256, 256, 512, 512, 256, 256)
 SCALAR_PIECES = 2
+VECTOR_PIECES = 2
 DEFER = 2
-SLOT = {1: 1, 4: 2, 7: 3}
 ORDER = (((0, True), (0, False), (1, True), (1, False)), ((0, True), (1, True), (0, False), (1, False)))
 
 
@@ -98,8 +98,13 @@ def tile_list_bike_route_rebalance_kernel(
                 v_plane_low[32 * q : 32 * q + 4, :].bitcast(I32), v_plane[32 * q + 4 : 32 * q + 8, :].bitcast(I32)
             )
         load_table(1)
-        load_weight("f01", flowT, 0, 1)
-        load_weight("f11", flowT, 1, 1)
+        for a in range(PASSES):
+            name = f"f{a}1"
+            raws[name] = stage.tile([P, 2, PACK, GROUP // 2], F32, name=f"raw_{name}", tag=f"raw_{name}", align_bytes=64)
+            for half in range(2):
+                cols = slice(GROUP + half * GROUP // 2, GROUP + (half + 1) * GROUP // 2)
+                rows = flowT[a * GROUP : (a + 1) * GROUP, cols]
+                nc.sync.dma_start(raws[name][:, half, :, :], rows.rearrange("(p i) c -> p i c", i=PACK))
         load_weight("w0", wm, 0, 0)
         load_weight("w1", wm, 1, 0)
         gT_rows = gT.rearrange("(p t) m -> p t m", t=PACK)
@@ -123,29 +128,37 @@ def tile_list_bike_route_rebalance_kernel(
         quantised = {}
         dealt_of = {}
 
-        def cast_weight(name, half, sign, on_vector):
+        def cast_weight(name, half, sign, on_vector, dealt=None):
             src = raws[name][:].rearrange("p i (m t) -> p m i t", t=PACK)[:, :, :, half * HALF : (half + 1) * HALF]
-            dealt = stage.tile([P, HALF * P * PACK], BF16, name=f"dealt_{name}{half}", tag=f"dealt_{name}{half}", align_bytes=64)
+            if dealt is None:
+                if name not in dealt_of:
+                    dealt_of[name] = stage.tile(
+                        [P, PACK * GROUP], BF16, name=f"dealt_{name}", tag=f"dealt_{name}", align_bytes=64
+                    )
+                dealt = dealt_of[name][:, half * HALF * GROUP : (half + 1) * HALF * GROUP]
             dealt_of[name, half] = dealt
-            dst = dealt[:].rearrange("p (t m i) -> p m i t", t=HALF, i=PACK)
+            dst = dealt.rearrange("p (t m i) -> p m i t", t=HALF, i=PACK)
             if on_vector:
                 nc.vector.tensor_scalar(dst, src, sign, None, ALU.mult)
             else:
                 nc.scalar.activation(dst, src, ACT.Copy, scale=sign)
 
-        def quantise_weight(name, half):
-            codes = held([P, HALF * P], U32, f"{name}_codes{half}")
-            plane = held([P, HALF * P], U8, f"{name}_plane{half}")
-            nc.vector.quantize_mx(out=codes[:].bitcast(FP8X4), scales=plane[:], in_=dealt_of[name, half][:])
-            for t in range(HALF):
-                cols = slice(t * P, (t + 1) * P)
-                quantised[name, half * HALF + t] = (codes[:, cols].bitcast(FP8X4), plane[:, cols])
+        def quantise_weight(name, t0, t1, dealt, codes=None):
+            if codes is None:
+                codes = held([P, (t1 - t0) * P], U32, f"{name}_codes{t0}")[:]
+            plane = held([P, (t1 - t0) * P], U8, f"{name}_plane{t0}")
+            nc.vector.quantize_mx(out=codes.bitcast(FP8X4), scales=plane[:], in_=dealt)
+            for t in range(t0, t1):
+                cols = slice((t - t0) * P, (t - t0 + 1) * P)
+                quantised[name, t] = (codes[:, cols].bitcast(FP8X4), plane[:, cols])
+
+        def quantise_half(name, half, codes=None):
+            quantise_weight(name, half * HALF, (half + 1) * HALF, dealt_of[name, half], codes)
 
         def prepare_weight(name, sign, vector_halves):
             for half in range(2):
                 cast_weight(name, half, sign, half in vector_halves)
-            for half in range(2):
-                quantise_weight(name, half)
+            quantise_weight(name, 0, PACK, dealt_of[name][:])
 
         v_words = [held([P, S], U32, f"v_words{a}") for a in range(PASSES)]
         flow_codes = held([P, PASSES * PASSES, PACK, 2 * P], U8, "flow_codes")
@@ -187,21 +200,17 @@ def tile_list_bike_route_rebalance_kernel(
         h_q = {}
         woven_of = {}
 
-        def quantise_h(woven, c, b, codes):
-            plane = held([P, CHUNK], U8, f"h_plane{c}{b}")
+        def quantise_h(woven, c, b0, b1, codes):
+            plane = held([P, (b1 - b0) * CHUNK], U8, f"h_plane{c}{b0}")
             nc.vector.quantize_mx(out=codes.bitcast(FP8X4), scales=plane[:], in_=woven)
-            h_q[c, b] = (codes, plane)
+            for b in range(b0, b1):
+                cols = slice((b - b0) * CHUNK, (b - b0 + 1) * CHUNK)
+                h_q[c, b] = (codes[:, cols], plane[:, cols])
 
-        def fresh_woven():
-            return ring.tile([P, CHUNK * PACK], BF16, name="woven", tag="woven", bufs=4, align_bytes=64)[:]
-
-        def fresh_bounded():
-            return ring.tile([P, BANK], F32, name="bounded", tag="bounded", bufs=4, align_bytes=64)[:]
-
-        def h_by_vector(c, b, pair, woven):
+        def h_by_vector(c, b, pair, woven, spent):
             for s in range(CHUNK // P):
                 imbalance(pair[s], b, [(t, c * CHUNK + s * P, P) for t in range(PACK)])
-                bounded = fresh_bounded().rearrange("p (j t) -> p j t", t=PACK)
+                bounded = spent[:, s, :].rearrange("p (j t) -> p j t", t=PACK)
                 nc.scalar.activation(bounded, pair[s][:].rearrange("p (t j) -> p j t", t=PACK), ACT.Tanh)
                 nc.vector.tensor_tensor(
                     woven[:, s * BANK : (s + 1) * BANK].rearrange("p (j t) -> p j t", t=PACK),
@@ -209,30 +218,33 @@ def tile_list_bike_route_rebalance_kernel(
                     gain_sb[:, b : b + 1, :].to_broadcast([P, P, PACK]),
                     ALU.mult,
                 )
-            quantise_h(woven, c, b, held([P, CHUNK], U32, f"h_codes{c}{b}")[:])
+            quantise_h(woven, c, b, b + 1, held([P, CHUNK], U32, f"h_codes{c}{b}")[:])
 
-        squashed = [held([P, BANK], F32, f"squashed{s}") for s in range(2)]
+        squashed = raws["f11"][:, 0, :, :].rearrange("p (u i) c -> p u (i c)", u=2)
         rounded = [held([P, PACK, CHUNK], BF16, f"rounded{b}") for b in range(PASSES)]
 
         def squash(c, b, s):
             imbalance(pairs[c, b][s], b, [(t, c * CHUNK, CHUNK) for t in range(s * HALF, (s + 1) * HALF)])
-            nc.scalar.activation(bounded_of(c, b, s), pairs[c, b][s][:], ACT.Tanh)
+            nc.scalar.activation(squashed[:, s, :], pairs[c, b][s][:], ACT.Tanh)
 
-        def bounded_of(c, b, s):
-            return raws["f11"][:, s, :] if (c, b) == (1, 0) else squashed[s][:]
+        def rounded_of(c, b):
+            if (c, b) == (1, 0):
+                return dealt_of["w0", 1].rearrange("p (t j) -> p t j", t=PACK)
+            return rounded[b][:]
 
         def weigh(c, b, s):
             for t in range(s * HALF, (s + 1) * HALF):
                 col = (t - s * HALF) * CHUNK
                 nc.scalar.activation(
-                    rounded[b][:, t, :], bounded_of(c, b, s)[:, col : col + CHUNK], ACT.Copy, scale=gain_sb[:, b, t : t + 1]
+                    rounded_of(c, b)[:, t, :], squashed[:, s, :][:, col : col + CHUNK], ACT.Copy, scale=gain_sb[:, b, t : t + 1]
                 )
 
         def weave(c, b):
-            woven_of[c, b] = fresh_woven()
+            if b == 0:
+                woven_of[c] = ring.tile([P, PASSES * CHUNK * PACK], BF16, name="woven", tag="woven", bufs=2, align_bytes=64)
             nc.scalar.copy(
-                woven_of[c, b].rearrange("p (c i t) -> p c t i", i=RUN, t=PACK),
-                rounded[b][:].rearrange("p t (c i) -> p c t i", i=RUN),
+                woven_of[c][:, b * CHUNK * PACK : (b + 1) * CHUNK * PACK].rearrange("p (c i t) -> p c t i", i=RUN, t=PACK),
+                rounded_of(c, b).rearrange("p t (c i) -> p c t i", i=RUN),
             )
 
         def h_by_scalar(c, b):
@@ -243,7 +255,7 @@ def tile_list_bike_route_rebalance_kernel(
                 squash(c + b, 1 - b, 0)
             weave(c, b)
 
-        move = held([P, PACK, S], F32, "move")
+        move = {}
 
         def move_pages(c, ts, tile, copy):
             bank = tile[:, 0 : len(ts) * CHUNK].rearrange("p (t j) -> p t j", j=CHUNK)
@@ -254,11 +266,29 @@ def tile_list_bike_route_rebalance_kernel(
                         lhsT=quantised[f"w{b}", t][0],
                         lhsT_scale=quantised[f"w{b}", t][1],
                         rhs=h_q[c, b][0].bitcast(FP8X4),
-                        rhs_scale=h_q[c, b][1][:],
+                        rhs_scale=h_q[c, b][1],
                         start=(b == 0),
                         stop=(b == PASSES - 1),
                     )
-            copy(move[:, ts[0] : ts[-1] + 1, c * CHUNK : (c + 1) * CHUNK], bank)
+            moved = ring.tile([P, len(ts), CHUNK], F32, name="move", tag=f"move{c}{ts[0]}", align_bytes=64)
+            copy(moved[:], bank)
+            for t in ts:
+                move[c, t] = moved[:, t - ts[0], :]
+
+        def move_wide(t, tile):
+            for c in range(DEFER, CHUNKS):
+                for b in range(PASSES):
+                    nc.tensor.matmul_mx(
+                        out=tile[:, (c - DEFER) * CHUNK : (c - DEFER + 1) * CHUNK],
+                        lhsT=quantised[f"w{b}", t][0],
+                        lhsT_scale=quantised[f"w{b}", t][1],
+                        rhs=h_q[c, b][0].bitcast(FP8X4),
+                        rhs_scale=h_q[c, b][1],
+                        start=(b == 0),
+                        stop=(b == PASSES - 1),
+                    )
+            move[DEFER, t] = held([P, BANK], F32, f"move_wide{t}")[:]
+            nc.scalar.copy(move[DEFER, t], tile[:])
 
         nc.vector.tensor_copy(
             flow_codes[:].bitcast(U16).rearrange("p g t m -> p g m t"),
@@ -269,96 +299,94 @@ def tile_list_bike_route_rebalance_kernel(
             flow_plane[:].rearrange("p g t m -> p g m t"),
             flow_plane_raw[:].rearrange("p a (b m t) -> p (a b) m t", m=P, t=PACK),
         )
-        prepare_weight("f00", -1.0, (1,))
+        prepare_weight("f00", -1.0, ())
         prepare_weight("f10", -1.0, (1,))
         gather_words(1, 0, CHUNK)
         gather_words(1, CHUNK, S)
-        prepare_weight("f01", -1.0, (1,))
-        prepare_weight("f11", -1.0, (1,))
-        h_by_vector(0, 0, banks[0:2], fresh_woven())
-        prepare_weight("w0", 1.0, (0, 1))
-        h_by_vector(0, 1, banks[2:4], dealt_of["w0", 0][:])
+        for name in ("f01", "f11"):
+            dealt = stage.tile([P, PACK * GROUP], BF16, name=f"dealt_{name}", tag=f"dealt_{name}", align_bytes=64)
+            for half in range(2):
+                src = raws[name][:, half, :, :].rearrange("p i (m t) -> p m i t", t=PACK)
+                dst = dealt[:].rearrange("p (t m i) -> p m i t", t=PACK, i=PACK)[:, half * P // 2 : (half + 1) * P // 2]
+                if half == 0:
+                    nc.scalar.activation(dst, src, ACT.Copy, scale=-1.0)
+                else:
+                    nc.vector.tensor_scalar(dst, src, -1.0, None, ALU.mult)
+            quantise_weight(name, 0, PACK, dealt[:])
+        h_by_vector(0, 0, banks[0:2], raws["f01"][:, 1, 0:HALF, :].rearrange("p i c -> p (i c)").bitcast(BF16), raws["f01"][:, 0, :, :].rearrange("p (u i) c -> p u (i c)", u=2))
+        for half in range(2):
+            cast_weight("w0", half, 1.0, True)
+        for half in range(2):
+            quantise_half("w0", half)
+        h_by_vector(0, 1, banks[2:4], dealt_of["w0", 0], held([P, CHUNK // P, BANK], F32, "bounded"))
         cast_weight("w1", 0, 1.0, True)
-        quantise_weight("w1", 0)
-        move_pages(0, (0,), banks[4], nc.vector.tensor_copy)
-        move_pages(0, (1,), banks[5], nc.vector.tensor_copy)
+        quantise_half("w1", 0)
+        move_pages(0, (0,), banks[0], nc.vector.tensor_copy)
+        move_pages(0, (1,), banks[1], nc.vector.tensor_copy)
         cast_weight("w1", 1, 1.0, True)
-        quantise_weight("w1", 1)
+        quantise_half("w1", 1)
         move_pages(0, (2,), banks[6], nc.scalar.copy)
         move_pages(0, (3,), banks[7], nc.scalar.copy)
 
-        steps = []
-        for c in range(CHUNKS):
-            steps.extend((t, c * CHUNK, (c + 1) * CHUNK) for t in range(PACK if c < DEFER else HALF))
-        steps.extend((t, DEFER * CHUNK, S) for t in range(HALF, PACK))
-        wide = S - DEFER * CHUNK
-        sum_tiles = [held([P, wide], F32, f"summed{x}") for x in range(2)]
-        clip_tiles = [held([P, wide], F32, f"clipped{x}") for x in range(2)]
-        clipped = {}
+        rooms = [held([P, BANK], F32, f"room{x}") for x in range(3)]
+        new = {}
 
-        def summed(n):
-            return sum_tiles[n % 2][:, 0 : steps[n][2] - steps[n][1]]
+        def span(c, t):
+            return (c * CHUNK, S if c == DEFER and t >= HALF else (c + 1) * CHUNK)
 
-        def add_state(n):
-            t, j0, j1 = steps[n]
-            nc.vector.tensor_tensor(summed(n), pages[t][:].indirect(listed(j0, j1)), move[:, t, j0:j1], ALU.add)
+        def add_state(c, t, room):
+            new[c, t] = room
+            nc.vector.tensor_tensor(room, pages[t][:].indirect(listed(*span(c, t))), move[c, t], ALU.add)
 
-        def clip(n):
-            t, j0, j1 = steps[n]
-            k = [k for k in range(HALF) if n - 1 - k in SLOT]
-            if k:
-                clipped[n] = woven_of[SLOT[n - 1 - k[0]], PASSES - 1].bitcast(F32)[:, k[0] * CHUNK : (k[0] + 1) * CHUNK]
-            elif n == 0:
-                clipped[n] = ring.tile([P, PASSES, CHUNK], F32, name="gate", tag="gate", align_bytes=64)[:, 0, :]
+        def clip(c, t, room=None):
+            j0, j1 = span(c, t)
+            summed = new[c, t]
+            new[c, t] = summed if room is None else room
+            nc.vector.tensor_tensor(new[c, t], summed, limit[:, j0:j1], ALU.min)
+
+        def put(c, t):
+            nc.vector.tensor_copy(pages[t][:].indirect(listed(*span(c, t))), new[c, t])
+
+        def next_chunk(c, tag):
+            codes = ring.tile([P, PASSES * CHUNK], U32, name="h_codes", tag=tag, align_bytes=64)
+            quantise_h(woven_of[c][:], c, 0, PASSES, codes[:])
+            after_quantise(c)
+            return [woven_of[c][:].bitcast(F32)[:, k * CHUNK : (k + 1) * CHUNK] for k in range(HALF)]
+
+        def update_pair(c, t0, room, ahead=None):
+            for k in range(HALF):
+                add_state(c, t0 + k, room[:, k * CHUNK : (k + 1) * CHUNK])
+            spent = [move[c, t0 + 1] if c == 0 else None, None]
+            if ahead is not None:
+                spent = next_chunk(ahead, f"h_codes{ahead}")
+            for k in range(HALF):
+                clip(c, t0 + k, spent[k])
+            for k in range(HALF):
+                put(c, t0 + k)
+
+        def after_quantise(c):
+            if c + 1 < CHUNKS:
+                h_by_scalar(c + 1, 0)
+            move_pages(c, (0, 1), banks[4], nc.scalar.copy)
+            if c < DEFER:
+                move_pages(c, (2, 3), banks[5], nc.scalar.copy)
+            if c + 1 < CHUNKS:
+                h_by_scalar(c + 1, 1)
             else:
-                clipped[n] = clip_tiles[n % 2][:, 0 : j1 - j0]
-            nc.vector.tensor_tensor(clipped[n], summed(n), limit[:, j0:j1], ALU.min)
+                for t in range(HALF, PACK):
+                    move_wide(t, banks[t])
 
-        def put(n):
-            t, j0, j1 = steps[n]
-            nc.vector.tensor_copy(pages[t][:].indirect(listed(j0, j1)), clipped[n])
-
-        def update_pages(n0, n1):
-            for n in range(n0, n1):
-                early = n in SLOT or (0 <= n < len(steps) - 2 and steps[n][0] == steps[n + 2][0])
-                if n + 2 < len(steps) and not early:
-                    add_state(n + 2)
-                if early:
-                    put(n)
-                if n in SLOT:
-                    c = SLOT[n]
-                    tag = "gate" if c == 1 else f"h_codes{c}"
-                    codes = ring.tile([P, PASSES, CHUNK], U32, name="h_codes", tag=tag, align_bytes=64)
-                    for b in range(PASSES - 1, -1, -1):
-                        quantise_h(woven_of[c, b], c, b, codes[:, b, :])
-                if 0 <= n + 1 < len(steps):
-                    clip(n + 1)
-                if n + 2 < len(steps) and early:
-                    add_state(n + 2)
-                if n >= 0 and not early:
-                    put(n)
-
-        pairs = {(c, b): banks[4 * min(c - 1, 1) + 2 * b :][0:2] for c in range(1, CHUNKS) for b in range(PASSES)}
+        pairs = {(c, b): [banks[x] for x in ((1, 6), (7, 0))[b]] for c in range(2, CHUNKS) for b in range(PASSES)}
+        pairs[1, 0] = banks[4:6]
+        pairs[1, 1] = [banks[2], banks[0]]
         squash(1, 0, 0)
         h_by_scalar(1, 0)
         h_by_scalar(1, 1)
-        done = -2
-        for n, c in SLOT.items():
-            update_pages(done, n + 1)
-            done = n + 1
-            if c + 1 < CHUNKS:
-                h_by_scalar(c + 1, 0)
-            move_pages(c, (0, 1), banks[0], nc.scalar.copy)
-            move_pages(c, (2, 3), banks[1], nc.scalar.copy)
-            if c + 1 < CHUNKS:
-                h_by_scalar(c + 1, 1)
-        update_pages(done, len(steps))
-
-        small = [f"dealt_f{a}{b}{half}" for a in range(PASSES) for b in range(PASSES) for half in range(2)]
-        large = ["raw_f00", "raw_f10", "raw_f01", "raw_w0"]
+        spare = [f"{kind}_{name}" for kind in ("dealt", "raw") for name in ("f00", "f10", "f01", "w0", "w1")]
+        spare.extend(("dealt_f11", "extra"))
 
         def late_tile(shape, width, name):
-            tag = (small if width == CHUNK else large).pop(0)
+            tag = spare.pop(0)
             return stage.tile(shape, BF16, name=name, tag=tag, align_bytes=64)
 
         out_rows = out_0.rearrange("(p t) m -> p t m", t=PACK)
@@ -369,11 +397,36 @@ def tile_list_bike_route_rebalance_kernel(
         y_woven = [
             late_tile([P, width * PACK], width, f"y_woven{q}") for q, width in enumerate(PIECES)
         ]
-        for t in range(PACK):
+
+        def hand_out(t):
             nc.sync.dma_start(out_rows[:, t, :], pages[t][:])
             for q, width in enumerate(PIECES):
-                copy = nc.vector.tensor_copy if q == 0 and t >= HALF else nc.scalar.copy
+                copy = nc.vector.tensor_copy if q < VECTOR_PIECES and t >= HALF else nc.scalar.copy
                 copy(paired[q][:, t // 2, :, t % 2], pages[t][:, starts[q] : starts[q] + width])
+
+        update_pair(0, 0, rooms[0])
+        next_chunk(1, "move01")
+        update_pair(0, HALF, rooms[1])
+        update_pair(1, 0, rooms[1])
+        update_pair(1, HALF, rooms[0], 2)
+        update_pair(2, 0, rooms[1], 3)
+        for t in range(HALF):
+            add_state(3, t, rooms[0][:, t * CHUNK : (t + 1) * CHUNK])
+        add_state(DEFER, 2, rooms[2][:])
+        for t in range(HALF):
+            clip(3, t)
+        put(3, 0)
+        hand_out(0)
+        clip(DEFER, 2)
+        put(3, 1)
+        hand_out(1)
+        add_state(DEFER, 3, move[DEFER, 2])
+        put(DEFER, 2)
+        clip(DEFER, 3)
+        hand_out(2)
+        put(DEFER, 3)
+        hand_out(3)
+
         y_plane = held([P, T], U8, "y_plane")
         y_codes = held([P, T], I32, "y_codes")
         words_out = out_1[0].rearrange("p m t -> p (m t)").bitcast(I32)
@@ -390,9 +443,9 @@ def tile_list_bike_route_rebalance_kernel(
             for r in range(4):
                 queues[r % 2].dma_start(scale_rows[r][:, m0:m1].bitcast(I32), y_plane[r:P:32, m0:m1].bitcast(I32))
 
-        weave_words(0)
         for q, width in enumerate(PIECES):
-            if q + 1 < len(PIECES):
+            if q % 2 == 0:
+                weave_words(q)
                 weave_words(q + 1)
             cols = slice(starts[q], starts[q] + width)
             nc.vector.quantize_mx(out=y_codes[:, cols].bitcast(FP8X4), scales=y_plane[:, cols], in_=y_woven[q][:])

@@ -256,6 +256,7 @@ def tile_list_bike_route_rebalance_kernel(
             weave(c, b)
 
         move = {}
+        margin = {}
 
         def move_pages(c, ts, tile, copy):
             bank = tile[:, 0 : len(ts) * CHUNK].rearrange("p (t j) -> p t j", j=CHUNK)
@@ -270,10 +271,11 @@ def tile_list_bike_route_rebalance_kernel(
                         start=(b == 0),
                         stop=(b == PASSES - 1),
                     )
-            moved = ring.tile([P, len(ts), CHUNK], F32, name="move", tag=f"move{c}{ts[0]}", align_bytes=64)
-            copy(moved[:], bank)
+            moved = ring.tile([P, len(ts) * CHUNK + P], F32, name="move", tag=f"move{c}{ts[0]}", align_bytes=64)
+            copy(moved[:, P:].rearrange("p (t j) -> p t j", j=CHUNK), bank)
+            margin[c, ts[0]] = moved[:, 0:CHUNK]
             for t in ts:
-                move[c, t] = moved[:, t - ts[0], :]
+                move[c, t] = moved[:, P + (t - ts[0]) * CHUNK : P + (t - ts[0] + 1) * CHUNK]
 
         def move_wide(t, tile):
             for c in range(DEFER, CHUNKS):
@@ -336,7 +338,11 @@ def tile_list_bike_route_rebalance_kernel(
 
         def add_state(c, t, room):
             new[c, t] = room
-            nc.vector.tensor_tensor(room, pages[t][:].indirect(listed(*span(c, t))), move[c, t], ALU.add)
+            j0, j1 = span(c, t)
+            width = P if c == 0 and t % HALF else j1 - j0
+            for d in range(0, j1 - j0, width):
+                picked = pages[t][:].indirect(listed(j0 + d, j0 + d + width))
+                nc.vector.tensor_tensor(room[:, d : d + width], picked, move[c, t][:, d : d + width], ALU.add)
 
         def clip(c, t, room=None):
             j0, j1 = span(c, t)
@@ -349,14 +355,20 @@ def tile_list_bike_route_rebalance_kernel(
 
         def next_chunk(c, tag):
             codes = ring.tile([P, PASSES * CHUNK], U32, name="h_codes", tag=tag, align_bytes=64)
-            quantise_h(woven_of[c][:], c, 0, PASSES, codes[:])
+            plane = held([P, PASSES * CHUNK], U8, f"h_plane{c}")
+            for m0, m1 in ((0, PASSES * CHUNK),) if c == 1 else ((0, CHUNK), (CHUNK, CHUNK + P), (CHUNK + P, 2 * CHUNK)):
+                nc.vector.quantize_mx(
+                    out=codes[:, m0:m1].bitcast(FP8X4), scales=plane[:, m0:m1], in_=woven_of[c][:, m0 * PACK : m1 * PACK]
+                )
+            for b in range(PASSES):
+                h_q[c, b] = (codes[:, b * CHUNK : (b + 1) * CHUNK], plane[:, b * CHUNK : (b + 1) * CHUNK])
             after_quantise(c)
-            return [woven_of[c][:].bitcast(F32)[:, k * CHUNK : (k + 1) * CHUNK] for k in range(HALF)]
+            return [woven_of[c][:].bitcast(F32)[:, (HALF + k) * CHUNK : (HALF + k + 1) * CHUNK] for k in range(HALF)]
 
         def update_pair(c, t0, room, ahead=None):
             for k in range(HALF):
                 add_state(c, t0 + k, room[:, k * CHUNK : (k + 1) * CHUNK])
-            spent = [move[c, t0 + 1] if c == 0 else None, None]
+            spent = [margin[c, t0 + 1] if c == 0 else None, None]
             if ahead is not None:
                 spent = next_chunk(ahead, f"h_codes{ahead}")
             for k in range(HALF):
@@ -365,14 +377,17 @@ def tile_list_bike_route_rebalance_kernel(
                 put(c, t0 + k)
 
         def after_quantise(c):
-            if c + 1 < CHUNKS:
-                h_by_scalar(c + 1, 0)
-            move_pages(c, (0, 1), banks[4], nc.scalar.copy)
             if c < DEFER:
+                h_by_scalar(c + 1, 0)
+                move_pages(c, (0, 1), banks[4], nc.scalar.copy)
                 move_pages(c, (2, 3), banks[5], nc.scalar.copy)
-            if c + 1 < CHUNKS:
                 h_by_scalar(c + 1, 1)
-            else:
+                return
+            if c + 1 < CHUNKS:
+                for b in range(PASSES):
+                    h_by_scalar(c + 1, b)
+            move_pages(c, (0, 1), banks[4], nc.scalar.copy)
+            if c + 1 == CHUNKS:
                 for t in range(HALF, PACK):
                     move_wide(t, banks[t])
 

@@ -225,18 +225,18 @@ def tile_list_bike_route_rebalance_kernel(
 
         def squash(c, b, s):
             imbalance(pairs[c, b][s], b, [(t, c * CHUNK, CHUNK) for t in range(s * HALF, (s + 1) * HALF)])
-            nc.scalar.activation(squashed[:, s, :], pairs[c, b][s][:], ACT.Tanh)
+            nc.scalar.activation(squashed[:, s if (c, b) == (1, 0) else 1 - s, :], pairs[c, b][s][:], ACT.Tanh)
 
         def rounded_of(c, b):
             if (c, b) == (1, 0):
-                return dealt_of["w0", 1].rearrange("p (t j) -> p t j", t=PACK)
+                return dealt_w0[:, part : 2 * part].rearrange("p (t j) -> p t j", t=PACK)
             return rounded[b][:]
 
         def weigh(c, b, s):
             for t in range(s * HALF, (s + 1) * HALF):
                 col = (t - s * HALF) * CHUNK
                 nc.scalar.activation(
-                    rounded_of(c, b)[:, t, :], squashed[:, s, :][:, col : col + CHUNK], ACT.Copy, scale=gain_sb[:, b, t : t + 1]
+                    rounded_of(c, b)[:, t, :], squashed[:, s if (c, b) == (1, 0) else 1 - s, :][:, col : col + CHUNK], ACT.Copy, scale=gain_sb[:, b, t : t + 1]
                 )
 
         def weave(c, b):
@@ -247,9 +247,11 @@ def tile_list_bike_route_rebalance_kernel(
                 rounded_of(c, b).rearrange("p t (c i) -> p c t i", i=RUN),
             )
 
-        def h_by_scalar(c, b):
+        def h_by_scalar(c, b, midway=None):
             squash(c, b, 1)
             weigh(c, b, 0)
+            if midway is not None:
+                midway()
             weigh(c, b, 1)
             if (c, b) != (CHUNKS - 1, PASSES - 1):
                 squash(c + b, 1 - b, 0)
@@ -258,7 +260,7 @@ def tile_list_bike_route_rebalance_kernel(
         move = {}
         margin = {}
 
-        def move_pages(c, ts, tile, copy):
+        def move_pages(c, ts, tile, copy, apart=False):
             bank = tile[:, 0 : len(ts) * CHUNK].rearrange("p (t j) -> p t j", j=CHUNK)
             for t in ts:
                 for b in range(PASSES):
@@ -271,11 +273,12 @@ def tile_list_bike_route_rebalance_kernel(
                         start=(b == 0),
                         stop=(b == PASSES - 1),
                     )
-            moved = ring.tile([P, len(ts) * CHUNK + P], F32, name="move", tag=f"move{c}{ts[0]}", align_bytes=64)
-            copy(moved[:, P:].rearrange("p (t j) -> p t j", j=CHUNK), bank)
-            margin[c, ts[0]] = moved[:, 0:CHUNK]
-            for t in ts:
-                move[c, t] = moved[:, P + (t - ts[0]) * CHUNK : P + (t - ts[0] + 1) * CHUNK]
+            for group in [(t,) for t in ts] if apart else [ts]:
+                moved = ring.tile([P, len(group) * CHUNK + P], F32, name="move", tag=f"move{c}{group[0]}", align_bytes=64)
+                copy(moved[:, P:].rearrange("p (t j) -> p t j", j=CHUNK), bank[:, group[0] - ts[0] : group[-1] - ts[0] + 1, :])
+                margin[c, group[0]] = moved[:, 0:CHUNK]
+                for t in group:
+                    move[c, t] = moved[:, P + (t - group[0]) * CHUNK : P + (t - group[0] + 1) * CHUNK]
 
         def move_wide(t, tile):
             for c in range(DEFER, CHUNKS):
@@ -316,8 +319,10 @@ def tile_list_bike_route_rebalance_kernel(
                     nc.vector.tensor_scalar(dst, src, -1.0, None, ALU.mult)
             quantise_weight(name, 0, PACK, dealt[:])
         h_by_vector(0, 0, banks[0:2], raws["f01"][:, 1, 0:HALF, :].rearrange("p i c -> p (i c)").bitcast(BF16), raws["f01"][:, 0, :, :].rearrange("p (u i) c -> p u (i c)", u=2))
+        part = HALF * GROUP
+        dealt_w0 = stage.tile([P, 2 * part + part // 2], BF16, name="dealt_w0", tag="dealt_w0", align_bytes=64)
         for half in range(2):
-            cast_weight("w0", half, 1.0, True)
+            cast_weight("w0", half, 1.0, True, dealt_w0[:, half * (part + part // 2) :][:, 0:part])
         for half in range(2):
             quantise_half("w0", half)
         h_by_vector(0, 1, banks[2:4], dealt_of["w0", 0], held([P, CHUNK // P, BANK], F32, "bounded"))
@@ -356,7 +361,7 @@ def tile_list_bike_route_rebalance_kernel(
         def next_chunk(c, tag):
             codes = ring.tile([P, PASSES * CHUNK], U32, name="h_codes", tag=tag, align_bytes=64)
             plane = held([P, PASSES * CHUNK], U8, f"h_plane{c}")
-            for m0, m1 in ((0, PASSES * CHUNK),) if c == 1 else ((0, CHUNK), (CHUNK, CHUNK + P), (CHUNK + P, 2 * CHUNK)):
+            for m0, m1 in ((0, PASSES * CHUNK),) if c == 1 else ((CHUNK, 2 * CHUNK), (0, CHUNK)):
                 nc.vector.quantize_mx(
                     out=codes[:, m0:m1].bitcast(FP8X4), scales=plane[:, m0:m1], in_=woven_of[c][:, m0 * PACK : m1 * PACK]
                 )
@@ -370,24 +375,23 @@ def tile_list_bike_route_rebalance_kernel(
                 add_state(c, t0 + k, room[:, k * CHUNK : (k + 1) * CHUNK])
             spent = [margin[c, t0 + 1] if c == 0 else None, None]
             if ahead is not None:
-                spent = next_chunk(ahead, f"h_codes{ahead}")
+                spent = next_chunk(ahead, f"move{c}{t0}")
             for k in range(HALF):
                 clip(c, t0 + k, spent[k])
             for k in range(HALF):
                 put(c, t0 + k)
 
         def after_quantise(c):
-            if c < DEFER:
-                h_by_scalar(c + 1, 0)
-                move_pages(c, (0, 1), banks[4], nc.scalar.copy)
-                move_pages(c, (2, 3), banks[5], nc.scalar.copy)
-                h_by_scalar(c + 1, 1)
-                return
             if c + 1 < CHUNKS:
-                for b in range(PASSES):
-                    h_by_scalar(c + 1, b)
-            move_pages(c, (0, 1), banks[4], nc.scalar.copy)
-            if c + 1 == CHUNKS:
+                h_by_scalar(c + 1, 0)
+            if c < DEFER:
+                move_pages(c, (0, 1), banks[4], nc.scalar.copy)
+                move_pages(c, (2, 3), banks[5], nc.scalar.copy, True)
+                h_by_scalar(c + 1, 1)
+            elif c + 1 < CHUNKS:
+                h_by_scalar(c + 1, 1, lambda: move_pages(c, (0, 1), banks[4], nc.scalar.copy, True))
+            else:
+                move_pages(c, (0, 1), banks[4], nc.scalar.copy)
                 for t in range(HALF, PACK):
                     move_wide(t, banks[t])
 

@@ -50,11 +50,13 @@ def tile_list_bike_route_rebalance_kernel(
 
         offsets = keep.tile([P, S // STRIPE], U16, name="offsets")
         tab_planes = held([P, T], U8, "tab_planes")
-        v_plane_low = held([P, S], U8, "v_plane_low")
+        v_planes = held([P, PASSES, S], U8, "v_planes")
         flow_plane_raw = held([P, PASSES, K], U8, "flow_plane_raw")
         nc.vector.memset(tab_planes[:].bitcast(I32), 0)
         nc.vector.memset(flow_plane_raw[:].bitcast(I32), 0)
-        nc.vector.memset(v_plane_low[:].bitcast(I32), 0)
+        nc.vector.memset(v_planes[:].bitcast(I32), 0)
+        lines = held([P, GROUP], F32, "lines")
+        nc.gpsimd.memset(lines[:], 0.0)
         ident = held([P, P], F32, "ident")
         make_identity(nc, ident[:])
         docks_rows = held([P, S // P], F32, "docks_rows")
@@ -79,24 +81,27 @@ def tile_list_bike_route_rebalance_kernel(
             nc.sync.dma_start(table[a][:], tab_words[a].rearrange("p t i -> p (t i)").bitcast(I32))
 
         v_plane = held([P, S], U8, "v_plane")
-        nc.scalar.dma_start(docks_rows[:], docks.rearrange("(p c) -> p c", p=P))
-        nc.sync.dma_start(flow_raw[:], flow_words.rearrange("a p c -> p a c").bitcast(I32))
+        nc.scalar.dma_start(lines[0:PASSES, :], gain.rearrange("(b r) -> b r", b=PASSES))
+        nc.scalar.dma_start(lines[PASSES : PASSES + S // P, 0:P], docks.rearrange("(c p) -> c p", p=P))
         nc.sync.dma_start(offsets[:], offs)
-        for q in range(QUADS):
-            nc.sync.dma_start(
-                tab_planes[32 * q : 32 * q + 4 * PASSES, :].bitcast(I32),
-                tab_scales[:, 4 * q : 4 * q + 4, :].bitcast(I32),
-            )
+        nc.sync.dma_start(flow_raw[:, 0, :], flow_words[0].bitcast(I32))
+        nc.sync.dma_start(tab_planes[0:P:4, :].bitcast(I32), tab_scales.rearrange("a q t -> (a q) t").bitcast(I32))
+        nc.sync.dma_start(flow_raw[:, 1, :], flow_words[1].bitcast(I32))
         load_table(0)
         load_planes(nc.sync, flow_plane_raw, flow_scales)
         load_weight("f00", flowT, 0, 0)
-        load_weight("f10", flowT, 1, 0)
-        nc.sync.dma_start(gain_sb[:], gain.rearrange("(b p t) -> p b t", p=P, t=PACK))
         nc.vector.tensor_copy(v_plane[:], tab_planes[:].indirect(offsets[:]))
-        for q in range(QUADS):
-            nc.sync.dma_start(
-                v_plane_low[32 * q : 32 * q + 4, :].bitcast(I32), v_plane[32 * q + 4 : 32 * q + 8, :].bitcast(I32)
-            )
+
+        def place_planes(a):
+            for q in range(QUADS):
+                first = 64 * a + 16 * q
+                nc.sync.dma_start(
+                    v_planes[32 * q : 32 * q + 4, a, :].bitcast(I32), v_plane[first : first + 16 : 4, :].bitcast(I32)
+                )
+
+        place_planes(0)
+        load_weight("f10", flowT, 1, 0)
+        place_planes(1)
         load_table(1)
         for a in range(PASSES):
             name = f"f{a}1"
@@ -113,17 +118,19 @@ def tile_list_bike_route_rebalance_kernel(
 
         banks = [psum.tile([P, BANK], F32, name=f"bank{x}") for x in range(8)]
 
+        for t in range(PACK):
+            nc.tensor.transpose(banks[4][:, t * P : (t + 1) * P], lines[:, t:GROUP:PACK], ident[:])
+        nc.tensor.transpose(banks[5][:, 0:P], lines[:, 0:P], ident[:])
+        nc.scalar.copy(docks_rows[:], banks[5][:, PASSES : PASSES + S // P])
+        nc.scalar.copy(gain_sb[:], banks[4][:].rearrange("p (t r) -> p r t", t=PACK)[:, 0:PASSES, :])
         limit = held([P, S], F32, "limit")
-        per_row = S // P
-        for half in range(per_row // PACK):
-            spread = banks[6 + half][:].rearrange("p (c r) -> p c r", c=PACK)
+        for half in range(S // BANK):
             for c in range(PACK):
                 col = half * PACK + c
-                nc.tensor.transpose(spread[:, c, :], docks_rows[:, col : col + 1].to_broadcast([P, P]), ident[:])
-            nc.scalar.copy(
-                limit[:].rearrange("p (r c) -> p r c", c=per_row)[:, :, half * PACK : (half + 1) * PACK],
-                spread.rearrange("p c r -> p r c"),
-            )
+                nc.tensor.transpose(
+                    banks[6 + half][:, c * P : (c + 1) * P], docks_rows[:, col : col + 1].to_broadcast([P, P]), ident[:]
+                )
+            nc.scalar.copy(limit[:, half * BANK : (half + 1) * BANK], banks[6 + half][:])
 
         quantised = {}
         dealt_of = {}
@@ -183,10 +190,10 @@ def tile_list_bike_route_rebalance_kernel(
                 if packed:
                     lhs = flow_codes[:, a * PASSES + b, t, :].bitcast(FP4X4)
                     lhs_plane = flow_plane[:, a * PASSES + b, t, :]
-                    rhs_plane = (v_plane, v_plane_low)[a][:, j0 : j0 + width]
+                    rhs_plane = v_planes[:, a, j0 : j0 + width]
                 else:
                     lhs, lhs_plane = quantised[f"f{a}{b}", t]
-                    rhs_plane = v_plane[4 * a : P, j0 : j0 + width]
+                    rhs_plane = v_planes[:, a, j0 : j0 + width]
                 nc.tensor.matmul_mx(
                     out=bank[:, col : col + width],
                     lhsT=lhs,
@@ -295,10 +302,11 @@ def tile_list_bike_route_rebalance_kernel(
             move[DEFER, t] = held([P, BANK], F32, f"move_wide{t}")[:]
             nc.scalar.copy(move[DEFER, t], tile[:])
 
-        nc.vector.tensor_copy(
-            flow_codes[:].bitcast(U16).rearrange("p g t m -> p g m t"),
-            flow_raw[:].bitcast(U16).rearrange("p a (b m t) -> p (a b) m t", m=P, t=PACK),
-        )
+        for a in range(PASSES):
+            nc.vector.tensor_copy(
+                flow_codes[:, a * PASSES : (a + 1) * PASSES].bitcast(U16).rearrange("p g t m -> p g m t"),
+                flow_raw[:, a, :].bitcast(U16).rearrange("p (b m t) -> p b m t", m=P, t=PACK),
+            )
         gather_words(0, 0, S)
         nc.vector.tensor_copy(
             flow_plane[:].rearrange("p g t m -> p g m t"),

@@ -81,12 +81,12 @@ def tile_list_bike_route_rebalance_kernel(
             nc.sync.dma_start(table[a][:], tab_words[a].rearrange("p t i -> p (t i)").bitcast(I32))
 
         v_plane = held([P, S], U8, "v_plane")
+        nc.scalar.dma_start(flow_raw[:, 1, :], flow_words[1].bitcast(I32))
         nc.scalar.dma_start(lines[0:PASSES, :], gain.rearrange("(b r) -> b r", b=PASSES))
         nc.scalar.dma_start(lines[PASSES : PASSES + S // P, 0:P], docks.rearrange("(c p) -> c p", p=P))
         nc.sync.dma_start(offsets[:], offs)
         nc.sync.dma_start(flow_raw[:, 0, :], flow_words[0].bitcast(I32))
         nc.sync.dma_start(tab_planes[0:P:4, :].bitcast(I32), tab_scales.rearrange("a q t -> (a q) t").bitcast(I32))
-        nc.sync.dma_start(flow_raw[:, 1, :], flow_words[1].bitcast(I32))
         load_table(0)
         load_planes(nc.sync, flow_plane_raw, flow_scales)
         load_weight("f00", flowT, 0, 0)

@@ -32,6 +32,8 @@ PIECES = (256, 256, 512, 512, 256, 256)
 SCALAR_PIECES = 2
 VECTOR_PIECES = 2
 DEFER = 2
+GPSIMD_FROM = 3
+LOWEST = -3.4028234663852886e38
 ORDER = (((0, True), (0, False), (1, True), (1, False)), ((0, True), (1, True), (0, False), (1, False)))
 
 
@@ -81,12 +83,12 @@ def tile_list_bike_route_rebalance_kernel(
             nc.sync.dma_start(table[a][:], tab_words[a].rearrange("p t i -> p (t i)").bitcast(I32))
 
         v_plane = held([P, S], U8, "v_plane")
-        nc.scalar.dma_start(flow_raw[:, 1, :], flow_words[1].bitcast(I32))
         nc.scalar.dma_start(lines[0:PASSES, :], gain.rearrange("(b r) -> b r", b=PASSES))
         nc.scalar.dma_start(lines[PASSES : PASSES + S // P, 0:P], docks.rearrange("(c p) -> c p", p=P))
         nc.sync.dma_start(offsets[:], offs)
         nc.sync.dma_start(flow_raw[:, 0, :], flow_words[0].bitcast(I32))
         nc.sync.dma_start(tab_planes[0:P:4, :].bitcast(I32), tab_scales.rearrange("a q t -> (a q) t").bitcast(I32))
+        nc.sync.dma_start(flow_raw[:, 1, :], flow_words[1].bitcast(I32))
         load_table(0)
         load_planes(nc.sync, flow_plane_raw, flow_scales)
         load_weight("f00", flowT, 0, 0)
@@ -378,7 +380,7 @@ def tile_list_bike_route_rebalance_kernel(
             after_quantise(c)
             return [woven_of[c][:].bitcast(F32)[:, (HALF + k) * CHUNK : (HALF + k + 1) * CHUNK] for k in range(HALF)]
 
-        def update_pair(c, t0, room, ahead=None):
+        def update_pair(c, t0, room, ahead=None, between=None):
             for k in range(HALF):
                 add_state(c, t0 + k, room[:, k * CHUNK : (k + 1) * CHUNK])
             spent = [margin[c, t0 + 1] if c == 0 else None, None]
@@ -386,6 +388,8 @@ def tile_list_bike_route_rebalance_kernel(
                 spent = next_chunk(ahead, f"move{c}{t0}")
             for k in range(HALF):
                 clip(c, t0 + k, spent[k])
+            if between is not None:
+                between()
             for k in range(HALF):
                 put(c, t0 + k)
 
@@ -409,8 +413,7 @@ def tile_list_bike_route_rebalance_kernel(
         squash(1, 0, 0)
         h_by_scalar(1, 0)
         h_by_scalar(1, 1)
-        spare = [f"{kind}_{name}" for kind in ("dealt", "raw") for name in ("f00", "f10", "f01", "w0", "w1")]
-        spare.extend(("dealt_f11", "extra"))
+        spare = [f"dealt_{name}" for name in ("f00", "f10", "f01", "w0", "w1", "f11")]
 
         def late_tile(shape, width, name):
             tag = spare.pop(0)
@@ -418,9 +421,7 @@ def tile_list_bike_route_rebalance_kernel(
 
         out_rows = out_0.rearrange("(p t) m -> p t m", t=PACK)
         starts = [sum(PIECES[:q]) for q in range(len(PIECES))]
-        paired = [
-            late_tile([P, HALF, width, 2], width, f"paired{q}") for q, width in enumerate(PIECES)
-        ]
+        paired = []
         y_woven = [
             late_tile([P, width * PACK], width, f"y_woven{q}") for q, width in enumerate(PIECES)
         ]
@@ -428,31 +429,59 @@ def tile_list_bike_route_rebalance_kernel(
         def hand_out(t):
             nc.sync.dma_start(out_rows[:, t, :], pages[t][:])
             for q, width in enumerate(PIECES):
-                copy = nc.vector.tensor_copy if q < VECTOR_PIECES and t >= HALF else nc.scalar.copy
-                copy(paired[q][:, t // 2, :, t % 2], pages[t][:, starts[q] : starts[q] + width])
+                dst = paired[q][:, t // 2, :, t % 2]
+                src = pages[t][:, starts[q] : starts[q] + width]
+                if t < HALF and q >= GPSIMD_FROM:
+                    nc.gpsimd.tensor_scalar(dst, src, 1.0, 1.0, ALU.mult, ALU.mult)
+                elif t >= HALF and q < VECTOR_PIECES:
+                    nc.vector.tensor_copy(dst, src)
+                else:
+                    nc.scalar.copy(dst, src)
 
         update_pair(0, 0, rooms[0])
         next_chunk(1, "move01")
         update_pair(0, HALF, rooms[1])
         update_pair(1, 0, rooms[1])
         update_pair(1, HALF, rooms[0], 2)
-        update_pair(2, 0, rooms[1], 3)
+
+        def update_turned(t, picked, turned):
+            nc.vector.tensor_copy(picked, pages[t][:].indirect(listed(*span(DEFER, t))))
+            for x in range(BANK // P):
+                cols = slice(x * P, (x + 1) * P)
+                for last, term in enumerate((move[DEFER, t][:, cols], picked[:, cols])):
+                    nc.tensor.matmul(turned[:, cols], term, ident[:], start=not last, stop=bool(last), is_transpose=True)
+            summed = stage.tile([P, BANK], F32, name=f"summed{t}", tag=("raw_f01", "raw_f00")[t % 2], align_bytes=64)
+            nc.scalar.copy(summed[:], turned[:])
+            clipped = stage.tile([P, BANK], F32, name=f"clipped{t}", tag=("raw_w0", "raw_f10")[t % 2], align_bytes=64)
+            for x in range(BANK // P):
+                cols = slice(x * P, (x + 1) * P)
+                block = DEFER * CHUNK // P + x
+                nc.gpsimd.tensor_scalar(
+                    clipped[:, cols], summed[:, cols], docks_rows[:, block : block + 1], LOWEST, ALU.min, ALU.max
+                )
+            for x in reversed(range(BANK // P)):
+                cols = slice(x * P, (x + 1) * P)
+                nc.tensor.transpose(banks[t][:, cols], clipped[:, cols], ident[:])
+            new[DEFER, t] = move[DEFER, t]
+            nc.scalar.copy(new[DEFER, t], banks[t][:])
+
+        update_pair(2, 0, rooms[1], 3, lambda: update_turned(2, rooms[1][:], banks[5]))
+        update_turned(3, woven_of[3][:].bitcast(F32)[:, BANK : 2 * BANK], banks[6])
+        for tag, q0, q1 in (("raw_f10", 0, GPSIMD_FROM), ("raw_f00", GPSIMD_FROM, len(PIECES))):
+            whole = stage.tile([P, sum(PIECES[q0:q1]) * PACK], BF16, name=f"paired{q0}", tag=tag, align_bytes=64)
+            for q in range(q0, q1):
+                first = (starts[q] - starts[q0]) * PACK
+                paired.append(whole[:, first : first + PIECES[q] * PACK].rearrange("p (u m e) -> p u m e", u=HALF, e=2))
         for t in range(HALF):
             add_state(3, t, rooms[0][:, t * CHUNK : (t + 1) * CHUNK])
-        add_state(DEFER, 2, rooms[2][:])
         for t in range(HALF):
             clip(3, t)
-        put(3, 0)
-        hand_out(0)
-        clip(DEFER, 2)
-        put(3, 1)
-        hand_out(1)
-        add_state(DEFER, 3, move[DEFER, 2])
-        put(DEFER, 2)
-        clip(DEFER, 3)
-        hand_out(2)
-        put(DEFER, 3)
-        hand_out(3)
+        for t in range(HALF):
+            put(3, t)
+            hand_out(t)
+        for t in range(HALF, PACK):
+            put(DEFER, t)
+            hand_out(t)
 
         y_plane = held([P, T], U8, "y_plane")
         y_codes = held([P, T], I32, "y_codes")
@@ -463,7 +492,7 @@ def tile_list_bike_route_rebalance_kernel(
             copy = nc.scalar.copy if q >= len(PIECES) - SCALAR_PIECES else nc.vector.tensor_copy
             copy(
                 y_woven[q][:].bitcast(U32).rearrange("p (m u) -> p m u", u=HALF),
-                paired[q][:].rearrange("p u m e -> p (u m e)").bitcast(U32).rearrange("p (u m) -> p m u", u=HALF),
+                paired[q].rearrange("p u m e -> p (u m e)").bitcast(U32).rearrange("p (u m) -> p m u", u=HALF),
             )
 
         def store_scales(m0, m1, queues):

@@ -28,8 +28,8 @@ CHUNK = 256
 CHUNKS = S // CHUNK
 STRIPE = 16
 RUN = 4
-PIECES = (256, 256, 512, 512, 256, 256)
-SCALAR_PIECES = 2
+PIECES = (256, 256, 512, 256, 256, 256, 256)
+SCALAR_PIECES = 3
 VECTOR_PIECES = 2
 DEFER = 2
 GPSIMD_FROM = 3
@@ -345,7 +345,8 @@ def tile_list_bike_route_rebalance_kernel(
         move_pages(0, (2,), banks[6], nc.scalar.copy)
         move_pages(0, (3,), banks[7], nc.scalar.copy)
 
-        rooms = [held([P, BANK], F32, f"room{x}") for x in range(3)]
+        whole_rooms = [held([P, BANK], F32, f"room{x}") for x in range(2)]
+        rooms = [[room[:, k * CHUNK : (k + 1) * CHUNK] for k in range(HALF)] for room in whole_rooms]
         new = {}
 
         def span(c, t):
@@ -382,7 +383,7 @@ def tile_list_bike_route_rebalance_kernel(
 
         def update_pair(c, t0, room, ahead=None, between=None):
             for k in range(HALF):
-                add_state(c, t0 + k, room[:, k * CHUNK : (k + 1) * CHUNK])
+                add_state(c, t0 + k, room[k])
             spent = [margin[c, t0 + 1] if c == 0 else None, None]
             if ahead is not None:
                 spent = next_chunk(ahead, f"move{c}{t0}")
@@ -413,7 +414,7 @@ def tile_list_bike_route_rebalance_kernel(
         squash(1, 0, 0)
         h_by_scalar(1, 0)
         h_by_scalar(1, 1)
-        spare = [f"dealt_{name}" for name in ("f00", "f10", "f01", "w0", "w1", "f11")]
+        spare = [f"dealt_{name}" for name in ("f00", "f10", "f01", "w0", "w1", "f11")] + ["raw_w1"]
 
         def late_tile(shape, width, name):
             tag = spare.pop(0)
@@ -422,6 +423,7 @@ def tile_list_bike_route_rebalance_kernel(
         out_rows = out_0.rearrange("(p t) m -> p t m", t=PACK)
         starts = [sum(PIECES[:q]) for q in range(len(PIECES))]
         paired = []
+        paired_words = []
         y_woven = [
             late_tile([P, width * PACK], width, f"y_woven{q}") for q, width in enumerate(PIECES)
         ]
@@ -444,43 +446,70 @@ def tile_list_bike_route_rebalance_kernel(
         update_pair(1, 0, rooms[1])
         update_pair(1, HALF, rooms[0], 2)
 
-        def update_turned(t, picked, turned):
-            nc.vector.tensor_copy(picked, pages[t][:].indirect(listed(*span(DEFER, t))))
-            for x in range(BANK // P):
-                cols = slice(x * P, (x + 1) * P)
-                for last, term in enumerate((move[DEFER, t][:, cols], picked[:, cols])):
-                    nc.tensor.matmul(turned[:, cols], term, ident[:], start=not last, stop=bool(last), is_transpose=True)
-            summed = stage.tile([P, BANK], F32, name=f"summed{t}", tag=("raw_f01", "raw_f00")[t % 2], align_bytes=64)
+        def pick(c, t, room):
+            nc.vector.tensor_copy(room, pages[t][:].indirect(listed(*span(c, t))))
+
+        def update_turned(name, steps, turned, tags):
+            for x, (moved, picked, block) in enumerate(steps):
+                for last, term in enumerate((moved, picked)):
+                    nc.tensor.matmul(
+                        turned[:, x * P : (x + 1) * P], term, ident[:], start=not last, stop=bool(last), is_transpose=True
+                    )
+            summed = stage.tile([P, BANK], F32, name=f"summed_{name}", tag=tags[0], align_bytes=64)
             nc.scalar.copy(summed[:], turned[:])
-            clipped = stage.tile([P, BANK], F32, name=f"clipped{t}", tag=("raw_w0", "raw_f10")[t % 2], align_bytes=64)
-            for x in range(BANK // P):
+            clipped = stage.tile([P, BANK], F32, name=f"clipped_{name}", tag=tags[1], align_bytes=64)
+            for x, (moved, picked, block) in enumerate(steps):
                 cols = slice(x * P, (x + 1) * P)
-                block = DEFER * CHUNK // P + x
                 nc.gpsimd.tensor_scalar(
                     clipped[:, cols], summed[:, cols], docks_rows[:, block : block + 1], LOWEST, ALU.min, ALU.max
                 )
-            for x in reversed(range(BANK // P)):
-                cols = slice(x * P, (x + 1) * P)
-                nc.tensor.transpose(banks[t][:, cols], clipped[:, cols], ident[:])
-            new[DEFER, t] = move[DEFER, t]
-            nc.scalar.copy(new[DEFER, t], banks[t][:])
+            return clipped
 
-        update_pair(2, 0, rooms[1], 3, lambda: update_turned(2, rooms[1][:], banks[5]))
-        update_turned(3, woven_of[3][:].bitcast(F32)[:, BANK : 2 * BANK], banks[6])
-        for tag, q0, q1 in (("raw_f10", 0, GPSIMD_FROM), ("raw_f00", GPSIMD_FROM, len(PIECES))):
-            whole = stage.tile([P, sum(PIECES[q0:q1]) * PACK], BF16, name=f"paired{q0}", tag=tag, align_bytes=64)
-            for q in range(q0, q1):
-                first = (starts[q] - starts[q0]) * PACK
-                paired.append(whole[:, first : first + PIECES[q] * PACK].rearrange("p (u m e) -> p u m e", u=HALF, e=2))
-        for t in range(HALF):
-            add_state(3, t, rooms[0][:, t * CHUNK : (t + 1) * CHUNK])
-        for t in range(HALF):
-            clip(3, t)
+        def turn_back(clipped, back):
+            for x in reversed(range(BANK // P)):
+                nc.tensor.transpose(back[:, x * P : (x + 1) * P], clipped[:, x * P : (x + 1) * P], ident[:])
+
+        def lay_out_pairs():
+            whole = stage.tile([P, T * PACK], BF16, name="paired", tag="raw_f10", align_bytes=64)
+            lead = starts[VECTOR_PIECES]
+            new[DEFER, PACK - 1] = whole[:, lead * HALF : lead * PACK].bitcast(F32)
+            for q, (first, width) in enumerate(zip(starts, PIECES)):
+                m0, m1 = (0, lead) if q < VECTOR_PIECES else (first, first + width)
+                block = whole[:, m0 * PACK : m1 * PACK]
+                cols = slice(first - m0, first - m0 + width)
+                paired.append(block.rearrange("p (u m e) -> p u m e", u=HALF, e=2)[:, :, cols, :])
+                paired_words.append(block.bitcast(U32).rearrange("p (u m) -> p m u", u=HALF)[:, cols, :])
+
+        def last_updates():
+            picked = stage.tile([P, HALF * BANK], F32, name="picked", tag="raw_w1", align_bytes=64)
+            for t in range(HALF, PACK):
+                pick(DEFER, t, picked[:, (t - HALF) * BANK : (t - HALF + 1) * BANK])
+            add_state(3, 0, rooms[0][0])
+            add_state(3, 1, stage.tile([P, CHUNK], F32, name="room_gate", tag="raw_w0", align_bytes=64)[:])
+            clip(3, 0)
+            clip(3, 1, rooms[0][1])
+            for t in range(HALF, PACK):
+                steps = [
+                    (move[DEFER, t][:, x * P : (x + 1) * P], picked[:, (t - HALF) * BANK + x * P :][:, 0:P], DEFER * CHUNK // P + x)
+                    for x in range(BANK // P)
+                ]
+                tags = (("raw_f01", "raw_w0"), ("raw_f00", "raw_f10"))[t % 2]
+                clipped = update_turned(t, steps, banks[3 + t], tags)
+                turn_back(clipped, banks[t])
+                if t == PACK - 1:
+                    lay_out_pairs()
+                else:
+                    new[DEFER, t] = move[DEFER, t]
+                nc.scalar.copy(new[DEFER, t], banks[t][:])
+
+        gate = stage.tile([P, CHUNK], F32, name="room_last", tag="raw_w1", align_bytes=64)
+        update_pair(2, 0, (gate[:], rooms[1][1]), 3, last_updates)
         for t in range(HALF):
             put(3, t)
             hand_out(t)
         for t in range(HALF, PACK):
             put(DEFER, t)
+        for t in range(HALF, PACK):
             hand_out(t)
 
         y_plane = held([P, T], U8, "y_plane")
@@ -492,7 +521,7 @@ def tile_list_bike_route_rebalance_kernel(
             copy = nc.scalar.copy if q >= len(PIECES) - SCALAR_PIECES else nc.vector.tensor_copy
             copy(
                 y_woven[q][:].bitcast(U32).rearrange("p (m u) -> p m u", u=HALF),
-                paired[q].rearrange("p u m e -> p (u m e)").bitcast(U32).rearrange("p (u m) -> p m u", u=HALF),
+                paired_words[q],
             )
 
         def store_scales(m0, m1, queues):
@@ -501,8 +530,8 @@ def tile_list_bike_route_rebalance_kernel(
 
         for q, width in enumerate(PIECES):
             if q % 2 == 0:
-                weave_words(q)
-                weave_words(q + 1)
+                for ahead in range(q, min(q + 2, len(PIECES))):
+                    weave_words(ahead)
             cols = slice(starts[q], starts[q] + width)
             nc.vector.quantize_mx(out=y_codes[:, cols].bitcast(FP8X4), scales=y_plane[:, cols], in_=y_woven[q][:])
             if cols.stop % BANK == 0:

@@ -25,14 +25,13 @@ PASSES = K // GROUP
 QUADS = 4
 BANK = 512
 CHUNK = 256
-CHUNKS = S // CHUNK
+WIDE = 2 * CHUNK
 STRIPE = 16
 RUN = 4
+KB = 1024
 PIECES = (256, 256, 512, 256, 256, 256, 256)
 SCALAR_PIECES = 3
-VECTOR_PIECES = 2
-DEFER = 2
-GPSIMD_FROM = 3
+SHARES = (((0, 0, 64, False), (1, 0, 64, True)), ((0, 0, 64, True), (1, 0, 64, False)))
 LOWEST = -3.4028234663852886e38
 ORDER = (((0, True), (0, False), (1, True), (1, False)), ((0, True), (1, True), (0, False), (1, False)))
 
@@ -43,12 +42,14 @@ def tile_list_bike_route_rebalance_kernel(
     nc = tc.nc
     with ExitStack() as ctx:
         keep = ctx.enter_context(tc.tile_pool(name="keep", bufs=1))
-        ring = ctx.enter_context(tc.tile_pool(name="ring", bufs=1))
+        work = ctx.enter_context(tc.tile_pool(name="work", bufs=1))
         psum = ctx.enter_context(tc.psum_pool(name="psum", bufs=1))
-        stage = ctx.enter_context(tc.tile_pool(name="stage", bufs=1))
 
         def held(shape, dtype, name):
             return keep.tile(shape, dtype, name=name, align_bytes=64)
+
+        def placed(kb, shape, dtype, name):
+            return work.tile(shape, dtype, name=name, align_bytes=64, offset=int(kb * KB))
 
         offsets = keep.tile([P, S // STRIPE], U16, name="offsets")
         tab_planes = held([P, T], U8, "tab_planes")
@@ -66,33 +67,15 @@ def tile_list_bike_route_rebalance_kernel(
         table = [held([P, T], I32, f"table{a}") for a in range(PASSES)]
         flow_raw = held([P, PASSES, K // 2], I32, "flow_raw")
         pages = [held([P, T], F32, f"page{t}") for t in range(PACK)]
-        raws = {}
+        v_plane = held([P, S], U8, "v_plane")
 
-        def load_planes(queue, tile, scales):
-            rows = scales.rearrange("a (q r) c -> r q a c", q=QUADS)
-            for r in range(4):
-                queue.dma_start(tile[r:P:32, :, :].bitcast(I32), rows[r].bitcast(I32))
-
-        def load_weight(name, w, a, b):
-            raw = stage.tile([P, PACK, GROUP], F32, name=f"raw_{name}", tag=f"raw_{name}", align_bytes=64)
-            rows = w[a * GROUP : (a + 1) * GROUP, b * GROUP : (b + 1) * GROUP]
-            nc.sync.dma_start(raw[:], rows.rearrange("(p i) c -> p i c", i=PACK))
-            raws[name] = raw
+        def load_rows(kb, name, w, a, c0, c1):
+            raw = placed(kb, [P, PACK, c1 - c0], F32, f"raw_{name}")
+            nc.sync.dma_start(raw[:], w[a * GROUP : (a + 1) * GROUP, c0:c1].rearrange("(p i) c -> p i c", i=PACK))
+            return raw
 
         def load_table(a):
             nc.sync.dma_start(table[a][:], tab_words[a].rearrange("p t i -> p (t i)").bitcast(I32))
-
-        v_plane = held([P, S], U8, "v_plane")
-        nc.scalar.dma_start(lines[0:PASSES, :], gain.rearrange("(b r) -> b r", b=PASSES))
-        nc.scalar.dma_start(lines[PASSES : PASSES + S // P, 0:P], docks.rearrange("(c p) -> c p", p=P))
-        nc.sync.dma_start(offsets[:], offs)
-        nc.sync.dma_start(flow_raw[:, 0, :], flow_words[0].bitcast(I32))
-        nc.sync.dma_start(tab_planes[0:P:4, :].bitcast(I32), tab_scales.rearrange("a q t -> (a q) t").bitcast(I32))
-        nc.sync.dma_start(flow_raw[:, 1, :], flow_words[1].bitcast(I32))
-        load_table(0)
-        load_planes(nc.sync, flow_plane_raw, flow_scales)
-        load_weight("f00", flowT, 0, 0)
-        nc.vector.tensor_copy(v_plane[:], tab_planes[:].indirect(offsets[:]))
 
         def place_planes(a):
             for q in range(QUADS):
@@ -101,19 +84,27 @@ def tile_list_bike_route_rebalance_kernel(
                     v_planes[32 * q : 32 * q + 4, a, :].bitcast(I32), v_plane[first : first + 16 : 4, :].bitcast(I32)
                 )
 
+        nc.scalar.dma_start(lines[0:PASSES, :], gain.rearrange("(b r) -> b r", b=PASSES))
+        nc.scalar.dma_start(lines[PASSES : PASSES + S // P, 0:P], docks.rearrange("(c p) -> c p", p=P))
+        nc.sync.dma_start(offsets[:], offs)
+        nc.sync.dma_start(flow_raw[:, 0, :], flow_words[0].bitcast(I32))
+        nc.sync.dma_start(tab_planes[0:P:4, :].bitcast(I32), tab_scales.rearrange("a q t -> (a q) t").bitcast(I32))
+        nc.sync.dma_start(flow_raw[:, 1, :], flow_words[1].bitcast(I32))
+        load_table(0)
+        scale_rows_in = flow_scales.rearrange("a (q r) c -> r q a c", q=QUADS)
+        for r in range(4):
+            nc.sync.dma_start(flow_plane_raw[r:P:32, :, :].bitcast(I32), scale_rows_in[r].bitcast(I32))
+        raw_f00 = load_rows(0, "f00", flowT, 0, 0, GROUP)
+        nc.vector.tensor_copy(v_plane[:], tab_planes[:].indirect(offsets[:]))
         place_planes(0)
-        load_weight("f10", flowT, 1, 0)
+        raw_f10 = load_rows(8, "f10", flowT, 1, 0, GROUP)
         place_planes(1)
         load_table(1)
-        for a in range(PASSES):
-            name = f"f{a}1"
-            raws[name] = stage.tile([P, 2, PACK, GROUP // 2], F32, name=f"raw_{name}", tag=f"raw_{name}", align_bytes=64)
-            for half in range(2):
-                cols = slice(GROUP + half * GROUP // 2, GROUP + (half + 1) * GROUP // 2)
-                rows = flowT[a * GROUP : (a + 1) * GROUP, cols]
-                nc.sync.dma_start(raws[name][:, half, :, :], rows.rearrange("(p i) c -> p i c", i=PACK))
-        load_weight("w0", wm, 0, 0)
-        load_weight("w1", wm, 1, 0)
+        raw_late = [
+            [load_rows(16 + 8 * a + 4 * x, f"f{a}1{x}", flowT, a, GROUP + x * GROUP // 2, GROUP + (x + 1) * GROUP // 2) for x in range(2)]
+            for a in range(PASSES)
+        ]
+        raw_w = [load_rows(32 + 8 * b, f"w{b}", wm, b, 0, N) for b in range(PASSES)]
         gT_rows = gT.rearrange("(p t) m -> p t m", t=PACK)
         for t in range(PACK):
             nc.sync.dma_start(pages[t][:], gT_rows[:, t, :])
@@ -135,177 +126,159 @@ def tile_list_bike_route_rebalance_kernel(
             nc.scalar.copy(limit[:, half * BANK : (half + 1) * BANK], banks[6 + half][:])
 
         quantised = {}
-        dealt_of = {}
 
-        def cast_weight(name, half, sign, on_vector, dealt=None):
-            src = raws[name][:].rearrange("p i (m t) -> p m i t", t=PACK)[:, :, :, half * HALF : (half + 1) * HALF]
-            if dealt is None:
-                if name not in dealt_of:
-                    dealt_of[name] = stage.tile(
-                        [P, PACK * GROUP], BF16, name=f"dealt_{name}", tag=f"dealt_{name}", align_bytes=64
-                    )
-                dealt = dealt_of[name][:, half * HALF * GROUP : (half + 1) * HALF * GROUP]
-            dealt_of[name, half] = dealt
-            dst = dealt.rearrange("p (t m i) -> p m i t", t=HALF, i=PACK)
+        def scaled_copy(on_vector, dst, src, sign):
             if on_vector:
                 nc.vector.tensor_scalar(dst, src, sign, None, ALU.mult)
             else:
                 nc.scalar.activation(dst, src, ACT.Copy, scale=sign)
 
-        def quantise_weight(name, t0, t1, dealt, codes=None):
-            if codes is None:
-                codes = held([P, (t1 - t0) * P], U32, f"{name}_codes{t0}")[:]
+        def cast_slots(raw, u, dealt, sign, on_vector):
+            src = raw[:].rearrange("p i (m t) -> p m i t", t=PACK)[:, :, :, u * HALF : (u + 1) * HALF]
+            scaled_copy(on_vector, dealt.rearrange("p (t m i) -> p m i t", t=HALF, i=PACK), src, sign)
+
+        def quantise_weight(name, t0, t1, dealt, kb=None):
+            shape = [P, (t1 - t0) * P]
+            codes = held(shape, U32, f"{name}_codes{t0}") if kb is None else placed(kb, shape, U32, f"{name}_codes{t0}")
             plane = held([P, (t1 - t0) * P], U8, f"{name}_plane{t0}")
-            nc.vector.quantize_mx(out=codes.bitcast(FP8X4), scales=plane[:], in_=dealt)
+            nc.vector.quantize_mx(out=codes[:].bitcast(FP8X4), scales=plane[:], in_=dealt)
             for t in range(t0, t1):
                 cols = slice((t - t0) * P, (t - t0 + 1) * P)
                 quantised[name, t] = (codes[:, cols].bitcast(FP8X4), plane[:, cols])
 
-        def quantise_half(name, half, codes=None):
-            quantise_weight(name, half * HALF, (half + 1) * HALF, dealt_of[name, half], codes)
-
-        def prepare_weight(name, sign, vector_halves):
-            for half in range(2):
-                cast_weight(name, half, sign, half in vector_halves)
-            quantise_weight(name, 0, PACK, dealt_of[name][:])
-
-        v_words = [held([P, S], U32, f"v_words{a}") for a in range(PASSES)]
+        v_words = {}
         flow_codes = held([P, PASSES * PASSES, PACK, 2 * P], U8, "flow_codes")
         flow_plane = held([P, PASSES * PASSES, PACK, P], U8, "flow_plane")
 
         def listed(j0, j1):
             return offsets[:, j0 // STRIPE : j1 // STRIPE]
 
-        def gather_words(a, j0, j1):
-            nc.vector.tensor_copy(v_words[a][:, j0:j1], table[a][:].bitcast(U32).indirect(listed(j0, j1)))
+        def gather_words(a, j0, j1, kb=None):
+            shape = [P, j1 - j0]
+            words = held(shape, U32, f"v_words{a}_{j0}") if kb is None else placed(kb, shape, U32, f"v_words{a}_{j0}")
+            nc.vector.tensor_copy(words[:], table[a][:].bitcast(U32).indirect(listed(j0, j1)))
+            for j in range(j0, j1, CHUNK):
+                v_words[a, j // CHUNK] = words[:, j - j0 : j - j0 + CHUNK]
 
-        def imbalance(bank, b, ranges):
-            steps = []
-            for a, packed in ORDER[b]:
-                if True:
-                    col = 0
-                    for t, j0, width in ranges:
-                        step = P if packed else width
-                        steps.extend((a, packed, t, j0 + d, col + d, step) for d in range(0, width, step))
-                        col += width
-            for n, (a, packed, t, j0, col, width) in enumerate(steps):
+        def imbalance(bank, b, slots, j0, width):
+            steps = [(a, packed, t) for a, packed in ORDER[b] for t in slots]
+            for n, (a, packed, t) in enumerate(steps):
                 if packed:
                     lhs = flow_codes[:, a * PASSES + b, t, :].bitcast(FP4X4)
                     lhs_plane = flow_plane[:, a * PASSES + b, t, :]
-                    rhs_plane = v_planes[:, a, j0 : j0 + width]
                 else:
                     lhs, lhs_plane = quantised[f"f{a}{b}", t]
-                    rhs_plane = v_planes[:, a, j0 : j0 + width]
+                col = (t - slots[0]) * width
                 nc.tensor.matmul_mx(
                     out=bank[:, col : col + width],
                     lhsT=lhs,
                     lhsT_scale=lhs_plane,
-                    rhs=v_words[a][:, j0 : j0 + width].bitcast(FP8X4),
-                    rhs_scale=rhs_plane,
+                    rhs=v_words[a, j0 // CHUNK][:, j0 % CHUNK : j0 % CHUNK + width].bitcast(FP8X4),
+                    rhs_scale=v_planes[:, a, j0 : j0 + width],
                     start=(n == 0),
                     stop=(n == len(steps) - 1),
                 )
 
-        h_q = {}
-        woven_of = {}
+        h_codes = [held([P, S], U32, f"h_codes{b}") for b in range(PASSES)]
+        h_plane = [held([P, S], U8, f"h_plane{b}") for b in range(PASSES)]
 
-        def quantise_h(woven, c, b0, b1, codes):
-            plane = held([P, (b1 - b0) * CHUNK], U8, f"h_plane{c}{b0}")
-            nc.vector.quantize_mx(out=codes.bitcast(FP8X4), scales=plane[:], in_=woven)
-            for b in range(b0, b1):
-                cols = slice((b - b0) * CHUNK, (b - b0 + 1) * CHUNK)
-                h_q[c, b] = (codes[:, cols], plane[:, cols])
+        def quantise_h(b, j0, j1, woven, codes=None):
+            if codes is None:
+                codes = h_codes[b][:, j0:j1]
+            nc.vector.quantize_mx(out=codes.bitcast(FP8X4), scales=h_plane[b][:, j0:j1], in_=woven)
 
-        def h_by_vector(c, b, pair, woven, spent):
+        def h_by_vector(b, pair, kb_bounded, kb_woven, codes):
+            woven = placed(kb_woven, [P, CHUNK * PACK], BF16, f"woven0{b}")
             for s in range(CHUNK // P):
-                imbalance(pair[s], b, [(t, c * CHUNK + s * P, P) for t in range(PACK)])
-                bounded = spent[:, s, :].rearrange("p (j t) -> p j t", t=PACK)
-                nc.scalar.activation(bounded, pair[s][:].rearrange("p (t j) -> p j t", t=PACK), ACT.Tanh)
+                imbalance(pair[s], b, range(PACK), s * P, P)
+                bounded = placed(kb_bounded[s], [P, P, PACK], F32, f"bounded0{b}{s}")
+                nc.scalar.activation(bounded[:], pair[s][:].rearrange("p (t j) -> p j t", t=PACK), ACT.Tanh)
                 nc.vector.tensor_tensor(
                     woven[:, s * BANK : (s + 1) * BANK].rearrange("p (j t) -> p j t", t=PACK),
-                    bounded,
+                    bounded[:],
                     gain_sb[:, b : b + 1, :].to_broadcast([P, P, PACK]),
                     ALU.mult,
                 )
-            quantise_h(woven, c, b, b + 1, held([P, CHUNK], U32, f"h_codes{c}{b}")[:])
+            quantise_h(b, 0, CHUNK, woven[:], codes)
 
-        squashed = raws["f11"][:, 0, :, :].rearrange("p (u i) c -> p u (i c)", u=2)
-        rounded = [held([P, PACK, CHUNK], BF16, f"rounded{b}") for b in range(PASSES)]
+        def products(c, b, pair):
+            for u in range(HALF):
+                imbalance(pair[u], b, range(u * HALF, (u + 1) * HALF), c * CHUNK, CHUNK)
 
-        def squash(c, b, s):
-            imbalance(pairs[c, b][s], b, [(t, c * CHUNK, CHUNK) for t in range(s * HALF, (s + 1) * HALF)])
-            nc.scalar.activation(squashed[:, s if (c, b) == (1, 0) else 1 - s, :], pairs[c, b][s][:], ACT.Tanh)
-
-        def rounded_of(c, b):
-            if (c, b) == (1, 0):
-                return dealt_w0[:, part : 2 * part].rearrange("p (t j) -> p t j", t=PACK)
-            return rounded[b][:]
-
-        def weigh(c, b, s):
-            for t in range(s * HALF, (s + 1) * HALF):
-                col = (t - s * HALF) * CHUNK
+        def squash_slots(c, pair, kb):
+            bounded = placed(kb, [P, PACK, CHUNK], F32, f"bounded{c}0")
+            for u in range(HALF):
                 nc.scalar.activation(
-                    rounded_of(c, b)[:, t, :], squashed[:, s if (c, b) == (1, 0) else 1 - s, :][:, col : col + CHUNK], ACT.Copy, scale=gain_sb[:, b, t : t + 1]
+                    bounded[:, u * HALF : (u + 1) * HALF, :].rearrange("p t j -> p (t j)"), pair[u][:], ACT.Tanh
+                )
+            return bounded
+
+        def weigh_on_scalar(c, bounded, kb_rounded, kb_woven):
+            rounded = placed(kb_rounded, [P, PACK, CHUNK], BF16, f"rounded{c}0")
+            woven = placed(kb_woven, [P, CHUNK * PACK], BF16, f"woven{c}0")
+            for t in range(PACK):
+                nc.scalar.activation(rounded[:, t, :], bounded[:, t, :], ACT.Copy, scale=gain_sb[:, 0, t : t + 1])
+            for s in range(CHUNK // P):
+                nc.scalar.copy(
+                    woven[:, s * BANK : (s + 1) * BANK].rearrange("p (c i t) -> p c t i", i=RUN, t=PACK),
+                    rounded[:, :, s * P : (s + 1) * P].rearrange("p t (c i) -> p c t i", i=RUN),
+                )
+            return woven
+
+        def squash_pairs(c, pair, kb):
+            bounded = placed(kb, [P, HALF, CHUNK * HALF], F32, f"bounded{c}1")
+            for u in range(HALF):
+                nc.scalar.activation(
+                    bounded[:, u, :].rearrange("p (j e) -> p j e", e=HALF),
+                    pair[u][:].rearrange("p (e j) -> p j e", e=HALF),
+                    ACT.Tanh,
+                )
+            return bounded
+
+        def weigh_on_gpsimd(bounded, j0, j1, kb, name):
+            woven = placed(kb, [P, (j1 - j0) * PACK], BF16, name)
+            nc.gpsimd.tensor_tensor(
+                woven[:].rearrange("p (j u e) -> p j u e", u=HALF, e=HALF),
+                bounded[:].rearrange("p u (j e) -> p j u e", e=HALF)[:, j0:j1],
+                gain_sb[:, 1:2, :].rearrange("p o (u e) -> p o u e", e=HALF).to_broadcast([P, j1 - j0, HALF, HALF]),
+                ALU.mult,
+            )
+            return woven
+
+        def move_product(out, t, j0, j1, elsewhere=None):
+            for b in range(PASSES):
+                codes = h_codes[b][:, j0:j1] if elsewhere is None else elsewhere[b]
+                nc.tensor.matmul_mx(
+                    out=out,
+                    lhsT=quantised[f"w{b}", t][0],
+                    lhsT_scale=quantised[f"w{b}", t][1],
+                    rhs=codes.bitcast(FP8X4),
+                    rhs_scale=h_plane[b][:, j0:j1],
+                    start=(b == 0),
+                    stop=(b == PASSES - 1),
                 )
 
-        def weave(c, b):
-            if b == 0:
-                woven_of[c] = ring.tile([P, PASSES * CHUNK * PACK], BF16, name="woven", tag="woven", bufs=2, align_bytes=64)
-            nc.scalar.copy(
-                woven_of[c][:, b * CHUNK * PACK : (b + 1) * CHUNK * PACK].rearrange("p (c i t) -> p c t i", i=RUN, t=PACK),
-                rounded_of(c, b).rearrange("p t (c i) -> p c t i", i=RUN),
-            )
+        def moved_alone(t, j0, j1, bank, kb, elsewhere=None):
+            move_product(bank[:, 0 : j1 - j0], t, j0, j1, elsewhere)
+            moved = placed(kb, [P, j1 - j0], F32, f"moved{j0}_{t}")
+            nc.scalar.copy(moved[:], bank[:, 0 : j1 - j0])
+            return moved
 
-        def h_by_scalar(c, b, midway=None):
-            squash(c, b, 1)
-            weigh(c, b, 0)
-            if midway is not None:
-                midway()
-            weigh(c, b, 1)
-            if (c, b) != (CHUNKS - 1, PASSES - 1):
-                squash(c + b, 1 - b, 0)
-            weave(c, b)
+        def add_state(t, j0, j1, moved, kb):
+            summed = placed(kb, [P, j1 - j0], F32, f"summed{j0}_{t}")
+            nc.vector.tensor_tensor(summed[:], pages[t][:].indirect(listed(j0, j1)), moved, ALU.add)
+            return summed
 
-        move = {}
-        margin = {}
+        def clip(t, j0, j1, summed, kb=None):
+            new = summed if kb is None else placed(kb, [P, j1 - j0], F32, f"new{j0}_{t}")
+            nc.vector.tensor_tensor(new[:], summed[:], limit[:, j0:j1], ALU.min)
+            return new
 
-        def move_pages(c, ts, tile, copy, apart=False):
-            bank = tile[:, 0 : len(ts) * CHUNK].rearrange("p (t j) -> p t j", j=CHUNK)
-            for t in ts:
-                for b in range(PASSES):
-                    nc.tensor.matmul_mx(
-                        out=bank[:, t - ts[0], :],
-                        lhsT=quantised[f"w{b}", t][0],
-                        lhsT_scale=quantised[f"w{b}", t][1],
-                        rhs=h_q[c, b][0].bitcast(FP8X4),
-                        rhs_scale=h_q[c, b][1],
-                        start=(b == 0),
-                        stop=(b == PASSES - 1),
-                    )
-            for group in [(t,) for t in ts] if apart else [ts]:
-                moved = ring.tile([P, len(group) * CHUNK + P], F32, name="move", tag=f"move{c}{group[0]}", align_bytes=64)
-                copy(moved[:, P:].rearrange("p (t j) -> p t j", j=CHUNK), bank[:, group[0] - ts[0] : group[-1] - ts[0] + 1, :])
-                margin[c, group[0]] = moved[:, 0:CHUNK]
-                for t in group:
-                    move[c, t] = moved[:, P + (t - group[0]) * CHUNK : P + (t - group[0] + 1) * CHUNK]
-
-        def move_wide(t, tile):
-            for c in range(DEFER, CHUNKS):
-                for b in range(PASSES):
-                    nc.tensor.matmul_mx(
-                        out=tile[:, (c - DEFER) * CHUNK : (c - DEFER + 1) * CHUNK],
-                        lhsT=quantised[f"w{b}", t][0],
-                        lhsT_scale=quantised[f"w{b}", t][1],
-                        rhs=h_q[c, b][0].bitcast(FP8X4),
-                        rhs_scale=h_q[c, b][1],
-                        start=(b == 0),
-                        stop=(b == PASSES - 1),
-                    )
-            move[DEFER, t] = held([P, BANK], F32, f"move_wide{t}")[:]
-            nc.scalar.copy(move[DEFER, t], tile[:])
+        def put(t, j0, j1, new):
+            nc.vector.tensor_copy(pages[t][:].indirect(listed(j0, j1)), new)
 
         for a in range(PASSES):
-            nc.vector.tensor_copy(
+            nc.scalar.copy(
                 flow_codes[:, a * PASSES : (a + 1) * PASSES].bitcast(U16).rearrange("p g t m -> p g m t"),
                 flow_raw[:, a, :].bitcast(U16).rearrange("p (b m t) -> p b m t", m=P, t=PACK),
             )
@@ -314,201 +287,170 @@ def tile_list_bike_route_rebalance_kernel(
             flow_plane[:].rearrange("p g t m -> p g m t"),
             flow_plane_raw[:].rearrange("p a (b m t) -> p (a b) m t", m=P, t=PACK),
         )
-        prepare_weight("f00", -1.0, ())
-        prepare_weight("f10", -1.0, (1,))
-        gather_words(1, 0, CHUNK)
-        gather_words(1, CHUNK, S)
-        for name in ("f01", "f11"):
-            dealt = stage.tile([P, PACK * GROUP], BF16, name=f"dealt_{name}", tag=f"dealt_{name}", align_bytes=64)
-            for half in range(2):
-                src = raws[name][:, half, :, :].rearrange("p i (m t) -> p m i t", t=PACK)
-                dst = dealt[:].rearrange("p (t m i) -> p m i t", t=PACK, i=PACK)[:, half * P // 2 : (half + 1) * P // 2]
-                if half == 0:
-                    nc.scalar.activation(dst, src, ACT.Copy, scale=-1.0)
-                else:
-                    nc.vector.tensor_scalar(dst, src, -1.0, None, ALU.mult)
-            quantise_weight(name, 0, PACK, dealt[:])
-        h_by_vector(0, 0, banks[0:2], raws["f01"][:, 1, 0:HALF, :].rearrange("p i c -> p (i c)").bitcast(BF16), raws["f01"][:, 0, :, :].rearrange("p (u i) c -> p u (i c)", u=2))
         part = HALF * GROUP
-        dealt_w0 = stage.tile([P, 2 * part + part // 2], BF16, name="dealt_w0", tag="dealt_w0", align_bytes=64)
-        for half in range(2):
-            cast_weight("w0", half, 1.0, True, dealt_w0[:, half * (part + part // 2) :][:, 0:part])
-        for half in range(2):
-            quantise_half("w0", half)
-        h_by_vector(0, 1, banks[2:4], dealt_of["w0", 0], held([P, CHUNK // P, BANK], F32, "bounded"))
-        cast_weight("w1", 0, 1.0, True)
-        quantise_half("w1", 0)
-        move_pages(0, (0,), banks[0], nc.vector.tensor_copy)
-        move_pages(0, (1,), banks[1], nc.vector.tensor_copy)
-        cast_weight("w1", 1, 1.0, True)
-        quantise_half("w1", 1)
-        move_pages(0, (2,), banks[6], nc.scalar.copy)
-        move_pages(0, (3,), banks[7], nc.scalar.copy)
+        for a, raw in enumerate((raw_f00, raw_f10)):
+            dealt = placed(48 + 4 * a, [P, PACK * GROUP], BF16, f"dealt_f{a}0")
+            for u in range(HALF):
+                cast_slots(raw, u, dealt[:, u * part : (u + 1) * part], -1.0, u == 1)
+            if a == 1:
+                gather_words(1, 0, CHUNK)
+            quantise_weight(f"f{a}0", 0, PACK, dealt[:])
+        gather_words(1, CHUNK, WIDE)
+        for a in range(PASSES):
+            dealt = placed(56 + 4 * a, [P, PACK * GROUP], BF16, f"dealt_f{a}1")
+            dst = dealt[:].rearrange("p (t m i) -> p m i t", t=PACK, i=PACK)
+            for x, m0, m1, on_vector in SHARES[a]:
+                src = raw_late[a][x][:].rearrange("p i (m t) -> p m i t", t=PACK)
+                scaled_copy(on_vector, dst[:, x * P // 2 + m0 : x * P // 2 + m1], src[:, m0:m1], -1.0)
+            quantise_weight(f"f{a}1", 0, PACK, dealt[:])
+        codes0 = [placed(63, [P, CHUNK], U32, "codes00")[:], h_codes[1][:, 0:CHUNK]]
+        h_by_vector(0, banks[0:2], (0, 2), 48, codes0[0])
+        dealt_w = {(b, u): placed(kb, [P, part], BF16, f"dealt_w{b}{u}") for b, u, kb in ((0, 0, 64), (1, 0, 5))}
+        cast_slots(raw_w[0], 0, dealt_w[0, 0][:], 1.0, True)
+        quantise_weight("w0", 0, HALF, dealt_w[0, 0][:])
+        h_by_vector(1, banks[2:4], (4, 66), 50, codes0[1])
+        cast_slots(raw_w[1], 0, dealt_w[1, 0][:], 1.0, True)
+        quantise_weight("w1", 0, HALF, dealt_w[1, 0][:])
+        products(1, 0, banks[4:6])
+        products(1, 1, banks[0:2])
 
-        whole_rooms = [held([P, BANK], F32, f"room{x}") for x in range(2)]
-        rooms = [[room[:, k * CHUNK : (k + 1) * CHUNK] for k in range(HALF)] for room in whole_rooms]
-        new = {}
+        def moved_in_parts(t, bank, kbs):
+            move_product(bank[:, 0:CHUNK], t, 0, CHUNK, codes0)
+            parts = [placed(kb, [P, P], F32, f"moved0_{t}_{s}") for s, kb in enumerate(kbs)]
+            for s, piece in enumerate(parts):
+                nc.scalar.copy(piece[:], bank[:, s * P : (s + 1) * P])
+            return parts
 
-        def span(c, t):
-            return (c * CHUNK, S if c == DEFER and t >= HALF else (c + 1) * CHUNK)
+        def add_state_in_parts(t, parts, kb):
+            summed = placed(kb, [P, CHUNK], F32, f"summed0_{t}")
+            for s, piece in enumerate(parts):
+                picks = pages[t][:].indirect(listed(s * P, (s + 1) * P))
+                nc.vector.tensor_tensor(summed[:, s * P : (s + 1) * P], picks, piece[:], ALU.add)
+            return summed
 
-        def add_state(c, t, room):
-            new[c, t] = room
-            j0, j1 = span(c, t)
-            width = P if c == 0 and t % HALF else j1 - j0
-            for d in range(0, j1 - j0, width):
-                picked = pages[t][:].indirect(listed(j0 + d, j0 + d + width))
-                nc.vector.tensor_tensor(room[:, d : d + width], picked, move[c, t][:, d : d + width], ALU.add)
+        def moved_pair(u, bank, kb, codes):
+            for k in range(HALF):
+                move_product(bank[:, k * CHUNK : (k + 1) * CHUNK], u * HALF + k, CHUNK, WIDE, codes)
+            both = placed(kb, [P, HALF, CHUNK], F32, f"moved1_{u}")
+            nc.scalar.copy(both[:].rearrange("p k j -> p (k j)"), bank[:])
+            return [both[:, k, :] for k in range(HALF)]
 
-        def clip(c, t, room=None):
-            j0, j1 = span(c, t)
-            summed = new[c, t]
-            new[c, t] = summed if room is None else room
-            nc.vector.tensor_tensor(new[c, t], summed, limit[:, j0:j1], ALU.min)
+        def clips_of(u, j0, sums, kbs):
+            return [clip(u * HALF + k, j0, j0 + CHUNK, sums[k], kbs[k]) for k in range(HALF)]
 
-        def put(c, t):
-            nc.vector.tensor_copy(pages[t][:].indirect(listed(*span(c, t))), new[c, t])
+        def puts_of(u, j0, news):
+            for k in range(HALF):
+                put(u * HALF + k, j0, j0 + CHUNK, news[k][:])
 
-        def next_chunk(c, tag):
-            codes = ring.tile([P, PASSES * CHUNK], U32, name="h_codes", tag=tag, align_bytes=64)
-            plane = held([P, PASSES * CHUNK], U8, f"h_plane{c}")
-            for m0, m1 in ((0, PASSES * CHUNK),) if c == 1 else ((CHUNK, 2 * CHUNK), (0, CHUNK)):
-                nc.vector.quantize_mx(
-                    out=codes[:, m0:m1].bitcast(FP8X4), scales=plane[:, m0:m1], in_=woven_of[c][:, m0 * PACK : m1 * PACK]
+        moved0 = moved_alone(0, 0, CHUNK, banks[6], 73, codes0)
+        moved1 = moved_in_parts(1, banks[7], (70, 74))
+        bounded11 = squash_pairs(1, banks[0:2], 12)
+        for b, kb in enumerate((3, 68)):
+            dealt_w[b, 1] = placed(kb, [P, part], BF16, f"dealt_w{b}1")
+            cast_slots(raw_w[b], 1, dealt_w[b, 1][:], 1.0, False)
+        bounded10 = squash_slots(1, banks[4:6], 28)
+        gather_words(1, WIDE, S, 6.5)
+        for b in range(PASSES):
+            quantise_weight(f"w{b}", HALF, PACK, dealt_w[b, 1][:], (5, 50)[b])
+
+        sums = [add_state(0, 0, CHUNK, moved0[:], 75), add_state_in_parts(1, moved1, 76)]
+        news = clips_of(0, 0, sums, (69.5, 79))
+        woven11 = weigh_on_gpsimd(bounded11, 0, CHUNK, 75, "woven11")
+        puts_of(0, 0, news)
+        woven10 = weigh_on_scalar(1, bounded10, 73, 77)
+        moved2 = moved_alone(2, 0, CHUNK, banks[4], 80, codes0)
+        moved3 = moved_in_parts(3, banks[5], (96, 81))
+        products(2, 1, banks[6:8])
+        bounded21 = squash_pairs(2, banks[6:8], 30)
+
+        codes1 = [placed(79, [P, CHUNK], U32, "codes10")[:], h_codes[1][:, CHUNK:WIDE]]
+        quantise_h(1, CHUNK, WIDE, woven11[:])
+        quantise_h(0, CHUNK, WIDE, woven10[:], codes1[0])
+        sums = [add_state(2, 0, CHUNK, moved2[:], 76), add_state_in_parts(3, moved3, 77)]
+        news = clips_of(1, 0, sums, (96, 97))
+        woven21 = weigh_on_gpsimd(bounded21, 0, CHUNK, 76, "woven21")
+        puts_of(1, 0, news)
+        moved = moved_pair(0, banks[2], 84, codes1) + moved_pair(1, banks[3], 86, codes1)
+        products(3, 1, banks[0:2])
+        bounded31 = squash_pairs(3, banks[0:2], 8.5)
+        products(2, 0, banks[4:6])
+        woven20 = weigh_on_scalar(2, squash_slots(2, banks[4:6], 26), 56, 92)
+        products(3, 0, banks[6:8])
+        woven30 = weigh_on_scalar(3, squash_slots(3, banks[6:8], 20), 60, 94)
+
+        quantise_h(1, WIDE, WIDE + CHUNK, woven21[:])
+        sums = [add_state(k, CHUNK, WIDE, moved[k], 96 + k) for k in range(HALF)]
+        news = clips_of(0, CHUNK, sums, (76, 77))
+        woven31 = weigh_on_gpsimd(bounded31, 0, CHUNK, 96, "woven31")
+        puts_of(0, CHUNK, news)
+
+        wide0 = placed(77, [P, WIDE], U32, "wide0")
+        quantise_h(0, WIDE, WIDE + CHUNK, woven20[:], wide0[:, 0:CHUNK])
+        quantise_h(0, WIDE + CHUNK, S, woven30[:], wide0[:, CHUNK:WIDE])
+        quantise_h(1, WIDE + CHUNK, S, woven31[:])
+        wide = [wide0[:], h_codes[1][:, WIDE:S]]
+        sums = [add_state(HALF + k, CHUNK, WIDE, moved[HALF + k], (93.5, 95.5)[k]) for k in range(HALF)]
+        news1 = clips_of(1, CHUNK, sums, (82, 83))
+        moved = [moved_alone(t, WIDE, S, banks[(2, 3, 0, 1)[t]], 32 + 2 * t, wide) for t in range(PACK)]
+        picked = [placed(kb, [P, WIDE], F32, f"picked{t}") for t, kb in enumerate((92, 94, 96, 86))]
+        for t in range(PACK):
+            nc.vector.tensor_copy(picked[t][:], pages[t][:].indirect(listed(WIDE, S)))
+        puts_of(1, CHUNK, news1)
+
+        news = []
+        for t, kb_summed, kb_clipped, kb_back in ((0, 0, 44, 56), (1, 8, 46, 58), (2, 10, 40, 60), (3, 98, 15, None)):
+            turned, returned = banks[4 + t % HALF], banks[6 + t % HALF]
+            for x in range(WIDE // P):
+                cols = slice(x * P, (x + 1) * P)
+                for last, term in enumerate((moved[t], picked[t])):
+                    nc.tensor.matmul(turned[:, cols], term[:, cols], ident[:], start=not last, stop=bool(last), is_transpose=True)
+            summed = placed(kb_summed, [P, WIDE], F32, f"summed_turned{t}")
+            nc.scalar.copy(summed[:], turned[:])
+            clipped = placed(kb_clipped, [P, WIDE], F32, f"clipped{t}")
+            for x in range(WIDE // P):
+                cols = slice(x * P, (x + 1) * P)
+                block = WIDE // P + x
+                nc.gpsimd.tensor_scalar(
+                    clipped[:, cols], summed[:, cols], docks_rows[:, block : block + 1], LOWEST, ALU.min, ALU.max
                 )
-            for b in range(PASSES):
-                h_q[c, b] = (codes[:, b * CHUNK : (b + 1) * CHUNK], plane[:, b * CHUNK : (b + 1) * CHUNK])
-            after_quantise(c)
-            return [woven_of[c][:].bitcast(F32)[:, (HALF + k) * CHUNK : (HALF + k + 1) * CHUNK] for k in range(HALF)]
-
-        def update_pair(c, t0, room, ahead=None, between=None):
-            for k in range(HALF):
-                add_state(c, t0 + k, room[k])
-            spent = [margin[c, t0 + 1] if c == 0 else None, None]
-            if ahead is not None:
-                spent = next_chunk(ahead, f"move{c}{t0}")
-            for k in range(HALF):
-                clip(c, t0 + k, spent[k])
-            if between is not None:
-                between()
-            for k in range(HALF):
-                put(c, t0 + k)
-
-        def after_quantise(c):
-            if c + 1 < CHUNKS:
-                h_by_scalar(c + 1, 0)
-            if c < DEFER:
-                move_pages(c, (0, 1), banks[4], nc.scalar.copy)
-                move_pages(c, (2, 3), banks[5], nc.scalar.copy, True)
-                h_by_scalar(c + 1, 1)
-            elif c + 1 < CHUNKS:
-                h_by_scalar(c + 1, 1, lambda: move_pages(c, (0, 1), banks[4], nc.scalar.copy, True))
-            else:
-                move_pages(c, (0, 1), banks[4], nc.scalar.copy)
-                for t in range(HALF, PACK):
-                    move_wide(t, banks[t])
-
-        pairs = {(c, b): [banks[x] for x in ((1, 6), (7, 0))[b]] for c in range(2, CHUNKS) for b in range(PASSES)}
-        pairs[1, 0] = banks[4:6]
-        pairs[1, 1] = [banks[2], banks[0]]
-        squash(1, 0, 0)
-        h_by_scalar(1, 0)
-        h_by_scalar(1, 1)
-        spare = [f"dealt_{name}" for name in ("f00", "f10", "f01", "w0", "w1", "f11")] + ["raw_w1"]
-
-        def late_tile(shape, width, name):
-            tag = spare.pop(0)
-            return stage.tile(shape, BF16, name=name, tag=tag, align_bytes=64)
+            for x in range(WIDE // P):
+                cols = slice(x * P, (x + 1) * P)
+                nc.tensor.transpose(returned[:, cols], clipped[:, cols], ident[:])
+            if kb_back is not None:
+                back = placed(kb_back, [P, WIDE], F32, f"back{t}")
+                nc.scalar.copy(back[:], returned[:])
+                news.append(back)
+        blocks = [
+            placed(kb, [P, HALF, width * HALF], BF16, f"paired{kb}") for kb, width in ((12, BANK), (16, T - BANK))
+        ]
+        back3 = blocks[0][:, 1, :].bitcast(F32)
+        nc.scalar.copy(back3, banks[7][:])
 
         out_rows = out_0.rearrange("(p t) m -> p t m", t=PACK)
         starts = [sum(PIECES[:q]) for q in range(len(PIECES))]
-        paired = []
-        paired_words = []
-        y_woven = [
-            late_tile([P, width * PACK], width, f"y_woven{q}") for q, width in enumerate(PIECES)
-        ]
+
+        def block_of(q):
+            x = min(starts[q] // BANK, 1)
+            return x, slice(starts[q] - x * BANK, starts[q] - x * BANK + PIECES[q])
 
         def hand_out(t):
             nc.sync.dma_start(out_rows[:, t, :], pages[t][:])
             for q, width in enumerate(PIECES):
-                dst = paired[q][:, t // 2, :, t % 2]
+                x, cols = block_of(q)
+                dst = blocks[x][:, t // HALF, :].rearrange("p (m e) -> p m e", e=HALF)[:, cols, t % HALF]
                 src = pages[t][:, starts[q] : starts[q] + width]
-                if t < HALF and q >= GPSIMD_FROM:
+                if t < HALF and starts[q] >= T // 2:
                     nc.gpsimd.tensor_scalar(dst, src, 1.0, 1.0, ALU.mult, ALU.mult)
-                elif t >= HALF and q < VECTOR_PIECES:
+                elif t >= HALF and x == 0:
                     nc.vector.tensor_copy(dst, src)
                 else:
                     nc.scalar.copy(dst, src)
 
-        update_pair(0, 0, rooms[0])
-        next_chunk(1, "move01")
-        update_pair(0, HALF, rooms[1])
-        update_pair(1, 0, rooms[1])
-        update_pair(1, HALF, rooms[0], 2)
-
-        def pick(c, t, room):
-            nc.vector.tensor_copy(room, pages[t][:].indirect(listed(*span(c, t))))
-
-        def update_turned(name, steps, turned, tags):
-            for x, (moved, picked, block) in enumerate(steps):
-                for last, term in enumerate((moved, picked)):
-                    nc.tensor.matmul(
-                        turned[:, x * P : (x + 1) * P], term, ident[:], start=not last, stop=bool(last), is_transpose=True
-                    )
-            summed = stage.tile([P, BANK], F32, name=f"summed_{name}", tag=tags[0], align_bytes=64)
-            nc.scalar.copy(summed[:], turned[:])
-            clipped = stage.tile([P, BANK], F32, name=f"clipped_{name}", tag=tags[1], align_bytes=64)
-            for x, (moved, picked, block) in enumerate(steps):
-                cols = slice(x * P, (x + 1) * P)
-                nc.gpsimd.tensor_scalar(
-                    clipped[:, cols], summed[:, cols], docks_rows[:, block : block + 1], LOWEST, ALU.min, ALU.max
-                )
-            return clipped
-
-        def turn_back(clipped, back):
-            for x in reversed(range(BANK // P)):
-                nc.tensor.transpose(back[:, x * P : (x + 1) * P], clipped[:, x * P : (x + 1) * P], ident[:])
-
-        def lay_out_pairs():
-            whole = stage.tile([P, T * PACK], BF16, name="paired", tag="raw_f10", align_bytes=64)
-            lead = starts[VECTOR_PIECES]
-            new[DEFER, PACK - 1] = whole[:, lead * HALF : lead * PACK].bitcast(F32)
-            for q, (first, width) in enumerate(zip(starts, PIECES)):
-                m0, m1 = (0, lead) if q < VECTOR_PIECES else (first, first + width)
-                block = whole[:, m0 * PACK : m1 * PACK]
-                cols = slice(first - m0, first - m0 + width)
-                paired.append(block.rearrange("p (u m e) -> p u m e", u=HALF, e=2)[:, :, cols, :])
-                paired_words.append(block.bitcast(U32).rearrange("p (u m) -> p m u", u=HALF)[:, cols, :])
-
-        def last_updates():
-            picked = stage.tile([P, HALF * BANK], F32, name="picked", tag="raw_w1", align_bytes=64)
-            for t in range(HALF, PACK):
-                pick(DEFER, t, picked[:, (t - HALF) * BANK : (t - HALF + 1) * BANK])
-            add_state(3, 0, rooms[0][0])
-            add_state(3, 1, stage.tile([P, CHUNK], F32, name="room_gate", tag="raw_w0", align_bytes=64)[:])
-            clip(3, 0)
-            clip(3, 1, rooms[0][1])
-            for t in range(HALF, PACK):
-                steps = [
-                    (move[DEFER, t][:, x * P : (x + 1) * P], picked[:, (t - HALF) * BANK + x * P :][:, 0:P], DEFER * CHUNK // P + x)
-                    for x in range(BANK // P)
-                ]
-                tags = (("raw_f01", "raw_w0"), ("raw_f00", "raw_f10"))[t % 2]
-                clipped = update_turned(t, steps, banks[3 + t], tags)
-                turn_back(clipped, banks[t])
-                if t == PACK - 1:
-                    lay_out_pairs()
-                else:
-                    new[DEFER, t] = move[DEFER, t]
-                nc.scalar.copy(new[DEFER, t], banks[t][:])
-
-        gate = stage.tile([P, CHUNK], F32, name="room_last", tag="raw_w1", align_bytes=64)
-        update_pair(2, 0, (gate[:], rooms[1][1]), 3, last_updates)
         for t in range(HALF):
-            put(3, t)
+            put(t, WIDE, S, news[t][:])
             hand_out(t)
-        for t in range(HALF, PACK):
-            put(DEFER, t)
+        put(2, WIDE, S, news[2][:])
+        put(3, WIDE, S, back3)
         for t in range(HALF, PACK):
             hand_out(t)
 
@@ -516,17 +458,15 @@ def tile_list_bike_route_rebalance_kernel(
         y_codes = held([P, T], I32, "y_codes")
         words_out = out_1[0].rearrange("p m t -> p (m t)").bitcast(I32)
         scale_rows = out_2[0].rearrange("(q r) m -> r q m", q=QUADS)
+        y_woven = [placed(28 + starts[q] * 8 / KB, [P, width * PACK], BF16, f"y_woven{q}") for q, width in enumerate(PIECES)]
 
         def weave_words(q):
+            x, cols = block_of(q)
             copy = nc.scalar.copy if q >= len(PIECES) - SCALAR_PIECES else nc.vector.tensor_copy
             copy(
                 y_woven[q][:].bitcast(U32).rearrange("p (m u) -> p m u", u=HALF),
-                paired_words[q],
+                blocks[x][:].bitcast(U32).rearrange("p u m -> p m u")[:, cols, :],
             )
-
-        def store_scales(m0, m1, queues):
-            for r in range(4):
-                queues[r % 2].dma_start(scale_rows[r][:, m0:m1].bitcast(I32), y_plane[r:P:32, m0:m1].bitcast(I32))
 
         for q, width in enumerate(PIECES):
             if q % 2 == 0:
@@ -537,4 +477,6 @@ def tile_list_bike_route_rebalance_kernel(
             if cols.stop % BANK == 0:
                 done_cols = slice(cols.stop - BANK, cols.stop)
                 nc.sync.dma_start(words_out[:, done_cols], y_codes[:, done_cols])
-        store_scales(0, T, (nc.sync, nc.scalar))
+        for r in range(4):
+            queue = (nc.sync, nc.scalar)[r % 2]
+            queue.dma_start(scale_rows[r].bitcast(I32), y_plane[r:P:32, :].bitcast(I32))

@@ -116,14 +116,10 @@ def tile_list_bike_route_rebalance_kernel(
         nc.tensor.transpose(banks[5][:, 0:P], lines[:, 0:P], ident[:])
         nc.scalar.copy(docks_rows[:], banks[5][:, PASSES : PASSES + S // P])
         nc.scalar.copy(gain_sb[:], banks[4][:].rearrange("p (t r) -> p r t", t=PACK)[:, 0:PASSES, :])
-        limit = held([P, S], F32, "limit")
-        for half in range(S // BANK):
-            for c in range(PACK):
-                col = half * PACK + c
-                nc.tensor.transpose(
-                    banks[6 + half][:, c * P : (c + 1) * P], docks_rows[:, col : col + 1].to_broadcast([P, P]), ident[:]
-                )
-            nc.scalar.copy(limit[:, half * BANK : (half + 1) * BANK], banks[6 + half][:])
+        limit = held([P, WIDE], F32, "limit")
+        for c in range(WIDE // P):
+            nc.tensor.transpose(banks[6][:, c * P : (c + 1) * P], docks_rows[:, c : c + 1].to_broadcast([P, P]), ident[:])
+        nc.scalar.copy(limit[:], banks[6][:])
 
         quantised = {}
 
@@ -179,15 +175,13 @@ def tile_list_bike_route_rebalance_kernel(
                     stop=(n == len(steps) - 1),
                 )
 
-        h_codes = [held([P, S], U32, f"h_codes{b}") for b in range(PASSES)]
-        h_plane = [held([P, S], U8, f"h_plane{b}") for b in range(PASSES)]
+        def quantise_h(name, woven, width, kb=None):
+            codes = held([P, width], U32, f"codes_{name}") if kb is None else placed(kb, [P, width], U32, f"codes_{name}")
+            plane = held([P, width], U8, f"plane_{name}")
+            nc.vector.quantize_mx(out=codes[:].bitcast(FP8X4), scales=plane[:], in_=woven)
+            return codes[:], plane[:]
 
-        def quantise_h(b, j0, j1, woven, codes=None):
-            if codes is None:
-                codes = h_codes[b][:, j0:j1]
-            nc.vector.quantize_mx(out=codes.bitcast(FP8X4), scales=h_plane[b][:, j0:j1], in_=woven)
-
-        def h_by_vector(b, pair, kb_bounded, kb_woven, codes):
+        def h_by_vector(b, pair, kb_bounded, kb_woven, kb_codes):
             woven = placed(kb_woven, [P, CHUNK * PACK], BF16, f"woven0{b}")
             for s in range(CHUNK // P):
                 imbalance(pair[s], b, range(PACK), s * P, P)
@@ -199,7 +193,7 @@ def tile_list_bike_route_rebalance_kernel(
                     gain_sb[:, b : b + 1, :].to_broadcast([P, P, PACK]),
                     ALU.mult,
                 )
-            quantise_h(b, 0, CHUNK, woven[:], codes)
+            return quantise_h(f"h0{b}", woven[:], CHUNK, kb_codes)
 
         def products(c, b, pair):
             for u in range(HALF):
@@ -213,9 +207,8 @@ def tile_list_bike_route_rebalance_kernel(
                 )
             return bounded
 
-        def weigh_on_scalar(c, bounded, kb_rounded, kb_woven):
+        def weigh_on_scalar(c, bounded, kb_rounded, woven):
             rounded = placed(kb_rounded, [P, PACK, CHUNK], BF16, f"rounded{c}0")
-            woven = placed(kb_woven, [P, CHUNK * PACK], BF16, f"woven{c}0")
             for t in range(PACK):
                 nc.scalar.activation(rounded[:, t, :], bounded[:, t, :], ACT.Copy, scale=gain_sb[:, 0, t : t + 1])
             for s in range(CHUNK // P):
@@ -223,7 +216,6 @@ def tile_list_bike_route_rebalance_kernel(
                     woven[:, s * BANK : (s + 1) * BANK].rearrange("p (c i t) -> p c t i", i=RUN, t=PACK),
                     rounded[:, :, s * P : (s + 1) * P].rearrange("p t (c i) -> p c t i", i=RUN),
                 )
-            return woven
 
         def squash_pairs(c, pair, kb):
             bounded = placed(kb, [P, HALF, CHUNK * HALF], F32, f"bounded{c}1")
@@ -235,44 +227,40 @@ def tile_list_bike_route_rebalance_kernel(
                 )
             return bounded
 
-        def weigh_on_gpsimd(bounded, j0, j1, kb, name):
-            woven = placed(kb, [P, (j1 - j0) * PACK], BF16, name)
+        def weigh_on_gpsimd(bounded, woven):
             nc.gpsimd.tensor_tensor(
-                woven[:].rearrange("p (j u e) -> p j u e", u=HALF, e=HALF),
-                bounded[:].rearrange("p u (j e) -> p j u e", e=HALF)[:, j0:j1],
-                gain_sb[:, 1:2, :].rearrange("p o (u e) -> p o u e", e=HALF).to_broadcast([P, j1 - j0, HALF, HALF]),
+                woven.rearrange("p (j u e) -> p j u e", u=HALF, e=HALF),
+                bounded[:].rearrange("p u (j e) -> p j u e", e=HALF),
+                gain_sb[:, 1:2, :].rearrange("p o (u e) -> p o u e", e=HALF).to_broadcast([P, CHUNK, HALF, HALF]),
                 ALU.mult,
             )
-            return woven
 
-        def move_product(out, t, j0, j1, elsewhere=None):
+        def move_product(out, t, h):
             for b in range(PASSES):
-                codes = h_codes[b][:, j0:j1] if elsewhere is None else elsewhere[b]
                 nc.tensor.matmul_mx(
                     out=out,
                     lhsT=quantised[f"w{b}", t][0],
                     lhsT_scale=quantised[f"w{b}", t][1],
-                    rhs=codes.bitcast(FP8X4),
-                    rhs_scale=h_plane[b][:, j0:j1],
+                    rhs=h[b][0].bitcast(FP8X4),
+                    rhs_scale=h[b][1],
                     start=(b == 0),
                     stop=(b == PASSES - 1),
                 )
 
-        def moved_alone(t, j0, j1, bank, kb, elsewhere=None):
-            move_product(bank[:, 0 : j1 - j0], t, j0, j1, elsewhere)
+        def moved_alone(t, j0, j1, bank, kb, h):
+            move_product(bank[:, 0 : j1 - j0], t, h)
             moved = placed(kb, [P, j1 - j0], F32, f"moved{j0}_{t}")
             nc.scalar.copy(moved[:], bank[:, 0 : j1 - j0])
             return moved
 
-        def add_state(t, j0, j1, moved, kb):
-            summed = placed(kb, [P, j1 - j0], F32, f"summed{j0}_{t}")
-            nc.vector.tensor_tensor(summed[:], pages[t][:].indirect(listed(j0, j1)), moved, ALU.add)
-            return summed
+        def room(kb, name):
+            return placed(kb, [P, CHUNK], F32, name)[:]
 
-        def clip(t, j0, j1, summed, kb=None):
-            new = summed if kb is None else placed(kb, [P, j1 - j0], F32, f"new{j0}_{t}")
-            nc.vector.tensor_tensor(new[:], summed[:], limit[:, j0:j1], ALU.min)
-            return new
+        def add_state(t, j0, j1, moved, summed):
+            nc.vector.tensor_tensor(summed, pages[t][:].indirect(listed(j0, j1)), moved, ALU.add)
+
+        def clip(j0, summed, new):
+            nc.vector.tensor_tensor(new, summed, limit[:, j0 : j0 + CHUNK], ALU.min)
 
         def put(t, j0, j1, new):
             nc.vector.tensor_copy(pages[t][:].indirect(listed(j0, j1)), new)
@@ -303,106 +291,114 @@ def tile_list_bike_route_rebalance_kernel(
                 src = raw_late[a][x][:].rearrange("p i (m t) -> p m i t", t=PACK)
                 scaled_copy(on_vector, dst[:, x * P // 2 + m0 : x * P // 2 + m1], src[:, m0:m1], -1.0)
             quantise_weight(f"f{a}1", 0, PACK, dealt[:])
-        codes0 = [placed(63, [P, CHUNK], U32, "codes00")[:], h_codes[1][:, 0:CHUNK]]
-        h_by_vector(0, banks[0:2], (0, 2), 48, codes0[0])
+        h0 = [h_by_vector(0, banks[0:2], (0, 2), 48, 63)]
         dealt_w = {(b, u): placed(kb, [P, part], BF16, f"dealt_w{b}{u}") for b, u, kb in ((0, 0, 64), (1, 0, 5))}
         cast_slots(raw_w[0], 0, dealt_w[0, 0][:], 1.0, True)
         quantise_weight("w0", 0, HALF, dealt_w[0, 0][:])
-        h_by_vector(1, banks[2:4], (4, 66), 50, codes0[1])
+        h0.append(h_by_vector(1, banks[2:4], (4, 66), 50, None))
         cast_slots(raw_w[1], 0, dealt_w[1, 0][:], 1.0, True)
         quantise_weight("w1", 0, HALF, dealt_w[1, 0][:])
         products(1, 0, banks[4:6])
         products(1, 1, banks[0:2])
 
-        def moved_in_parts(t, bank, kbs):
-            move_product(bank[:, 0:CHUNK], t, 0, CHUNK, codes0)
-            parts = [placed(kb, [P, P], F32, f"moved0_{t}_{s}") for s, kb in enumerate(kbs)]
+        def moved_in_parts(t, bank, parts):
+            move_product(bank[:, 0:CHUNK], t, h0)
             for s, piece in enumerate(parts):
-                nc.scalar.copy(piece[:], bank[:, s * P : (s + 1) * P])
-            return parts
+                nc.scalar.copy(piece, bank[:, s * P : (s + 1) * P])
 
-        def add_state_in_parts(t, parts, kb):
-            summed = placed(kb, [P, CHUNK], F32, f"summed0_{t}")
-            for s, piece in enumerate(parts):
-                picks = pages[t][:].indirect(listed(s * P, (s + 1) * P))
-                nc.vector.tensor_tensor(summed[:, s * P : (s + 1) * P], picks, piece[:], ALU.add)
-            return summed
-
-        def moved_pair(u, bank, kb, codes):
+        def moved_pair(u, bank, kb, h):
             for k in range(HALF):
-                move_product(bank[:, k * CHUNK : (k + 1) * CHUNK], u * HALF + k, CHUNK, WIDE, codes)
+                move_product(bank[:, k * CHUNK : (k + 1) * CHUNK], u * HALF + k, h)
             both = placed(kb, [P, HALF, CHUNK], F32, f"moved1_{u}")
             nc.scalar.copy(both[:].rearrange("p k j -> p (k j)"), bank[:])
             return [both[:, k, :] for k in range(HALF)]
 
-        def clips_of(u, j0, sums, kbs):
-            return [clip(u * HALF + k, j0, j0 + CHUNK, sums[k], kbs[k]) for k in range(HALF)]
+        def update_pair(u, j0, moved, sums, news):
+            add_state(u * HALF, j0, j0 + CHUNK, moved[0], sums[0])
+            width = CHUNK // len(moved[1])
+            for s, piece in enumerate(moved[1]):
+                add_state(u * HALF + 1, j0 + s * width, j0 + (s + 1) * width, piece, sums[1][:, s * width : (s + 1) * width])
+            for k in range(HALF):
+                clip(j0, sums[k], news[k])
 
         def puts_of(u, j0, news):
             for k in range(HALF):
-                put(u * HALF + k, j0, j0 + CHUNK, news[k][:])
+                put(u * HALF + k, j0, j0 + CHUNK, news[k])
 
-        moved0 = moved_alone(0, 0, CHUNK, banks[6], 73, codes0)
-        moved1 = moved_in_parts(1, banks[7], (70, 74))
+        moved0 = moved_alone(0, 0, CHUNK, banks[6], 73, h0)
+        moved1 = [placed(kb, [P, P], F32, f"moved0_1_{s}")[:] for s, kb in enumerate((99.5, 74))]
+        moved_in_parts(1, banks[7], moved1)
         bounded11 = squash_pairs(1, banks[0:2], 12)
-        for b, kb in enumerate((3, 68)):
+        for b, kb in enumerate((2.5, 95)):
             dealt_w[b, 1] = placed(kb, [P, part], BF16, f"dealt_w{b}1")
             cast_slots(raw_w[b], 1, dealt_w[b, 1][:], 1.0, False)
         bounded10 = squash_slots(1, banks[4:6], 28)
-        gather_words(1, WIDE, S, 6.5)
+        gather_words(1, WIDE, WIDE + CHUNK, 6.5)
         for b in range(PASSES):
-            quantise_weight(f"w{b}", HALF, PACK, dealt_w[b, 1][:], (5, 50)[b])
+            quantise_weight(f"w{b}", HALF, PACK, dealt_w[b, 1][:], (4.5, 5.5)[b])
 
-        sums = [add_state(0, 0, CHUNK, moved0[:], 75), add_state_in_parts(1, moved1, 76)]
-        news = clips_of(0, 0, sums, (69.5, 79))
-        woven11 = weigh_on_gpsimd(bounded11, 0, CHUNK, 75, "woven11")
+        half = CHUNK * PACK
+        woven1 = placed(100, [P, PASSES * half], BF16, "woven1")
+        rooms1 = woven1[:].bitcast(F32).rearrange("p (x j) -> p x j", j=CHUNK)
+        woven_wide1 = placed(96, [P, 2 * half], BF16, "woven_wide1")
+        rooms2 = woven_wide1[:].bitcast(F32).rearrange("p (x j) -> p x j", j=CHUNK)
+
+        news = [rooms2[:, 0, :], room(79, "new0_1")]
+        update_pair(0, 0, [moved0[:], moved1], [rooms1[:, 2, :], room(90, "summed0_1")], news)
+        weigh_on_gpsimd(bounded11, woven1[:, half:])
+        gather_words(1, WIDE + CHUNK, S, 74)
         puts_of(0, 0, news)
-        woven10 = weigh_on_scalar(1, bounded10, 73, 77)
-        moved2 = moved_alone(2, 0, CHUNK, banks[4], 80, codes0)
-        moved3 = moved_in_parts(3, banks[5], (96, 81))
+        weigh_on_scalar(1, bounded10, 71.5, woven1[:, 0:half])
+        moved2 = moved_alone(2, 0, CHUNK, banks[4], 80, h0)
+        moved3 = [rooms2[:, 2, 0:P], placed(81, [P, P], F32, "moved0_3_1")[:]]
+        moved_in_parts(3, banks[5], moved3)
         products(2, 1, banks[6:8])
         bounded21 = squash_pairs(2, banks[6:8], 30)
 
-        codes1 = [placed(79, [P, CHUNK], U32, "codes10")[:], h_codes[1][:, CHUNK:WIDE]]
-        quantise_h(1, CHUNK, WIDE, woven11[:])
-        quantise_h(0, CHUNK, WIDE, woven10[:], codes1[0])
-        sums = [add_state(2, 0, CHUNK, moved2[:], 76), add_state_in_parts(3, moved3, 77)]
-        news = clips_of(1, 0, sums, (96, 97))
-        woven21 = weigh_on_gpsimd(bounded21, 0, CHUNK, 76, "woven21")
+        codes, plane = quantise_h("h1", woven1[:], PASSES * CHUNK)
+        h1 = [(codes[:, b * CHUNK : (b + 1) * CHUNK], plane[:, b * CHUNK : (b + 1) * CHUNK]) for b in range(PASSES)]
+        news = [rooms2[:, 2, :], room(82, "new0_3")]
+        update_pair(1, 0, [moved2[:], moved3], [rooms2[:, 0, :], room(103, "summed0_3")], news)
+        weigh_on_gpsimd(bounded21, woven_wide1[:, 0:half])
         puts_of(1, 0, news)
-        moved = moved_pair(0, banks[2], 84, codes1) + moved_pair(1, banks[3], 86, codes1)
+        products(2, 0, banks[4:6])
+        bounded20 = squash_slots(2, banks[4:6], 26)
+        moved = moved_pair(0, banks[5], 84, h1)
         products(3, 1, banks[0:2])
         bounded31 = squash_pairs(3, banks[0:2], 8.5)
-        products(2, 0, banks[4:6])
-        woven20 = weigh_on_scalar(2, squash_slots(2, banks[4:6], 26), 56, 92)
-        products(3, 0, banks[6:8])
-        woven30 = weigh_on_scalar(3, squash_slots(3, banks[6:8], 20), 60, 94)
+        woven_wide0 = placed(92, [P, 2 * half], BF16, "woven_wide0")
+        weigh_on_scalar(2, bounded20, 56, woven_wide0[:, 0:half])
+        products(3, 0, banks[2:4])
+        moved.extend(moved_pair(1, banks[1], 86, h1))
+        weigh_on_scalar(3, squash_slots(3, banks[2:4], 20), 60, woven_wide0[:, half:])
 
-        quantise_h(1, WIDE, WIDE + CHUNK, woven21[:])
-        sums = [add_state(k, CHUNK, WIDE, moved[k], 96 + k) for k in range(HALF)]
-        news = clips_of(0, CHUNK, sums, (76, 77))
-        woven31 = weigh_on_gpsimd(bounded31, 0, CHUNK, 96, "woven31")
+        news = [room(76, "new1_0"), room(79, "new1_1")]
+        update_pair(0, CHUNK, [moved[0], [moved[1]]], [rooms2[:, 2, :], room(82, "summed1_1")], news)
+        weigh_on_gpsimd(bounded31, woven_wide1[:, half:])
         puts_of(0, CHUNK, news)
 
-        wide0 = placed(77, [P, WIDE], U32, "wide0")
-        quantise_h(0, WIDE, WIDE + CHUNK, woven20[:], wide0[:, 0:CHUNK])
-        quantise_h(0, WIDE + CHUNK, S, woven30[:], wide0[:, CHUNK:WIDE])
-        quantise_h(1, WIDE + CHUNK, S, woven31[:])
-        wide = [wide0[:], h_codes[1][:, WIDE:S]]
-        sums = [add_state(HALF + k, CHUNK, WIDE, moved[HALF + k], (93.5, 95.5)[k]) for k in range(HALF)]
-        news1 = clips_of(1, CHUNK, sums, (82, 83))
-        moved = [moved_alone(t, WIDE, S, banks[(2, 3, 0, 1)[t]], 32 + 2 * t, wide) for t in range(PACK)]
-        picked = [placed(kb, [P, WIDE], F32, f"picked{t}") for t, kb in enumerate((92, 94, 96, 86))]
-        for t in range(PACK):
+        wide = [quantise_h("wide0", woven_wide0[:], WIDE, 76), quantise_h("wide1", woven_wide1[:], WIDE)]
+        picked = [placed(kb, [P, WIDE], F32, f"picked{t}") for t, kb in enumerate((90.5, 94.5, 85, 87))]
+
+        def pick(t):
             nc.vector.tensor_copy(picked[t][:], pages[t][:].indirect(listed(WIDE, S)))
+
+        for t in range(HALF):
+            pick(t)
+        sums = placed(92.5, [P, HALF, CHUNK], F32, "summed1_23")
+        news1 = [room(82, "new1_2"), room(83, "new1_3")]
+        update_pair(1, CHUNK, [moved[2], [moved[3]]], [sums[:, k, :] for k in range(HALF)], news1)
+        for t in range(HALF, PACK):
+            pick(t)
         puts_of(1, CHUNK, news1)
 
         news = []
-        for t, kb_summed, kb_clipped, kb_back in ((0, 0, 44, 56), (1, 8, 46, 58), (2, 10, 40, 60), (3, 98, 15, None)):
-            turned, returned = banks[4 + t % HALF], banks[6 + t % HALF]
+        for t, kb_summed, kb_clipped, kb_back in ((0, 0, 92.5, 56), (1, 8, 46, 58), (2, 10, 40, 60), (3, 106, 15, None)):
+            turned, returned = banks[(6, 7, 5, 1)[t]], banks[(5, 1, 2, 3)[t]]
+            moved = moved_alone(t, WIDE, S, banks[(6, 7, 4, 0)[t]], 32 + 2 * t, wide)
             for x in range(WIDE // P):
                 cols = slice(x * P, (x + 1) * P)
-                for last, term in enumerate((moved[t], picked[t])):
+                for last, term in enumerate((moved, picked[t])):
                     nc.tensor.matmul(turned[:, cols], term[:, cols], ident[:], start=not last, stop=bool(last), is_transpose=True)
             summed = placed(kb_summed, [P, WIDE], F32, f"summed_turned{t}")
             nc.scalar.copy(summed[:], turned[:])
@@ -424,7 +420,7 @@ def tile_list_bike_route_rebalance_kernel(
             placed(kb, [P, HALF, width * HALF], BF16, f"paired{kb}") for kb, width in ((12, BANK), (16, T - BANK))
         ]
         back3 = blocks[0][:, 1, :].bitcast(F32)
-        nc.scalar.copy(back3, banks[7][:])
+        nc.scalar.copy(back3, banks[3][:])
 
         out_rows = out_0.rearrange("(p t) m -> p t m", t=PACK)
         starts = [sum(PIECES[:q]) for q in range(len(PIECES))]

@@ -116,10 +116,14 @@ def tile_list_bike_route_rebalance_kernel(
         nc.tensor.transpose(banks[5][:, 0:P], lines[:, 0:P], ident[:])
         nc.scalar.copy(docks_rows[:], banks[5][:, PASSES : PASSES + S // P])
         nc.scalar.copy(gain_sb[:], banks[4][:].rearrange("p (t r) -> p r t", t=PACK)[:, 0:PASSES, :])
-        limit = held([P, WIDE], F32, "limit")
-        for c in range(WIDE // P):
-            nc.tensor.transpose(banks[6][:, c * P : (c + 1) * P], docks_rows[:, c : c + 1].to_broadcast([P, P]), ident[:])
-        nc.scalar.copy(limit[:], banks[6][:])
+        limit = held([P, S], F32, "limit")
+        for x in range(S // BANK):
+            for c in range(BANK // P):
+                col = x * BANK // P + c
+                nc.tensor.transpose(
+                    banks[6 + x][:, c * P : (c + 1) * P], docks_rows[:, col : col + 1].to_broadcast([P, P]), ident[:]
+                )
+            nc.scalar.copy(limit[:, x * BANK : (x + 1) * BANK], banks[6 + x][:])
 
         quantised = {}
 
@@ -361,6 +365,13 @@ def tile_list_bike_route_rebalance_kernel(
         update_pair(1, 0, [moved2[:], moved3], [rooms2[:, 0, :], room(103, "summed0_3")], news)
         weigh_on_gpsimd(bounded21, woven_wide1[:, 0:half])
         puts_of(1, 0, news)
+        picked = {}
+
+        def pick(t, kb):
+            picked[t] = placed(kb, [P, WIDE], F32, f"picked{t}")
+            nc.vector.tensor_copy(picked[t][:], pages[t][:].indirect(listed(WIDE, S)))
+
+        pick(2, 88)
         products(2, 0, banks[4:6])
         bounded20 = squash_slots(2, banks[4:6], 26)
         moved = moved_pair(0, banks[5], 84, h1)
@@ -375,26 +386,31 @@ def tile_list_bike_route_rebalance_kernel(
         news = [room(76, "new1_0"), room(79, "new1_1")]
         update_pair(0, CHUNK, [moved[0], [moved[1]]], [rooms2[:, 2, :], room(82, "summed1_1")], news)
         weigh_on_gpsimd(bounded31, woven_wide1[:, half:])
+        pick(3, 80.5)
         puts_of(0, CHUNK, news)
 
         wide = [quantise_h("wide0", woven_wide0[:], WIDE, 76), quantise_h("wide1", woven_wide1[:], WIDE)]
-        picked = [placed(kb, [P, WIDE], F32, f"picked{t}") for t, kb in enumerate((90.5, 94.5, 85, 87))]
-
-        def pick(t):
-            nc.vector.tensor_copy(picked[t][:], pages[t][:].indirect(listed(WIDE, S)))
-
-        for t in range(HALF):
-            pick(t)
+        pick(1, 94.5)
+        move_product(banks[6][:], 0, wide)
+        moved_wide0 = [room(32 + s, f"moved_wide0_{s}") for s in range(WIDE // CHUNK)]
+        for s, piece in enumerate(moved_wide0):
+            nc.scalar.copy(piece, banks[6][:, s * CHUNK : (s + 1) * CHUNK])
         sums = placed(92.5, [P, HALF, CHUNK], F32, "summed1_23")
-        news1 = [room(82, "new1_2"), room(83, "new1_3")]
-        update_pair(1, CHUNK, [moved[2], [moved[3]]], [sums[:, k, :] for k in range(HALF)], news1)
-        for t in range(HALF, PACK):
-            pick(t)
+        for k in range(HALF):
+            add_state(HALF + k, CHUNK, WIDE, moved[HALF + k], sums[:, k, :])
+        summed = placed(90.5, [P, WIDE], F32, "summed_wide0")
+        for s, piece in enumerate(moved_wide0):
+            add_state(0, WIDE + s * CHUNK, WIDE + (s + 1) * CHUNK, piece, summed[:, s * CHUNK : (s + 1) * CHUNK])
+        both = placed(30.5, [P, HALF, CHUNK], F32, "new1_23")
+        news1 = [both[:, k, :] for k in range(HALF)]
+        for k in range(HALF):
+            clip(CHUNK, sums[:, k, :], news1[k])
+        news = [placed(86, [P, WIDE], F32, "new_wide0")]
+        nc.vector.tensor_tensor(news[0][:], summed[:], limit[:, WIDE:S], ALU.min)
         puts_of(1, CHUNK, news1)
 
-        news = []
-        for t, kb_summed, kb_clipped, kb_back in ((0, 0, 92.5, 56), (1, 8, 46, 58), (2, 10, 40, 60), (3, 106, 15, None)):
-            turned, returned = banks[(6, 7, 5, 1)[t]], banks[(5, 1, 2, 3)[t]]
+        for t, kb_summed, kb_clipped, kb_back in ((1, 8, 90.5, 58), (2, 10, 40, 60), (3, 106, 15, None)):
+            turned, returned = banks[(6, 7, 4, 0)[t]], banks[(5, 1, 2, 3)[t]]
             moved = moved_alone(t, WIDE, S, banks[(6, 7, 4, 0)[t]], 32 + 2 * t, wide)
             for x in range(WIDE // P):
                 cols = slice(x * P, (x + 1) * P)

@@ -31,9 +31,9 @@ RUN = 4
 KB = 1024
 PIECES = (256, 256, 512, 256, 256, 256, 256)
 SCALAR_PIECES = 3
-SHARES = (((0, 0, 64, False), (1, 0, 64, True)), ((0, 0, 64, True), (1, 0, 64, False)))
+SCALAR_EIGHTHS = 3
 LOWEST = -3.4028234663852886e38
-ORDER = (((0, True), (0, False), (1, True), (1, False)), ((0, True), (1, True), (0, False), (1, False)))
+ORDER = ((0, True), (0, False), (1, True), (1, False))
 
 
 def tile_list_bike_route_rebalance_kernel(
@@ -94,16 +94,16 @@ def tile_list_bike_route_rebalance_kernel(
         scale_rows_in = flow_scales.rearrange("a (q r) c -> r q a c", q=QUADS)
         for r in range(4):
             nc.sync.dma_start(flow_plane_raw[r:P:32, :, :].bitcast(I32), scale_rows_in[r].bitcast(I32))
-        raw_f00 = load_rows(0, "f00", flowT, 0, 0, GROUP)
+        raw_f0 = placed(0, [P, PACK, K], F32, "raw_f0")
+        rows_f0 = flowT[0:GROUP, :].rearrange("(p i) c -> p i c", i=PACK)
+        nc.sync.dma_start(raw_f0[:, 0:HALF, :], rows_f0[:, 0:HALF, :])
         nc.vector.tensor_copy(v_plane[:], tab_planes[:].indirect(offsets[:]))
         place_planes(0)
-        raw_f10 = load_rows(8, "f10", flowT, 1, 0, GROUP)
+        nc.sync.dma_start(raw_f0[:, HALF:PACK, :], rows_f0[:, HALF:PACK, :])
         place_planes(1)
         load_table(1)
-        raw_late = [
-            [load_rows(16 + 8 * a + 4 * x, f"f{a}1{x}", flowT, a, GROUP + x * GROUP // 2, GROUP + (x + 1) * GROUP // 2) for x in range(2)]
-            for a in range(PASSES)
-        ]
+        raw_f10 = load_rows(16, "f10", flowT, 1, 0, GROUP)
+        raw_f11 = [load_rows(24 + 4 * x, f"f11{x}", flowT, 1, GROUP + x * GROUP // 2, GROUP + (x + 1) * GROUP // 2) for x in range(2)]
         raw_w = [load_rows(32 + 8 * b, f"w{b}", wm, b, 0, N) for b in range(PASSES)]
         gT_rows = gT.rearrange("(p t) m -> p t m", t=PACK)
         for t in range(PACK):
@@ -134,7 +134,7 @@ def tile_list_bike_route_rebalance_kernel(
                 nc.scalar.activation(dst, src, ACT.Copy, scale=sign)
 
         def cast_slots(raw, u, dealt, sign, on_vector):
-            src = raw[:].rearrange("p i (m t) -> p m i t", t=PACK)[:, :, :, u * HALF : (u + 1) * HALF]
+            src = raw.rearrange("p i (m t) -> p m i t", t=PACK)[:, :, :, u * HALF : (u + 1) * HALF]
             scaled_copy(on_vector, dealt.rearrange("p (t m i) -> p m i t", t=HALF, i=PACK), src, sign)
 
         def quantise_weight(name, t0, t1, dealt, kb=None):
@@ -161,7 +161,7 @@ def tile_list_bike_route_rebalance_kernel(
                 v_words[a, j // CHUNK] = words[:, j - j0 : j - j0 + CHUNK]
 
         def imbalance(bank, b, slots, j0, width):
-            steps = [(a, packed, t) for a, packed in ORDER[b] for t in slots]
+            steps = [(a, packed, t) for a, packed in ORDER for t in slots]
             for n, (a, packed, t) in enumerate(steps):
                 if packed:
                     lhs = flow_codes[:, a * PASSES + b, t, :].bitcast(FP4X4)
@@ -280,27 +280,29 @@ def tile_list_bike_route_rebalance_kernel(
             flow_plane_raw[:].rearrange("p a (b m t) -> p (a b) m t", m=P, t=PACK),
         )
         part = HALF * GROUP
-        for a, raw in enumerate((raw_f00, raw_f10)):
-            dealt = placed(48 + 4 * a, [P, PACK * GROUP], BF16, f"dealt_f{a}0")
+        for name, raw, kb in (("f00", raw_f0[:, :, 0:GROUP], 48), ("f01", raw_f0[:, :, GROUP:K], 56)):
+            dealt = placed(kb, [P, PACK * GROUP], BF16, f"dealt_{name}")
             for u in range(HALF):
                 cast_slots(raw, u, dealt[:, u * part : (u + 1) * part], -1.0, u == 1)
-            if a == 1:
-                gather_words(1, 0, CHUNK)
-            quantise_weight(f"f{a}0", 0, PACK, dealt[:])
+            quantise_weight(name, 0, PACK, dealt[:])
+        gather_words(1, 0, CHUNK)
         gather_words(1, CHUNK, WIDE)
-        for a in range(PASSES):
-            dealt = placed(56 + 4 * a, [P, PACK * GROUP], BF16, f"dealt_f{a}1")
+        for name, loads, kb in (("f10", [(raw_f10, True)], 52), ("f11", [(raw_f11[0], False), (raw_f11[1], True)], 60)):
+            dealt = placed(kb, [P, PACK * GROUP], BF16, f"dealt_{name}")
             dst = dealt[:].rearrange("p (t m i) -> p m i t", t=PACK, i=PACK)
-            for x, m0, m1, on_vector in SHARES[a]:
-                src = raw_late[a][x][:].rearrange("p i (m t) -> p m i t", t=PACK)
-                scaled_copy(on_vector, dst[:, x * P // 2 + m0 : x * P // 2 + m1], src[:, m0:m1], -1.0)
-            quantise_weight(f"f{a}1", 0, PACK, dealt[:])
+            width = P // len(loads)
+            for x, (raw, shared) in enumerate(loads):
+                src = raw[:].rearrange("p i (m t) -> p m i t", t=PACK)
+                split = width * SCALAR_EIGHTHS // 8 if shared else 0
+                for m0, m1 in ((0, split), (split, width)) if shared else ((0, width),):
+                    scaled_copy(m1 == width, dst[:, x * width + m0 : x * width + m1], src[:, m0:m1], -1.0)
+            quantise_weight(name, 0, PACK, dealt[:])
         h0 = [h_by_vector(0, banks[0:2], (0, 2), 48, 63)]
         dealt_w = {(b, u): placed(kb, [P, part], BF16, f"dealt_w{b}{u}") for b, u, kb in ((0, 0, 64), (1, 0, 5))}
-        cast_slots(raw_w[0], 0, dealt_w[0, 0][:], 1.0, True)
+        cast_slots(raw_w[0][:], 0, dealt_w[0, 0][:], 1.0, True)
         quantise_weight("w0", 0, HALF, dealt_w[0, 0][:])
         h0.append(h_by_vector(1, banks[2:4], (4, 66), 50, None))
-        cast_slots(raw_w[1], 0, dealt_w[1, 0][:], 1.0, True)
+        cast_slots(raw_w[1][:], 0, dealt_w[1, 0][:], 1.0, True)
         quantise_weight("w1", 0, HALF, dealt_w[1, 0][:])
         products(1, 0, banks[4:6])
         products(1, 1, banks[0:2])
@@ -335,7 +337,7 @@ def tile_list_bike_route_rebalance_kernel(
         bounded11 = squash_pairs(1, banks[0:2], 12)
         for b, kb in enumerate((2.5, 95)):
             dealt_w[b, 1] = placed(kb, [P, part], BF16, f"dealt_w{b}1")
-            cast_slots(raw_w[b], 1, dealt_w[b, 1][:], 1.0, False)
+            cast_slots(raw_w[b][:], 1, dealt_w[b, 1][:], 1.0, False)
         bounded10 = squash_slots(1, banks[4:6], 28)
         gather_words(1, WIDE, WIDE + CHUNK, 6.5)
         for b in range(PASSES):

@@ -31,7 +31,8 @@ RUN = 4
 KB = 1024
 PIECES = (256, 256, 512, 256, 256, 256, 256)
 SCALAR_PIECES = 3
-SCALAR_EIGHTHS = 3
+SCALAR_SHARE = 48
+GPSIMD_FROM = 1024
 LOWEST = -3.4028234663852886e38
 ORDER = ((0, True), (0, False), (1, True), (1, False))
 
@@ -103,7 +104,7 @@ def tile_list_bike_route_rebalance_kernel(
         place_planes(1)
         load_table(1)
         raw_f10 = load_rows(16, "f10", flowT, 1, 0, GROUP)
-        raw_f11 = [load_rows(24 + 4 * x, f"f11{x}", flowT, 1, GROUP + x * GROUP // 2, GROUP + (x + 1) * GROUP // 2) for x in range(2)]
+        raw_f11 = load_rows(24, "f11", flowT, 1, GROUP, K)
         raw_w = [load_rows(32 + 8 * b, f"w{b}", wm, b, 0, N) for b in range(PASSES)]
         gT_rows = gT.rearrange("(p t) m -> p t m", t=PACK)
         for t in range(PACK):
@@ -116,14 +117,10 @@ def tile_list_bike_route_rebalance_kernel(
         nc.tensor.transpose(banks[5][:, 0:P], lines[:, 0:P], ident[:])
         nc.scalar.copy(docks_rows[:], banks[5][:, PASSES : PASSES + S // P])
         nc.scalar.copy(gain_sb[:], banks[4][:].rearrange("p (t r) -> p r t", t=PACK)[:, 0:PASSES, :])
-        limit = held([P, S], F32, "limit")
-        for x in range(S // BANK):
-            for c in range(BANK // P):
-                col = x * BANK // P + c
-                nc.tensor.transpose(
-                    banks[6 + x][:, c * P : (c + 1) * P], docks_rows[:, col : col + 1].to_broadcast([P, P]), ident[:]
-                )
-            nc.scalar.copy(limit[:, x * BANK : (x + 1) * BANK], banks[6 + x][:])
+        limit = held([P, WIDE], F32, "limit")
+        for c in range(WIDE // P):
+            nc.tensor.transpose(banks[6][:, c * P : (c + 1) * P], docks_rows[:, c : c + 1].to_broadcast([P, P]), ident[:])
+        nc.scalar.copy(limit[:], banks[6][:])
 
         quantised = {}
 
@@ -287,15 +284,12 @@ def tile_list_bike_route_rebalance_kernel(
             quantise_weight(name, 0, PACK, dealt[:])
         gather_words(1, 0, CHUNK)
         gather_words(1, CHUNK, WIDE)
-        for name, loads, kb in (("f10", [(raw_f10, True)], 52), ("f11", [(raw_f11[0], False), (raw_f11[1], True)], 60)):
+        for name, raw, kb in (("f10", raw_f10, 52), ("f11", raw_f11, 60)):
             dealt = placed(kb, [P, PACK * GROUP], BF16, f"dealt_{name}")
             dst = dealt[:].rearrange("p (t m i) -> p m i t", t=PACK, i=PACK)
-            width = P // len(loads)
-            for x, (raw, shared) in enumerate(loads):
-                src = raw[:].rearrange("p i (m t) -> p m i t", t=PACK)
-                split = width * SCALAR_EIGHTHS // 8 if shared else 0
-                for m0, m1 in ((0, split), (split, width)) if shared else ((0, width),):
-                    scaled_copy(m1 == width, dst[:, x * width + m0 : x * width + m1], src[:, m0:m1], -1.0)
+            src = raw[:].rearrange("p i (m t) -> p m i t", t=PACK)
+            for m0, m1 in ((0, SCALAR_SHARE), (SCALAR_SHARE, P)):
+                scaled_copy(m1 == P, dst[:, m0:m1], src[:, m0:m1], -1.0)
             quantise_weight(name, 0, PACK, dealt[:])
         h0 = [h_by_vector(0, banks[0:2], (0, 2), 48, 63)]
         dealt_w = {(b, u): placed(kb, [P, part], BF16, f"dealt_w{b}{u}") for b, u, kb in ((0, 0, 64), (1, 0, 5))}
@@ -369,11 +363,13 @@ def tile_list_bike_route_rebalance_kernel(
         puts_of(1, 0, news)
         picked = {}
 
-        def pick(t, kb):
-            picked[t] = placed(kb, [P, WIDE], F32, f"picked{t}")
-            nc.vector.tensor_copy(picked[t][:], pages[t][:].indirect(listed(WIDE, S)))
+        def pick(t, j0, j1, kb):
+            tile = placed(kb, [P, j1 - j0], F32, f"picked{t}_{j0}")
+            nc.vector.tensor_copy(tile[:], pages[t][:].indirect(listed(j0, j1)))
+            for j in range(j0, j1, P):
+                picked[t, j // P] = tile[:, j - j0 : j - j0 + P]
 
-        pick(2, 88)
+        pick(2, WIDE, WIDE + CHUNK, 90)
         products(2, 0, banks[4:6])
         bounded20 = squash_slots(2, banks[4:6], 26)
         moved = moved_pair(0, banks[5], 84, h1)
@@ -388,36 +384,26 @@ def tile_list_bike_route_rebalance_kernel(
         news = [room(76, "new1_0"), room(79, "new1_1")]
         update_pair(0, CHUNK, [moved[0], [moved[1]]], [rooms2[:, 2, :], room(82, "summed1_1")], news)
         weigh_on_gpsimd(bounded31, woven_wide1[:, half:])
-        pick(3, 80.5)
         puts_of(0, CHUNK, news)
+        pick(2, WIDE + CHUNK, S, 84)
 
         wide = [quantise_h("wide0", woven_wide0[:], WIDE, 76), quantise_h("wide1", woven_wide1[:], WIDE)]
-        pick(1, 94.5)
-        move_product(banks[6][:], 0, wide)
-        moved_wide0 = [room(32 + s, f"moved_wide0_{s}") for s in range(WIDE // CHUNK)]
-        for s, piece in enumerate(moved_wide0):
-            nc.scalar.copy(piece, banks[6][:, s * CHUNK : (s + 1) * CHUNK])
+        pick(0, WIDE, S, 94.5)
         sums = placed(92.5, [P, HALF, CHUNK], F32, "summed1_23")
-        for k in range(HALF):
-            add_state(HALF + k, CHUNK, WIDE, moved[HALF + k], sums[:, k, :])
-        summed = placed(90.5, [P, WIDE], F32, "summed_wide0")
-        for s, piece in enumerate(moved_wide0):
-            add_state(0, WIDE + s * CHUNK, WIDE + (s + 1) * CHUNK, piece, summed[:, s * CHUNK : (s + 1) * CHUNK])
-        both = placed(30.5, [P, HALF, CHUNK], F32, "new1_23")
-        news1 = [both[:, k, :] for k in range(HALF)]
-        for k in range(HALF):
-            clip(CHUNK, sums[:, k, :], news1[k])
-        news = [placed(86, [P, WIDE], F32, "new_wide0")]
-        nc.vector.tensor_tensor(news[0][:], summed[:], limit[:, WIDE:S], ALU.min)
+        news1 = [room(82, "new1_2"), room(83, "new1_3")]
+        update_pair(1, CHUNK, [moved[2], [moved[3]]], [sums[:, k, :] for k in range(HALF)], news1)
+        for t, kb in ((1, 85), (3, 87)):
+            pick(t, WIDE, S, kb)
         puts_of(1, CHUNK, news1)
 
-        for t, kb_summed, kb_clipped, kb_back in ((1, 8, 90.5, 58), (2, 10, 40, 60), (3, 106, 15, None)):
-            turned, returned = banks[(6, 7, 4, 0)[t]], banks[(5, 1, 2, 3)[t]]
+        news = []
+        for t, kb_summed, kb_clipped, kb_back in ((0, 0, 92.5, 56), (1, 8, 46, 58), (2, 10, 40, 60), (3, 106, 15, None)):
+            turned, returned = banks[(6, 7, 5, 1)[t]], banks[(5, 1, 2, 3)[t]]
             moved = moved_alone(t, WIDE, S, banks[(6, 7, 4, 0)[t]], 32 + 2 * t, wide)
             for x in range(WIDE // P):
                 cols = slice(x * P, (x + 1) * P)
-                for last, term in enumerate((moved, picked[t])):
-                    nc.tensor.matmul(turned[:, cols], term[:, cols], ident[:], start=not last, stop=bool(last), is_transpose=True)
+                for last, term in enumerate((moved[:, cols], picked[t, WIDE // P + x])):
+                    nc.tensor.matmul(turned[:, cols], term, ident[:], start=not last, stop=bool(last), is_transpose=True)
             summed = placed(kb_summed, [P, WIDE], F32, f"summed_turned{t}")
             nc.scalar.copy(summed[:], turned[:])
             clipped = placed(kb_clipped, [P, WIDE], F32, f"clipped{t}")
@@ -453,7 +439,7 @@ def tile_list_bike_route_rebalance_kernel(
                 x, cols = block_of(q)
                 dst = blocks[x][:, t // HALF, :].rearrange("p (m e) -> p m e", e=HALF)[:, cols, t % HALF]
                 src = pages[t][:, starts[q] : starts[q] + width]
-                if t < HALF and starts[q] >= T // 2:
+                if t < HALF and starts[q] >= GPSIMD_FROM:
                     nc.gpsimd.tensor_scalar(dst, src, 1.0, 1.0, ALU.mult, ALU.mult)
                 elif t >= HALF and x == 0:
                     nc.vector.tensor_copy(dst, src)

@@ -288,9 +288,10 @@ def tile_list_bike_route_rebalance_kernel(
             dealt = placed(kb, [P, PACK * GROUP], BF16, f"dealt_{name}")
             dst = dealt[:].rearrange("p (t m i) -> p m i t", t=PACK, i=PACK)
             src = raw[:].rearrange("p i (m t) -> p m i t", t=PACK)
-            for m0, m1 in ((0, SCALAR_SHARE), (SCALAR_SHARE, P)):
+            for m0, m1 in ((0, SCALAR_SHARE), (SCALAR_SHARE, P)) if name == "f10" else ((0, P),):
                 scaled_copy(m1 == P, dst[:, m0:m1], src[:, m0:m1], -1.0)
             quantise_weight(name, 0, PACK, dealt[:])
+        gather_words(1, WIDE, WIDE + CHUNK, 52)
         h0 = [h_by_vector(0, banks[0:2], (0, 2), 48, 63)]
         dealt_w = {(b, u): placed(kb, [P, part], BF16, f"dealt_w{b}{u}") for b, u, kb in ((0, 0, 64), (1, 0, 5))}
         cast_slots(raw_w[0][:], 0, dealt_w[0, 0][:], 1.0, True)
@@ -333,7 +334,7 @@ def tile_list_bike_route_rebalance_kernel(
             dealt_w[b, 1] = placed(kb, [P, part], BF16, f"dealt_w{b}1")
             cast_slots(raw_w[b][:], 1, dealt_w[b, 1][:], 1.0, False)
         bounded10 = squash_slots(1, banks[4:6], 28)
-        gather_words(1, WIDE, WIDE + CHUNK, 6.5)
+        gather_words(1, WIDE + CHUNK, S, 6.5)
         for b in range(PASSES):
             quantise_weight(f"w{b}", HALF, PACK, dealt_w[b, 1][:], (4.5, 5.5)[b])
 
@@ -343,10 +344,18 @@ def tile_list_bike_route_rebalance_kernel(
         woven_wide1 = placed(96, [P, 2 * half], BF16, "woven_wide1")
         rooms2 = woven_wide1[:].bitcast(F32).rearrange("p (x j) -> p x j", j=CHUNK)
 
+        picked = {}
+
+        def pick(t, j0, j1, kb):
+            tile = placed(kb, [P, j1 - j0], F32, f"picked{t}_{j0}")
+            nc.vector.tensor_copy(tile[:], pages[t][:].indirect(listed(j0, j1)))
+            for j in range(j0, j1, P):
+                picked[t, j // P] = tile[:, j - j0 : j - j0 + P]
+
         news = [rooms2[:, 0, :], room(79, "new0_1")]
         update_pair(0, 0, [moved0[:], moved1], [rooms1[:, 2, :], room(90, "summed0_1")], news)
         weigh_on_gpsimd(bounded11, woven1[:, half:])
-        gather_words(1, WIDE + CHUNK, S, 74)
+        pick(0, WIDE, WIDE + CHUNK, 74)
         puts_of(0, 0, news)
         weigh_on_scalar(1, bounded10, 71.5, woven1[:, 0:half])
         moved2 = moved_alone(2, 0, CHUNK, banks[4], 80, h0)
@@ -361,14 +370,6 @@ def tile_list_bike_route_rebalance_kernel(
         update_pair(1, 0, [moved2[:], moved3], [rooms2[:, 0, :], room(103, "summed0_3")], news)
         weigh_on_gpsimd(bounded21, woven_wide1[:, 0:half])
         puts_of(1, 0, news)
-        picked = {}
-
-        def pick(t, j0, j1, kb):
-            tile = placed(kb, [P, j1 - j0], F32, f"picked{t}_{j0}")
-            nc.vector.tensor_copy(tile[:], pages[t][:].indirect(listed(j0, j1)))
-            for j in range(j0, j1, P):
-                picked[t, j // P] = tile[:, j - j0 : j - j0 + P]
-
         pick(2, WIDE, WIDE + CHUNK, 90)
         products(2, 0, banks[4:6])
         bounded20 = squash_slots(2, banks[4:6], 26)
@@ -388,7 +389,7 @@ def tile_list_bike_route_rebalance_kernel(
         pick(2, WIDE + CHUNK, S, 84)
 
         wide = [quantise_h("wide0", woven_wide0[:], WIDE, 76), quantise_h("wide1", woven_wide1[:], WIDE)]
-        pick(0, WIDE, S, 94.5)
+        pick(0, WIDE + CHUNK, S, 95.5)
         sums = placed(92.5, [P, HALF, CHUNK], F32, "summed1_23")
         news1 = [room(82, "new1_2"), room(83, "new1_3")]
         update_pair(1, CHUNK, [moved[2], [moved[3]]], [sums[:, k, :] for k in range(HALF)], news1)
@@ -396,17 +397,24 @@ def tile_list_bike_route_rebalance_kernel(
             pick(t, WIDE, S, kb)
         puts_of(1, CHUNK, news1)
 
+        blocks = [
+            placed(kb, [P, HALF, width * HALF], BF16, f"paired{kb}") for kb, width in ((12, BANK), (16, T - BANK))
+        ]
+        middle = (T - BANK) * HALF
         news = []
-        for t, kb_summed, kb_clipped, kb_back in ((0, 0, 92.5, 56), (1, 8, 46, 58), (2, 10, 40, 60), (3, 106, 15, None)):
+        for t, kb_summed, kb_clipped, kb_back in ((0, 0, 92.5, 56), (1, 8, 46, 58), (2, 10, 15, 60), (3, 106, None, None)):
             turned, returned = banks[(6, 7, 5, 1)[t]], banks[(5, 1, 2, 3)[t]]
-            moved = moved_alone(t, WIDE, S, banks[(6, 7, 4, 0)[t]], 32 + 2 * t, wide)
+            moved = moved_alone(t, WIDE, S, banks[6 + t % HALF], 32 + 2 * t, wide)
             for x in range(WIDE // P):
                 cols = slice(x * P, (x + 1) * P)
                 for last, term in enumerate((moved[:, cols], picked[t, WIDE // P + x])):
                     nc.tensor.matmul(turned[:, cols], term, ident[:], start=not last, stop=bool(last), is_transpose=True)
             summed = placed(kb_summed, [P, WIDE], F32, f"summed_turned{t}")
             nc.scalar.copy(summed[:], turned[:])
-            clipped = placed(kb_clipped, [P, WIDE], F32, f"clipped{t}")
+            if kb_clipped is None:
+                clipped = blocks[1][:].rearrange("p u m -> p (u m)")[:, middle - WIDE : middle + WIDE].bitcast(F32)
+            else:
+                clipped = placed(kb_clipped, [P, WIDE], F32, f"clipped{t}")
             for x in range(WIDE // P):
                 cols = slice(x * P, (x + 1) * P)
                 block = WIDE // P + x
@@ -420,9 +428,6 @@ def tile_list_bike_route_rebalance_kernel(
                 back = placed(kb_back, [P, WIDE], F32, f"back{t}")
                 nc.scalar.copy(back[:], returned[:])
                 news.append(back)
-        blocks = [
-            placed(kb, [P, HALF, width * HALF], BF16, f"paired{kb}") for kb, width in ((12, BANK), (16, T - BANK))
-        ]
         back3 = blocks[0][:, 1, :].bitcast(F32)
         nc.scalar.copy(back3, banks[3][:])
 
@@ -435,11 +440,18 @@ def tile_list_bike_route_rebalance_kernel(
 
         def hand_out(t):
             nc.sync.dma_start(out_rows[:, t, :], pages[t][:])
-            for q, width in enumerate(PIECES):
-                x, cols = block_of(q)
+            if t < HALF:
+                edges = (0, BANK, GPSIMD_FROM, T)
+            elif t < PACK - 1:
+                edges = (*[start for start in starts if start <= BANK], T)
+            else:
+                edges = (*starts, T)
+            for m0, m1 in zip(edges, edges[1:]):
+                x = min(m0 // BANK, 1)
+                cols = slice(m0 - x * BANK, m1 - x * BANK)
                 dst = blocks[x][:, t // HALF, :].rearrange("p (m e) -> p m e", e=HALF)[:, cols, t % HALF]
-                src = pages[t][:, starts[q] : starts[q] + width]
-                if t < HALF and starts[q] >= GPSIMD_FROM:
+                src = pages[t][:, m0:m1]
+                if t < HALF and m0 >= GPSIMD_FROM:
                     nc.gpsimd.tensor_scalar(dst, src, 1.0, 1.0, ALU.mult, ALU.mult)
                 elif t >= HALF and x == 0:
                     nc.vector.tensor_copy(dst, src)

@@ -31,6 +31,7 @@ RUN = 4
 KB = 1024
 PIECES = (256, 256, 512, 256, 256, 256, 256)
 SCALAR_PIECES = 3
+STORES = (512, 1024, 1536, 1792, 2048)
 SCALAR_SHARE = 48
 GPSIMD_FROM = 1024
 LOWEST = -3.4028234663852886e38
@@ -78,18 +79,17 @@ def tile_list_bike_route_rebalance_kernel(
         def load_table(a):
             nc.sync.dma_start(table[a][:], tab_words[a].rearrange("p t i -> p (t i)").bitcast(I32))
 
-        def place_planes(a):
+        def place_planes():
             for q in range(QUADS):
-                first = 64 * a + 16 * q
                 nc.sync.dma_start(
-                    v_planes[32 * q : 32 * q + 4, a, :].bitcast(I32), v_plane[first : first + 16 : 4, :].bitcast(I32)
+                    v_planes[32 * q : 32 * q + 4, :, :].bitcast(I32), v_plane[32 * q : 32 * q + 32 : 4, :].bitcast(I32)
                 )
 
         nc.scalar.dma_start(lines[0:PASSES, :], gain.rearrange("(b r) -> b r", b=PASSES))
         nc.scalar.dma_start(lines[PASSES : PASSES + S // P, 0:P], docks.rearrange("(c p) -> c p", p=P))
         nc.sync.dma_start(offsets[:], offs)
         nc.sync.dma_start(flow_raw[:, 0, :], flow_words[0].bitcast(I32))
-        nc.sync.dma_start(tab_planes[0:P:4, :].bitcast(I32), tab_scales.rearrange("a q t -> (a q) t").bitcast(I32))
+        nc.sync.dma_start(tab_planes[0:P:4, :].bitcast(I32), tab_scales.rearrange("a q t -> q a t").bitcast(I32))
         nc.sync.dma_start(flow_raw[:, 1, :], flow_words[1].bitcast(I32))
         load_table(0)
         scale_rows_in = flow_scales.rearrange("a (q r) c -> r q a c", q=QUADS)
@@ -99,9 +99,8 @@ def tile_list_bike_route_rebalance_kernel(
         rows_f0 = flowT[0:GROUP, :].rearrange("(p i) c -> p i c", i=PACK)
         nc.sync.dma_start(raw_f0[:, 0:HALF, :], rows_f0[:, 0:HALF, :])
         nc.vector.tensor_copy(v_plane[:], tab_planes[:].indirect(offsets[:]))
-        place_planes(0)
+        place_planes()
         nc.sync.dma_start(raw_f0[:, HALF:PACK, :], rows_f0[:, HALF:PACK, :])
-        place_planes(1)
         load_table(1)
         raw_f10 = load_rows(16, "f10", flowT, 1, 0, GROUP)
         raw_f11 = load_rows(24, "f11", flowT, 1, GROUP, K)
@@ -292,7 +291,7 @@ def tile_list_bike_route_rebalance_kernel(
                 scaled_copy(m1 == P, dst[:, m0:m1], src[:, m0:m1], -1.0)
             quantise_weight(name, 0, PACK, dealt[:])
         gather_words(1, WIDE, WIDE + CHUNK, 52)
-        h0 = [h_by_vector(0, banks[0:2], (0, 2), 48, 63)]
+        h0 = [h_by_vector(0, banks[0:2], (0, 2), 48, None)]
         dealt_w = {(b, u): placed(kb, [P, part], BF16, f"dealt_w{b}{u}") for b, u, kb in ((0, 0, 64), (1, 0, 5))}
         cast_slots(raw_w[0][:], 0, dealt_w[0, 0][:], 1.0, True)
         quantise_weight("w0", 0, HALF, dealt_w[0, 0][:])
@@ -334,7 +333,7 @@ def tile_list_bike_route_rebalance_kernel(
             dealt_w[b, 1] = placed(kb, [P, part], BF16, f"dealt_w{b}1")
             cast_slots(raw_w[b][:], 1, dealt_w[b, 1][:], 1.0, False)
         bounded10 = squash_slots(1, banks[4:6], 28)
-        gather_words(1, WIDE + CHUNK, S, 6.5)
+        gather_words(1, WIDE + CHUNK, S, 50)
         for b in range(PASSES):
             quantise_weight(f"w{b}", HALF, PACK, dealt_w[b, 1][:], (4.5, 5.5)[b])
 
@@ -486,8 +485,8 @@ def tile_list_bike_route_rebalance_kernel(
                     weave_words(ahead)
             cols = slice(starts[q], starts[q] + width)
             nc.vector.quantize_mx(out=y_codes[:, cols].bitcast(FP8X4), scales=y_plane[:, cols], in_=y_woven[q][:])
-            if cols.stop % BANK == 0:
-                done_cols = slice(cols.stop - BANK, cols.stop)
+            if cols.stop in STORES:
+                done_cols = slice(max(edge for edge in (0, *STORES) if edge < cols.stop), cols.stop)
                 nc.sync.dma_start(words_out[:, done_cols], y_codes[:, done_cols])
         for r in range(4):
             queue = (nc.sync, nc.scalar)[r % 2]

@@ -276,21 +276,22 @@ def tile_list_bike_route_rebalance_kernel(
             flow_plane_raw[:].rearrange("p a (b m t) -> p (a b) m t", m=P, t=PACK),
         )
         part = HALF * GROUP
-        for name, raw, kb in (("f00", raw_f0[:, :, 0:GROUP], 48), ("f01", raw_f0[:, :, GROUP:K], 56)):
-            dealt = placed(kb, [P, PACK * GROUP], BF16, f"dealt_{name}")
-            for u in range(HALF):
-                cast_slots(raw, u, dealt[:, u * part : (u + 1) * part], -1.0, u == 1)
-            quantise_weight(name, 0, PACK, dealt[:])
-        gather_words(1, 0, CHUNK)
-        gather_words(1, CHUNK, WIDE)
-        for name, raw, kb in (("f10", raw_f10, 52), ("f11", raw_f11, 60)):
+
+        def prepare_flow(name, raw, kb, share):
             dealt = placed(kb, [P, PACK * GROUP], BF16, f"dealt_{name}")
             dst = dealt[:].rearrange("p (t m i) -> p m i t", t=PACK, i=PACK)
-            src = raw[:].rearrange("p i (m t) -> p m i t", t=PACK)
-            for m0, m1 in ((0, SCALAR_SHARE), (SCALAR_SHARE, P)) if name == "f10" else ((0, P),):
+            src = raw.rearrange("p i (m t) -> p m i t", t=PACK)
+            for m0, m1 in ((0, share), (share, P)) if share else ((0, P),):
                 scaled_copy(m1 == P, dst[:, m0:m1], src[:, m0:m1], -1.0)
             quantise_weight(name, 0, PACK, dealt[:])
-        gather_words(1, WIDE, WIDE + CHUNK, 52)
+
+        prepare_flow("f00", raw_f0[:, :, 0:GROUP], 48, SCALAR_SHARE)
+        prepare_flow("f01", raw_f0[:, :, GROUP:K], 56, SCALAR_SHARE)
+        gather_words(1, 0, CHUNK)
+        gather_words(1, CHUNK, WIDE + CHUNK)
+        prepare_flow("f10", raw_f10[:], 52, SCALAR_SHARE)
+        prepare_flow("f11", raw_f11[:], 60, 0)
+        gather_words(1, WIDE + CHUNK, S, 52)
         h0 = [h_by_vector(0, banks[0:2], (0, 2), 48, None)]
         dealt_w = {(b, u): placed(kb, [P, part], BF16, f"dealt_w{b}{u}") for b, u, kb in ((0, 0, 64), (1, 0, 5))}
         cast_slots(raw_w[0][:], 0, dealt_w[0, 0][:], 1.0, True)
@@ -315,6 +316,8 @@ def tile_list_bike_route_rebalance_kernel(
 
         def update_pair(u, j0, moved, sums, news):
             add_state(u * HALF, j0, j0 + CHUNK, moved[0], sums[0])
+            if (u, j0) == (0, 0):
+                quantise_weight("w1", HALF, PACK, dealt_w[1, 1][:], 73.5)
             width = CHUNK // len(moved[1])
             for s, piece in enumerate(moved[1]):
                 add_state(u * HALF + 1, j0 + s * width, j0 + (s + 1) * width, piece, sums[1][:, s * width : (s + 1) * width])
@@ -326,16 +329,14 @@ def tile_list_bike_route_rebalance_kernel(
                 put(u * HALF + k, j0, j0 + CHUNK, news[k])
 
         moved0 = moved_alone(0, 0, CHUNK, banks[6], 73, h0)
-        moved1 = [placed(kb, [P, P], F32, f"moved0_1_{s}")[:] for s, kb in enumerate((99.5, 74))]
+        moved1 = [placed(kb, [P, P], F32, f"moved0_1_{s}")[:] for s, kb in enumerate((99.5, 75))]
         moved_in_parts(1, banks[7], moved1)
         bounded11 = squash_pairs(1, banks[0:2], 12)
         for b, kb in enumerate((2.5, 95)):
             dealt_w[b, 1] = placed(kb, [P, part], BF16, f"dealt_w{b}1")
             cast_slots(raw_w[b][:], 1, dealt_w[b, 1][:], 1.0, False)
         bounded10 = squash_slots(1, banks[4:6], 28)
-        gather_words(1, WIDE + CHUNK, S, 50)
-        for b in range(PASSES):
-            quantise_weight(f"w{b}", HALF, PACK, dealt_w[b, 1][:], (4.5, 5.5)[b])
+        quantise_weight("w0", HALF, PACK, dealt_w[0, 1][:], 4.5)
 
         half = CHUNK * PACK
         woven1 = placed(100, [P, PASSES * half], BF16, "woven1")
@@ -351,10 +352,11 @@ def tile_list_bike_route_rebalance_kernel(
             for j in range(j0, j1, P):
                 picked[t, j // P] = tile[:, j - j0 : j - j0 + P]
 
+        pick(0, WIDE, WIDE + CHUNK, 6.5)
         news = [rooms2[:, 0, :], room(79, "new0_1")]
         update_pair(0, 0, [moved0[:], moved1], [rooms1[:, 2, :], room(90, "summed0_1")], news)
         weigh_on_gpsimd(bounded11, woven1[:, half:])
-        pick(0, WIDE, WIDE + CHUNK, 74)
+        pick(0, WIDE + CHUNK, S, 75)
         puts_of(0, 0, news)
         weigh_on_scalar(1, bounded10, 71.5, woven1[:, 0:half])
         moved2 = moved_alone(2, 0, CHUNK, banks[4], 80, h0)
@@ -373,13 +375,13 @@ def tile_list_bike_route_rebalance_kernel(
         products(2, 0, banks[4:6])
         bounded20 = squash_slots(2, banks[4:6], 26)
         moved = moved_pair(0, banks[5], 84, h1)
-        products(3, 1, banks[0:2])
-        bounded31 = squash_pairs(3, banks[0:2], 8.5)
+        products(3, 1, banks[6:8])
+        bounded31 = squash_pairs(3, banks[6:8], 8.5)
         woven_wide0 = placed(92, [P, 2 * half], BF16, "woven_wide0")
         weigh_on_scalar(2, bounded20, 56, woven_wide0[:, 0:half])
-        products(3, 0, banks[2:4])
-        moved.extend(moved_pair(1, banks[1], 86, h1))
-        weigh_on_scalar(3, squash_slots(3, banks[2:4], 20), 60, woven_wide0[:, half:])
+        products(3, 0, banks[4:6])
+        moved.extend(moved_pair(1, banks[7], 86, h1))
+        weigh_on_scalar(3, squash_slots(3, banks[4:6], 20), 60, woven_wide0[:, half:])
 
         news = [room(76, "new1_0"), room(79, "new1_1")]
         update_pair(0, CHUNK, [moved[0], [moved[1]]], [rooms2[:, 2, :], room(82, "summed1_1")], news)
@@ -388,8 +390,7 @@ def tile_list_bike_route_rebalance_kernel(
         pick(2, WIDE + CHUNK, S, 84)
 
         wide = [quantise_h("wide0", woven_wide0[:], WIDE, 76), quantise_h("wide1", woven_wide1[:], WIDE)]
-        pick(0, WIDE + CHUNK, S, 95.5)
-        sums = placed(92.5, [P, HALF, CHUNK], F32, "summed1_23")
+        sums = placed(95, [P, HALF, CHUNK], F32, "summed1_23")
         news1 = [room(82, "new1_2"), room(83, "new1_3")]
         update_pair(1, CHUNK, [moved[2], [moved[3]]], [sums[:, k, :] for k in range(HALF)], news1)
         for t, kb in ((1, 85), (3, 87)):
@@ -401,7 +402,7 @@ def tile_list_bike_route_rebalance_kernel(
         ]
         middle = (T - BANK) * HALF
         news = []
-        for t, kb_summed, kb_clipped, kb_back in ((0, 0, 92.5, 56), (1, 8, 46, 58), (2, 10, 15, 60), (3, 106, None, None)):
+        for t, kb_summed, kb_clipped, kb_back in ((0, 0, 96, 56), (1, 8, 46, 58), (2, 10, 15, 60), (3, 106, None, None)):
             turned, returned = banks[(6, 7, 5, 1)[t]], banks[(5, 1, 2, 3)[t]]
             moved = moved_alone(t, WIDE, S, banks[6 + t % HALF], 32 + 2 * t, wide)
             for x in range(WIDE // P):

@@ -371,7 +371,7 @@ def tile_list_bike_route_rebalance_kernel(
         update_pair(1, 0, [moved2[:], moved3], [rooms2[:, 0, :], room(103, "summed0_3")], news)
         weigh_on_gpsimd(bounded21, woven_wide1[:, 0:half])
         puts_of(1, 0, news)
-        pick(2, WIDE, WIDE + CHUNK, 90)
+        pick(2, WIDE, WIDE + P, 90)
         products(2, 0, banks[4:6])
         bounded20 = squash_slots(2, banks[4:6], 26)
         moved = moved_pair(0, banks[5], 84, h1)
@@ -387,14 +387,14 @@ def tile_list_bike_route_rebalance_kernel(
         update_pair(0, CHUNK, [moved[0], [moved[1]]], [rooms2[:, 2, :], room(82, "summed1_1")], news)
         weigh_on_gpsimd(bounded31, woven_wide1[:, half:])
         puts_of(0, CHUNK, news)
-        pick(2, WIDE + CHUNK, S, 84)
+        pick(2, WIDE + P, WIDE + CHUNK, 84)
 
         wide = [quantise_h("wide0", woven_wide0[:], WIDE, 76), quantise_h("wide1", woven_wide1[:], WIDE)]
         sums = placed(95, [P, HALF, CHUNK], F32, "summed1_23")
         news1 = [room(82, "new1_2"), room(83, "new1_3")]
         update_pair(1, CHUNK, [moved[2], [moved[3]]], [sums[:, k, :] for k in range(HALF)], news1)
-        for t, kb in ((1, 85), (3, 87)):
-            pick(t, WIDE, S, kb)
+        for t, j0, kb in ((1, WIDE, 85), (2, WIDE + CHUNK, 94.25), (3, WIDE, 87)):
+            pick(t, j0, S, kb)
         puts_of(1, CHUNK, news1)
 
         blocks = [

@@ -121,6 +121,9 @@ def tile_list_bike_route_rebalance_kernel(
             nc.tensor.transpose(banks[6][:, c * P : (c + 1) * P], docks_rows[:, c : c + 1].to_broadcast([P, P]), ident[:])
         nc.scalar.copy(limit[:], banks[6][:])
 
+        gain_row = held([P, CHUNK * PACK], F32, "gain_row")
+        nc.scalar.copy(gain_row[:].rearrange("p (j t) -> p j t", t=PACK), gain_sb[:, 1:2, :].to_broadcast([P, CHUNK, PACK]))
+
         quantised = {}
 
         def scaled_copy(on_vector, dst, src, sign):
@@ -128,10 +131,6 @@ def tile_list_bike_route_rebalance_kernel(
                 nc.vector.tensor_scalar(dst, src, sign, None, ALU.mult)
             else:
                 nc.scalar.activation(dst, src, ACT.Copy, scale=sign)
-
-        def cast_slots(raw, u, dealt, sign, on_vector):
-            src = raw.rearrange("p i (m t) -> p m i t", t=PACK)[:, :, :, u * HALF : (u + 1) * HALF]
-            scaled_copy(on_vector, dealt.rearrange("p (t m i) -> p m i t", t=HALF, i=PACK), src, sign)
 
         def quantise_weight(name, t0, t1, dealt, kb=None):
             shape = [P, (t1 - t0) * P]
@@ -217,23 +216,22 @@ def tile_list_bike_route_rebalance_kernel(
                     rounded[:, :, s * P : (s + 1) * P].rearrange("p t (c i) -> p c t i", i=RUN),
                 )
 
-        def squash_pairs(c, pair, kb):
-            bounded = placed(kb, [P, HALF, CHUNK * HALF], F32, f"bounded{c}1")
-            for u in range(HALF):
+        def woven_products(c, pair):
+            for s in range(CHUNK // P):
+                imbalance(pair[s], 1, range(PACK), c * CHUNK + s * P, P)
+
+        def squash_woven(c, pair, kb):
+            bounded = placed(kb, [P, CHUNK * PACK], F32, f"bounded{c}1")
+            for s in range(CHUNK // P):
                 nc.scalar.activation(
-                    bounded[:, u, :].rearrange("p (j e) -> p j e", e=HALF),
-                    pair[u][:].rearrange("p (e j) -> p j e", e=HALF),
+                    bounded[:, s * BANK : (s + 1) * BANK].rearrange("p (j t) -> p j t", t=PACK),
+                    pair[s][:].rearrange("p (t j) -> p j t", t=PACK),
                     ACT.Tanh,
                 )
             return bounded
 
         def weigh_on_gpsimd(bounded, woven):
-            nc.gpsimd.tensor_tensor(
-                woven.rearrange("p (j u e) -> p j u e", u=HALF, e=HALF),
-                bounded[:].rearrange("p u (j e) -> p j u e", e=HALF),
-                gain_sb[:, 1:2, :].rearrange("p o (u e) -> p o u e", e=HALF).to_broadcast([P, CHUNK, HALF, HALF]),
-                ALU.mult,
-            )
+            nc.gpsimd.tensor_tensor(woven, bounded[:], gain_row[:], ALU.mult)
 
         def move_product(out, t, h):
             for b in range(PASSES):
@@ -275,32 +273,30 @@ def tile_list_bike_route_rebalance_kernel(
             flow_plane[:].rearrange("p g t m -> p g m t"),
             flow_plane_raw[:].rearrange("p a (b m t) -> p (a b) m t", m=P, t=PACK),
         )
-        part = HALF * GROUP
 
-        def prepare_flow(name, raw, kb, share):
+        def prepare(name, raw, kb, sign, share, parts=1):
             dealt = placed(kb, [P, PACK * GROUP], BF16, f"dealt_{name}")
             dst = dealt[:].rearrange("p (t m i) -> p m i t", t=PACK, i=PACK)
             src = raw.rearrange("p i (m t) -> p m i t", t=PACK)
             for m0, m1 in ((0, share), (share, P)) if share else ((0, P),):
-                scaled_copy(m1 == P, dst[:, m0:m1], src[:, m0:m1], -1.0)
-            quantise_weight(name, 0, PACK, dealt[:])
+                scaled_copy(m1 == P, dst[:, m0:m1], src[:, m0:m1], sign)
+            slots = PACK // parts
+            for t0 in range(0, PACK, slots):
+                quantise_weight(name, t0, t0 + slots, dealt[:, t0 * GROUP : (t0 + slots) * GROUP])
 
-        prepare_flow("f00", raw_f0[:, :, 0:GROUP], 48, SCALAR_SHARE)
-        prepare_flow("f01", raw_f0[:, :, GROUP:K], 56, SCALAR_SHARE)
+        prepare("f00", raw_f0[:, :, 0:GROUP], 48, -1.0, SCALAR_SHARE)
+        prepare("f01", raw_f0[:, :, GROUP:K], 56, -1.0, SCALAR_SHARE)
         gather_words(1, 0, CHUNK)
         gather_words(1, CHUNK, WIDE + CHUNK)
-        prepare_flow("f10", raw_f10[:], 52, SCALAR_SHARE)
-        prepare_flow("f11", raw_f11[:], 60, 0)
+        prepare("f10", raw_f10[:], 52, -1.0, SCALAR_SHARE)
+        prepare("f11", raw_f11[:], 60, -1.0, 0)
         gather_words(1, WIDE + CHUNK, S, 52)
         h0 = [h_by_vector(0, banks[0:2], (0, 2), 48, None)]
-        dealt_w = {(b, u): placed(kb, [P, part], BF16, f"dealt_w{b}{u}") for b, u, kb in ((0, 0, 64), (1, 0, 5))}
-        cast_slots(raw_w[0][:], 0, dealt_w[0, 0][:], 1.0, True)
-        quantise_weight("w0", 0, HALF, dealt_w[0, 0][:])
-        h0.append(h_by_vector(1, banks[2:4], (4, 66), 50, None))
-        cast_slots(raw_w[1][:], 0, dealt_w[1, 0][:], 1.0, True)
-        quantise_weight("w1", 0, HALF, dealt_w[1, 0][:])
+        prepare("w0", raw_w[0][:], 64, 1.0, SCALAR_SHARE)
+        h0.append(h_by_vector(1, banks[2:4], (4, 68), 50, None))
+        prepare("w1", raw_w[1][:], 3.5, 1.0, SCALAR_SHARE, 2)
         products(1, 0, banks[4:6])
-        products(1, 1, banks[0:2])
+        woven_products(1, banks[0:2])
 
         def moved_in_parts(t, bank, parts):
             move_product(bank[:, 0:CHUNK], t, h0)
@@ -316,8 +312,6 @@ def tile_list_bike_route_rebalance_kernel(
 
         def update_pair(u, j0, moved, sums, news):
             add_state(u * HALF, j0, j0 + CHUNK, moved[0], sums[0])
-            if (u, j0) == (0, 0):
-                quantise_weight("w1", HALF, PACK, dealt_w[1, 1][:], 73.5)
             width = CHUNK // len(moved[1])
             for s, piece in enumerate(moved[1]):
                 add_state(u * HALF + 1, j0 + s * width, j0 + (s + 1) * width, piece, sums[1][:, s * width : (s + 1) * width])
@@ -331,12 +325,8 @@ def tile_list_bike_route_rebalance_kernel(
         moved0 = moved_alone(0, 0, CHUNK, banks[6], 73, h0)
         moved1 = [placed(kb, [P, P], F32, f"moved0_1_{s}")[:] for s, kb in enumerate((99.5, 75))]
         moved_in_parts(1, banks[7], moved1)
-        bounded11 = squash_pairs(1, banks[0:2], 12)
-        for b, kb in enumerate((2.5, 95)):
-            dealt_w[b, 1] = placed(kb, [P, part], BF16, f"dealt_w{b}1")
-            cast_slots(raw_w[b][:], 1, dealt_w[b, 1][:], 1.0, False)
+        bounded11 = squash_woven(1, banks[0:2], 12)
         bounded10 = squash_slots(1, banks[4:6], 28)
-        quantise_weight("w0", HALF, PACK, dealt_w[0, 1][:], 4.5)
 
         half = CHUNK * PACK
         woven1 = placed(100, [P, PASSES * half], BF16, "woven1")
@@ -352,18 +342,17 @@ def tile_list_bike_route_rebalance_kernel(
             for j in range(j0, j1, P):
                 picked[t, j // P] = tile[:, j - j0 : j - j0 + P]
 
-        pick(0, WIDE, WIDE + CHUNK, 6.5)
+        pick(0, WIDE, S, 6.5)
         news = [rooms2[:, 0, :], room(79, "new0_1")]
         update_pair(0, 0, [moved0[:], moved1], [rooms1[:, 2, :], room(90, "summed0_1")], news)
         weigh_on_gpsimd(bounded11, woven1[:, half:])
-        pick(0, WIDE + CHUNK, S, 75)
         puts_of(0, 0, news)
         weigh_on_scalar(1, bounded10, 71.5, woven1[:, 0:half])
         moved2 = moved_alone(2, 0, CHUNK, banks[4], 80, h0)
         moved3 = [rooms2[:, 2, 0:P], placed(81, [P, P], F32, "moved0_3_1")[:]]
         moved_in_parts(3, banks[5], moved3)
-        products(2, 1, banks[6:8])
-        bounded21 = squash_pairs(2, banks[6:8], 30)
+        woven_products(2, banks[6:8])
+        bounded21 = squash_woven(2, banks[6:8], 30)
 
         codes, plane = quantise_h("h1", woven1[:], PASSES * CHUNK)
         h1 = [(codes[:, b * CHUNK : (b + 1) * CHUNK], plane[:, b * CHUNK : (b + 1) * CHUNK]) for b in range(PASSES)]
@@ -371,12 +360,11 @@ def tile_list_bike_route_rebalance_kernel(
         update_pair(1, 0, [moved2[:], moved3], [rooms2[:, 0, :], room(103, "summed0_3")], news)
         weigh_on_gpsimd(bounded21, woven_wide1[:, 0:half])
         puts_of(1, 0, news)
-        pick(2, WIDE, WIDE + P, 90)
         products(2, 0, banks[4:6])
         bounded20 = squash_slots(2, banks[4:6], 26)
         moved = moved_pair(0, banks[5], 84, h1)
-        products(3, 1, banks[6:8])
-        bounded31 = squash_pairs(3, banks[6:8], 8.5)
+        woven_products(3, banks[6:8])
+        bounded31 = squash_woven(3, banks[6:8], 8.5)
         woven_wide0 = placed(92, [P, 2 * half], BF16, "woven_wide0")
         weigh_on_scalar(2, bounded20, 56, woven_wide0[:, 0:half])
         products(3, 0, banks[4:6])
@@ -387,14 +375,13 @@ def tile_list_bike_route_rebalance_kernel(
         update_pair(0, CHUNK, [moved[0], [moved[1]]], [rooms2[:, 2, :], room(82, "summed1_1")], news)
         weigh_on_gpsimd(bounded31, woven_wide1[:, half:])
         puts_of(0, CHUNK, news)
-        pick(2, WIDE + P, WIDE + CHUNK, 84)
 
         wide = [quantise_h("wide0", woven_wide0[:], WIDE, 76), quantise_h("wide1", woven_wide1[:], WIDE)]
         sums = placed(95, [P, HALF, CHUNK], F32, "summed1_23")
         news1 = [room(82, "new1_2"), room(83, "new1_3")]
         update_pair(1, CHUNK, [moved[2], [moved[3]]], [sums[:, k, :] for k in range(HALF)], news1)
-        for t, j0, kb in ((1, WIDE, 85), (2, WIDE + CHUNK, 94.25), (3, WIDE, 87)):
-            pick(t, j0, S, kb)
+        for t, kb in ((1, 85), (2, 93.25), (3, 87)):
+            pick(t, WIDE, S, kb)
         puts_of(1, CHUNK, news1)
 
         blocks = [

@@ -346,6 +346,7 @@ def tile_list_bike_route_rebalance_kernel(
         news = [rooms2[:, 0, :], room(79, "new0_1")]
         update_pair(0, 0, [moved0[:], moved1], [rooms1[:, 2, :], room(90, "summed0_1")], news)
         weigh_on_gpsimd(bounded11, woven1[:, half:])
+        pick(1, WIDE, WIDE + P, 75)
         puts_of(0, 0, news)
         weigh_on_scalar(1, bounded10, 71.5, woven1[:, 0:half])
         moved2 = moved_alone(2, 0, CHUNK, banks[4], 80, h0)
@@ -360,6 +361,7 @@ def tile_list_bike_route_rebalance_kernel(
         update_pair(1, 0, [moved2[:], moved3], [rooms2[:, 0, :], room(103, "summed0_3")], news)
         weigh_on_gpsimd(bounded21, woven_wide1[:, 0:half])
         puts_of(1, 0, news)
+        pick(2, WIDE, WIDE + P, 90)
         products(2, 0, banks[4:6])
         bounded20 = squash_slots(2, banks[4:6], 26)
         moved = moved_pair(0, banks[5], 84, h1)
@@ -375,13 +377,14 @@ def tile_list_bike_route_rebalance_kernel(
         update_pair(0, CHUNK, [moved[0], [moved[1]]], [rooms2[:, 2, :], room(82, "summed1_1")], news)
         weigh_on_gpsimd(bounded31, woven_wide1[:, half:])
         puts_of(0, CHUNK, news)
+        pick(2, WIDE + P, WIDE + CHUNK, 84)
 
         wide = [quantise_h("wide0", woven_wide0[:], WIDE, 76), quantise_h("wide1", woven_wide1[:], WIDE)]
         sums = placed(95, [P, HALF, CHUNK], F32, "summed1_23")
         news1 = [room(82, "new1_2"), room(83, "new1_3")]
         update_pair(1, CHUNK, [moved[2], [moved[3]]], [sums[:, k, :] for k in range(HALF)], news1)
-        for t, kb in ((1, 85), (2, 93.25), (3, 87)):
-            pick(t, WIDE, S, kb)
+        for t, j0, kb in ((1, WIDE + P, 85), (2, WIDE + CHUNK, 94.25), (3, WIDE, 87)):
+            pick(t, j0, S, kb)
         puts_of(1, CHUNK, news1)
 
         blocks = [

from contextlib import ExitStack

import concourse.mybir as mybir
from concourse.masks import make_identity

K, N, T, S = 1024, 512, 2048, 1024
FLOPS = 2 * K * K * S * 2 + 2 * K * N * S

F32 = mybir.dt.float32
BF16 = mybir.dt.bfloat16
I32 = mybir.dt.int32
U32 = mybir.dt.uint32
U16 = mybir.dt.uint16
U8 = mybir.dt.uint8
FP8X4 = mybir.dt.float8_e4m3fn_x4
FP4X4 = mybir.dt.float4_e2m1fn_x4
ACT = mybir.ActivationFunctionType
ALU = mybir.AluOpType

P = 128
PACK = 4
HALF = PACK // 2
GROUP = P * PACK
PASSES = K // GROUP
QUADS = 4
BANK = 512
CHUNK = 256
WIDE = 2 * CHUNK
STRIPE = 16
RUN = 4
KB = 1024
PIECES = (256, 256, 512, 256, 256, 256, 256)
SCALAR_PIECES = 3
STORES = (512, 1024, 1536, 1792, 2048)
SCALAR_SHARE = 48
GPSIMD_FROM = 1024
LOWEST = -3.4028234663852886e38
ORDER = ((0, True), (0, False), (1, True), (1, False))


def tile_list_bike_route_rebalance_kernel(
    tc, tab_words, tab_scales, offs, flow_words, flow_scales, flowT, gain, wm, gT, docks, out_0, out_1, out_2
):
    nc = tc.nc
    with ExitStack() as ctx:
        keep = ctx.enter_context(tc.tile_pool(name="keep", bufs=1))
        work = ctx.enter_context(tc.tile_pool(name="work", bufs=1))
        psum = ctx.enter_context(tc.psum_pool(name="psum", bufs=1))

        def held(shape, dtype, name):
            return keep.tile(shape, dtype, name=name, align_bytes=64)

        def placed(kb, shape, dtype, name):
            return work.tile(shape, dtype, name=name, align_bytes=64, offset=int(kb * KB))

        offsets = keep.tile([P, S // STRIPE], U16, name="offsets")
        tab_planes = held([P, T], U8, "tab_planes")
        v_planes = held([P, PASSES, S], U8, "v_planes")
        flow_plane_raw = held([P, PASSES, K], U8, "flow_plane_raw")
        nc.vector.memset(tab_planes[:].bitcast(I32), 0)
        nc.vector.memset(flow_plane_raw[:].bitcast(I32), 0)
        nc.vector.memset(v_planes[:].bitcast(I32), 0)
        lines = held([P, GROUP], F32, "lines")
        nc.gpsimd.memset(lines[:], 0.0)
        ident = held([P, P], F32, "ident")
        make_identity(nc, ident[:])
        docks_rows = held([P, S // P], F32, "docks_rows")
        gain_sb = held([P, PASSES, PACK], F32, "gain_sb")
        table = [held([P, T], I32, f"table{a}") for a in range(PASSES)]
        flow_raw = held([P, PASSES, K // 2], I32, "flow_raw")
        pages = [held([P, T], F32, f"page{t}") for t in range(PACK)]
        v_plane = held([P, S], U8, "v_plane")

        def load_rows(kb, name, w, a, c0, c1):
            raw = placed(kb, [P, PACK, c1 - c0], F32, f"raw_{name}")
            nc.sync.dma_start(raw[:], w[a * GROUP : (a + 1) * GROUP, c0:c1].rearrange("(p i) c -> p i c", i=PACK))
            return raw

        def load_table(a):
            nc.sync.dma_start(table[a][:], tab_words[a].rearrange("p t i -> p (t i)").bitcast(I32))

        def place_planes():
            for q in range(QUADS):
                nc.sync.dma_start(
                    v_planes[32 * q : 32 * q + 4, :, :].bitcast(I32), v_plane[32 * q : 32 * q + 32 : 4, :].bitcast(I32)
                )

        nc.scalar.dma_start(lines[0:PASSES, :], gain.rearrange("(b r) -> b r", b=PASSES))
        nc.scalar.dma_start(lines[PASSES : PASSES + S // P, 0:P], docks.rearrange("(c p) -> c p", p=P))
        nc.sync.dma_start(offsets[:], offs)
        nc.sync.dma_start(flow_raw[:, 0, :], flow_words[0].bitcast(I32))
        nc.sync.dma_start(tab_planes[0:P:4, :].bitcast(I32), tab_scales.rearrange("a q t -> q a t").bitcast(I32))
        nc.sync.dma_start(flow_raw[:, 1, :], flow_words[1].bitcast(I32))
        load_table(0)
        scale_rows_in = flow_scales.rearrange("a (q r) c -> r q a c", q=QUADS)
        for r in range(4):
            nc.sync.dma_start(flow_plane_raw[r:P:32, :, :].bitcast(I32), scale_rows_in[r].bitcast(I32))
        raw_f0 = placed(0, [P, PACK, K], F32, "raw_f0")
        rows_f0 = flowT[0:GROUP, :].rearrange("(p i) c -> p i c", i=PACK)
        nc.sync.dma_start(raw_f0[:, 0:HALF, :], rows_f0[:, 0:HALF, :])
        nc.vector.tensor_copy(v_plane[:], tab_planes[:].indirect(offsets[:]))
        place_planes()
        nc.sync.dma_start(raw_f0[:, HALF:PACK, :], rows_f0[:, HALF:PACK, :])
        load_table(1)
        raw_f10 = load_rows(16, "f10", flowT, 1, 0, GROUP)
        raw_f11 = load_rows(24, "f11", flowT, 1, GROUP, K)
        raw_w = [load_rows(32 + 8 * b, f"w{b}", wm, b, 0, N) for b in range(PASSES)]
        gT_rows = gT.rearrange("(p t) m -> p t m", t=PACK)
        for t in range(PACK):
            nc.sync.dma_start(pages[t][:], gT_rows[:, t, :])

        banks = [psum.tile([P, BANK], F32, name=f"bank{x}") for x in range(8)]

        for t in range(PACK):
            nc.tensor.transpose(banks[4][:, t * P : (t + 1) * P], lines[:, t:GROUP:PACK], ident[:])
        nc.tensor.transpose(banks[5][:, 0:P], lines[:, 0:P], ident[:])
        nc.scalar.copy(docks_rows[:], banks[5][:, PASSES : PASSES + S // P])
        nc.scalar.copy(gain_sb[:], banks[4][:].rearrange("p (t r) -> p r t", t=PACK)[:, 0:PASSES, :])
        limit = held([P, WIDE], F32, "limit")
        for c in range(WIDE // P):
            nc.tensor.transpose(banks[6][:, c * P : (c + 1) * P], docks_rows[:, c : c + 1].to_broadcast([P, P]), ident[:])
        nc.scalar.copy(limit[:], banks[6][:])

        gain_row = held([P, CHUNK * PACK], F32, "gain_row")
        nc.scalar.copy(gain_row[:].rearrange("p (j t) -> p j t", t=PACK), gain_sb[:, 1:2, :].to_broadcast([P, CHUNK, PACK]))

        quantised = {}

        def scaled_copy(on_vector, dst, src, sign):
            if on_vector:
                nc.vector.tensor_scalar(dst, src, sign, None, ALU.mult)
            else:
                nc.scalar.activation(dst, src, ACT.Copy, scale=sign)

        def quantise_weight(name, t0, t1, dealt, kb=None):
            shape = [P, (t1 - t0) * P]
            codes = held(shape, U32, f"{name}_codes{t0}") if kb is None else placed(kb, shape, U32, f"{name}_codes{t0}")
            plane = held([P, (t1 - t0) * P], U8, f"{name}_plane{t0}")
            nc.vector.quantize_mx(out=codes[:].bitcast(FP8X4), scales=plane[:], in_=dealt)
            for t in range(t0, t1):
                cols = slice((t - t0) * P, (t - t0 + 1) * P)
                quantised[name, t] = (codes[:, cols].bitcast(FP8X4), plane[:, cols])

        v_words = {}
        flow_codes = held([P, PASSES * PASSES, PACK, 2 * P], U8, "flow_codes")
        flow_plane = held([P, PASSES * PASSES, PACK, P], U8, "flow_plane")

        def listed(j0, j1):
            return offsets[:, j0 // STRIPE : j1 // STRIPE]

        def gather_words(a, j0, j1, kb=None):
            shape = [P, j1 - j0]
            words = held(shape, U32, f"v_words{a}_{j0}") if kb is None else placed(kb, shape, U32, f"v_words{a}_{j0}")
            nc.vector.tensor_copy(words[:], table[a][:].bitcast(U32).indirect(listed(j0, j1)))
            for j in range(j0, j1, CHUNK):
                v_words[a, j // CHUNK] = words[:, j - j0 : j - j0 + CHUNK]

        def imbalance(bank, b, slots, j0, width):
            steps = [(a, packed, t) for a, packed in ORDER for t in slots]
            for n, (a, packed, t) in enumerate(steps):
                if packed:
                    lhs = flow_codes[:, a * PASSES + b, t, :].bitcast(FP4X4)
                    lhs_plane = flow_plane[:, a * PASSES + b, t, :]
                else:
                    lhs, lhs_plane = quantised[f"f{a}{b}", t]
                col = (t - slots[0]) * width
                nc.tensor.matmul_mx(
                    out=bank[:, col : col + width],
                    lhsT=lhs,
                    lhsT_scale=lhs_plane,
                    rhs=v_words[a, j0 // CHUNK][:, j0 % CHUNK : j0 % CHUNK + width].bitcast(FP8X4),
                    rhs_scale=v_planes[:, a, j0 : j0 + width],
                    start=(n == 0),
                    stop=(n == len(steps) - 1),
                )

        def quantise_h(name, woven, width, kb=None):
            codes = held([P, width], U32, f"codes_{name}") if kb is None else placed(kb, [P, width], U32, f"codes_{name}")
            plane = held([P, width], U8, f"plane_{name}")
            nc.vector.quantize_mx(out=codes[:].bitcast(FP8X4), scales=plane[:], in_=woven)
            return codes[:], plane[:]

        def h_by_vector(b, pair, kb_bounded, kb_woven, kb_codes):
            woven = placed(kb_woven, [P, CHUNK * PACK], BF16, f"woven0{b}")
            for s in range(CHUNK // P):
                imbalance(pair[s], b, range(PACK), s * P, P)
                bounded = placed(kb_bounded[s], [P, P, PACK], F32, f"bounded0{b}{s}")
                nc.scalar.activation(bounded[:], pair[s][:].rearrange("p (t j) -> p j t", t=PACK), ACT.Tanh)
                nc.vector.tensor_tensor(
                    woven[:, s * BANK : (s + 1) * BANK].rearrange("p (j t) -> p j t", t=PACK),
                    bounded[:],
                    gain_sb[:, b : b + 1, :].to_broadcast([P, P, PACK]),
                    ALU.mult,
                )
            return quantise_h(f"h0{b}", woven[:], CHUNK, kb_codes)

        def products(c, b, pair):
            for u in range(HALF):
                imbalance(pair[u], b, range(u * HALF, (u + 1) * HALF), c * CHUNK, CHUNK)

        def squash_slots(c, pair, kb):
            bounded = placed(kb, [P, PACK, CHUNK], F32, f"bounded{c}0")
            for u in range(HALF):
                nc.scalar.activation(
                    bounded[:, u * HALF : (u + 1) * HALF, :].rearrange("p t j -> p (t j)"), pair[u][:], ACT.Tanh
                )
            return bounded

        def weigh_on_scalar(c, bounded, kb_rounded, woven):
            rounded = placed(kb_rounded, [P, PACK, CHUNK], BF16, f"rounded{c}0")
            for t in range(PACK):
                nc.scalar.activation(rounded[:, t, :], bounded[:, t, :], ACT.Copy, scale=gain_sb[:, 0, t : t + 1])
            for s in range(CHUNK // P):
                nc.scalar.copy(
                    woven[:, s * BANK : (s + 1) * BANK].rearrange("p (c i t) -> p c t i", i=RUN, t=PACK),
                    rounded[:, :, s * P : (s + 1) * P].rearrange("p t (c i) -> p c t i", i=RUN),
                )

        def woven_products(c, pair):
            for s in range(CHUNK // P):
                imbalance(pair[s], 1, range(PACK), c * CHUNK + s * P, P)

        def squash_woven(c, pair, kb):
            bounded = placed(kb, [P, CHUNK * PACK], F32, f"bounded{c}1")
            for s in range(CHUNK // P):
                nc.scalar.activation(
                    bounded[:, s * BANK : (s + 1) * BANK].rearrange("p (j t) -> p j t", t=PACK),
                    pair[s][:].rearrange("p (t j) -> p j t", t=PACK),
                    ACT.Tanh,
                )
            return bounded

        def weigh_on_gpsimd(bounded, woven):
            nc.gpsimd.tensor_tensor(woven, bounded[:], gain_row[:], ALU.mult)

        def move_product(out, t, h):
            for b in range(PASSES):
                nc.tensor.matmul_mx(
                    out=out,
                    lhsT=quantised[f"w{b}", t][0],
                    lhsT_scale=quantised[f"w{b}", t][1],
                    rhs=h[b][0].bitcast(FP8X4),
                    rhs_scale=h[b][1],
                    start=(b == 0),
                    stop=(b == PASSES - 1),
                )

        def moved_alone(t, j0, j1, bank, kb, h):
            move_product(bank[:, 0 : j1 - j0], t, h)
            moved = placed(kb, [P, j1 - j0], F32, f"moved{j0}_{t}")
            nc.scalar.copy(moved[:], bank[:, 0 : j1 - j0])
            return moved

        def room(kb, name):
            return placed(kb, [P, CHUNK], F32, name)[:]

        def add_state(t, j0, j1, moved, summed):
            nc.vector.tensor_tensor(summed, pages[t][:].indirect(listed(j0, j1)), moved, ALU.add)

        def clip(j0, summed, new):
            nc.vector.tensor_tensor(new, summed, limit[:, j0 : j0 + CHUNK], ALU.min)

        def put(t, j0, j1, new):
            nc.vector.tensor_copy(pages[t][:].indirect(listed(j0, j1)), new)

        for a in range(PASSES):
            nc.scalar.copy(
                flow_codes[:, a * PASSES : (a + 1) * PASSES].bitcast(U16).rearrange("p g t m -> p g m t"),
                flow_raw[:, a, :].bitcast(U16).rearrange("p (b m t) -> p b m t", m=P, t=PACK),
            )
        gather_words(0, 0, S)
        nc.vector.tensor_copy(
            flow_plane[:].rearrange("p g t m -> p g m t"),
            flow_plane_raw[:].rearrange("p a (b m t) -> p (a b) m t", m=P, t=PACK),
        )

        def prepare(name, raw, kb, sign, share, parts=1):
            dealt = placed(kb, [P, PACK * GROUP], BF16, f"dealt_{name}")
            dst = dealt[:].rearrange("p (t m i) -> p m i t", t=PACK, i=PACK)
            src = raw.rearrange("p i (m t) -> p m i t", t=PACK)
            for m0, m1 in ((0, share), (share, P)) if share else ((0, P),):
                scaled_copy(m1 == P, dst[:, m0:m1], src[:, m0:m1], sign)
            slots = PACK // parts
            for t0 in range(0, PACK, slots):
                quantise_weight(name, t0, t0 + slots, dealt[:, t0 * GROUP : (t0 + slots) * GROUP])

        prepare("f00", raw_f0[:, :, 0:GROUP], 48, -1.0, SCALAR_SHARE)
        prepare("f01", raw_f0[:, :, GROUP:K], 56, -1.0, SCALAR_SHARE)
        gather_words(1, 0, CHUNK)
        gather_words(1, CHUNK, WIDE + CHUNK)
        prepare("f10", raw_f10[:], 52, -1.0, SCALAR_SHARE)
        prepare("f11", raw_f11[:], 60, -1.0, 0)
        gather_words(1, WIDE + CHUNK, S, 52)
        h0 = [h_by_vector(0, banks[0:2], (0, 2), 48, None)]
        prepare("w0", raw_w[0][:], 64, 1.0, SCALAR_SHARE)
        h0.append(h_by_vector(1, banks[2:4], (4, 68), 50, None))
        prepare("w1", raw_w[1][:], 3.5, 1.0, SCALAR_SHARE, 2)
        products(1, 0, banks[4:6])
        woven_products(1, banks[0:2])

        def moved_in_parts(t, bank, parts):
            move_product(bank[:, 0:CHUNK], t, h0)
            for s, piece in enumerate(parts):
                nc.scalar.copy(piece, bank[:, s * P : (s + 1) * P])

        def moved_pair(u, bank, kb, h):
            for k in range(HALF):
                move_product(bank[:, k * CHUNK : (k + 1) * CHUNK], u * HALF + k, h)
            both = placed(kb, [P, HALF, CHUNK], F32, f"moved1_{u}")
            nc.scalar.copy(both[:].rearrange("p k j -> p (k j)"), bank[:])
            return [both[:, k, :] for k in range(HALF)]

        def update_pair(u, j0, moved, sums, news):
            add_state(u * HALF, j0, j0 + CHUNK, moved[0], sums[0])
            width = CHUNK // len(moved[1])
            for s, piece in enumerate(moved[1]):
                add_state(u * HALF + 1, j0 + s * width, j0 + (s + 1) * width, piece, sums[1][:, s * width : (s + 1) * width])
            for k in range(HALF):
                clip(j0, sums[k], news[k])

        def puts_of(u, j0, news):
            for k in range(HALF):
                put(u * HALF + k, j0, j0 + CHUNK, news[k])

        moved0 = moved_alone(0, 0, CHUNK, banks[6], 73, h0)
        moved1 = [placed(kb, [P, P], F32, f"moved0_1_{s}")[:] for s, kb in enumerate((99.5, 75))]
        moved_in_parts(1, banks[7], moved1)
        bounded11 = squash_woven(1, banks[0:2], 12)
        bounded10 = squash_slots(1, banks[4:6], 28)

        half = CHUNK * PACK
        woven1 = placed(100, [P, PASSES * half], BF16, "woven1")
        rooms1 = woven1[:].bitcast(F32).rearrange("p (x j) -> p x j", j=CHUNK)
        woven_wide1 = placed(96, [P, 2 * half], BF16, "woven_wide1")
        rooms2 = woven_wide1[:].bitcast(F32).rearrange("p (x j) -> p x j", j=CHUNK)

        picked = {}

        def pick(t, j0, j1, kb):
            tile = placed(kb, [P, j1 - j0], F32, f"picked{t}_{j0}")
            nc.vector.tensor_copy(tile[:], pages[t][:].indirect(listed(j0, j1)))
            for j in range(j0, j1, P):
                picked[t, j // P] = tile[:, j - j0 : j - j0 + P]

        pick(0, WIDE, S, 6.5)
        news = [rooms2[:, 0, :], room(79, "new0_1")]
        update_pair(0, 0, [moved0[:], moved1], [rooms1[:, 2, :], room(90, "summed0_1")], news)
        weigh_on_gpsimd(bounded11, woven1[:, half:])
        pick(1, WIDE, WIDE + P, 75)
        puts_of(0, 0, news)
        weigh_on_scalar(1, bounded10, 71.5, woven1[:, 0:half])
        moved2 = moved_alone(2, 0, CHUNK, banks[4], 80, h0)
        moved3 = [rooms2[:, 2, 0:P], placed(81, [P, P], F32, "moved0_3_1")[:]]
        moved_in_parts(3, banks[5], moved3)
        woven_products(2, banks[6:8])
        bounded21 = squash_woven(2, banks[6:8], 30)

        codes, plane = quantise_h("h1", woven1[:], PASSES * CHUNK)
        h1 = [(codes[:, b * CHUNK : (b + 1) * CHUNK], plane[:, b * CHUNK : (b + 1) * CHUNK]) for b in range(PASSES)]
        news = [rooms2[:, 2, :], room(82, "new0_3")]
        update_pair(1, 0, [moved2[:], moved3], [rooms2[:, 0, :], room(103, "summed0_3")], news)
        weigh_on_gpsimd(bounded21, woven_wide1[:, 0:half])
        puts_of(1, 0, news)
        pick(2, WIDE, WIDE + P, 90)
        products(2, 0, banks[4:6])
        bounded20 = squash_slots(2, banks[4:6], 26)
        moved = moved_pair(0, banks[5], 84, h1)
        woven_products(3, banks[6:8])
        bounded31 = squash_woven(3, banks[6:8], 8.5)
        woven_wide0 = placed(92, [P, 2 * half], BF16, "woven_wide0")
        weigh_on_scalar(2, bounded20, 56, woven_wide0[:, 0:half])
        products(3, 0, banks[4:6])
        moved.extend(moved_pair(1, banks[7], 86, h1))
        weigh_on_scalar(3, squash_slots(3, banks[4:6], 20), 60, woven_wide0[:, half:])

        news = [room(76, "new1_0"), room(79, "new1_1")]
        update_pair(0, CHUNK, [moved[0], [moved[1]]], [rooms2[:, 2, :], room(82, "summed1_1")], news)
        weigh_on_gpsimd(bounded31, woven_wide1[:, half:])
        puts_of(0, CHUNK, news)
        pick(2, WIDE + P, WIDE + CHUNK, 84)

        wide = [quantise_h("wide0", woven_wide0[:], WIDE, 76), quantise_h("wide1", woven_wide1[:], WIDE)]
        sums = placed(95, [P, HALF, CHUNK], F32, "summed1_23")
        news1 = [room(82, "new1_2"), room(83, "new1_3")]
        update_pair(1, CHUNK, [moved[2], [moved[3]]], [sums[:, k, :] for k in range(HALF)], news1)
        for t, j0, kb in ((1, WIDE + P, 85), (2, WIDE + CHUNK, 94.25), (3, WIDE, 87)):
            pick(t, j0, S, kb)
        puts_of(1, CHUNK, news1)

        blocks = [
            placed(kb, [P, HALF, width * HALF], BF16, f"paired{kb}") for kb, width in ((12, BANK), (16, T - BANK))
        ]
        middle = (T - BANK) * HALF
        news = []
        for t, kb_summed, kb_clipped, kb_back in ((0, 0, 96, 56), (1, 8, 46, 58), (2, 10, 15, 60), (3, 106, None, None)):
            turned, returned = banks[(6, 7, 5, 1)[t]], banks[(5, 1, 2, 3)[t]]
            moved = moved_alone(t, WIDE, S, banks[6 + t % HALF], 32 + 2 * t, wide)
            for x in range(WIDE // P):
                cols = slice(x * P, (x + 1) * P)
                for last, term in enumerate((moved[:, cols], picked[t, WIDE // P + x])):
                    nc.tensor.matmul(turned[:, cols], term, ident[:], start=not last, stop=bool(last), is_transpose=True)
            summed = placed(kb_summed, [P, WIDE], F32, f"summed_turned{t}")
            nc.scalar.copy(summed[:], turned[:])
            if kb_clipped is None:
                clipped = blocks[1][:].rearrange("p u m -> p (u m)")[:, middle - WIDE : middle + WIDE].bitcast(F32)
            else:
                clipped = placed(kb_clipped, [P, WIDE], F32, f"clipped{t}")
            for x in range(WIDE // P):
                cols = slice(x * P, (x + 1) * P)
                block = WIDE // P + x
                nc.gpsimd.tensor_scalar(
                    clipped[:, cols], summed[:, cols], docks_rows[:, block : block + 1], LOWEST, ALU.min, ALU.max
                )
            for x in range(WIDE // P):
                cols = slice(x * P, (x + 1) * P)
                nc.tensor.transpose(returned[:, cols], clipped[:, cols], ident[:])
            if kb_back is not None:
                back = placed(kb_back, [P, WIDE], F32, f"back{t}")
                nc.scalar.copy(back[:], returned[:])
                news.append(back)
        back3 = blocks[0][:, 1, :].bitcast(F32)
        nc.scalar.copy(back3, banks[3][:])

        out_rows = out_0.rearrange("(p t) m -> p t m", t=PACK)
        starts = [sum(PIECES[:q]) for q in range(len(PIECES))]

        def block_of(q):
            x = min(starts[q] // BANK, 1)
            return x, slice(starts[q] - x * BANK, starts[q] - x * BANK + PIECES[q])

        def hand_out(t):
            nc.sync.dma_start(out_rows[:, t, :], pages[t][:])
            if t < HALF:
                edges = (0, BANK, GPSIMD_FROM, T)
            elif t < PACK - 1:
                edges = (*[start for start in starts if start <= BANK], T)
            else:
                edges = (*starts, T)
            for m0, m1 in zip(edges, edges[1:]):
                x = min(m0 // BANK, 1)
                cols = slice(m0 - x * BANK, m1 - x * BANK)
                dst = blocks[x][:, t // HALF, :].rearrange("p (m e) -> p m e", e=HALF)[:, cols, t % HALF]
                src = pages[t][:, m0:m1]
                if t < HALF and m0 >= GPSIMD_FROM:
                    nc.gpsimd.tensor_scalar(dst, src, 1.0, 1.0, ALU.mult, ALU.mult)
                elif t >= HALF and x == 0:
                    nc.vector.tensor_copy(dst, src)
                else:
                    nc.scalar.copy(dst, src)

        for t in range(HALF):
            put(t, WIDE, S, news[t][:])
            hand_out(t)
        put(2, WIDE, S, news[2][:])
        put(3, WIDE, S, back3)
        for t in range(HALF, PACK):
            hand_out(t)

        y_plane = held([P, T], U8, "y_plane")
        y_codes = held([P, T], I32, "y_codes")
        words_out = out_1[0].rearrange("p m t -> p (m t)").bitcast(I32)
        scale_rows = out_2[0].rearrange("(q r) m -> r q m", q=QUADS)
        y_woven = [placed(28 + starts[q] * 8 / KB, [P, width * PACK], BF16, f"y_woven{q}") for q, width in enumerate(PIECES)]

        def weave_words(q):
            x, cols = block_of(q)
            copy = nc.scalar.copy if q >= len(PIECES) - SCALAR_PIECES else nc.vector.tensor_copy
            copy(
                y_woven[q][:].bitcast(U32).rearrange("p (m u) -> p m u", u=HALF),
                blocks[x][:].bitcast(U32).rearrange("p u m -> p m u")[:, cols, :],
            )

        for q, width in enumerate(PIECES):
            if q % 2 == 0:
                for ahead in range(q, min(q + 2, len(PIECES))):
                    weave_words(ahead)
            cols = slice(starts[q], starts[q] + width)
            nc.vector.quantize_mx(out=y_codes[:, cols].bitcast(FP8X4), scales=y_plane[:, cols], in_=y_woven[q][:])
            if cols.stop in STORES:
                done_cols = slice(max(edge for edge in (0, *STORES) if edge < cols.stop), cols.stop)
                nc.sync.dma_start(words_out[:, done_cols], y_codes[:, done_cols])
        for r in range(4):
            queue = (nc.sync, nc.scalar)[r % 2]
            queue.dma_start(scale_rows[r].bitcast(I32), y_plane[r:P:32, :].bitcast(I32))
